import numpy as np, ml_dtypes
CORES = [2,3,42,43,82,83,122,123]
N = 8
import mx_ref
BF = ml_dtypes.bfloat16
def gcols(t, e):
    v = np.concatenate([t.reshape(8, 16, -1, 4), np.zeros((8, 16, 1, 4), BF)], axis=2)
    return np.ascontiguousarray(np.stack([v[g][:, e[g]] for g in range(8)])).reshape(128, -1)
def tile(rs):
    return np.stack(rs, axis=2).reshape(128, -1).astype(BF)
def pick(q, e):
    c = np.concatenate([q[0].reshape(128, -1, 4), np.zeros((128, 1, 4), np.uint8)], axis=1); s = np.concatenate([q[1], np.ones((16, 1), np.uint8)], axis=1)
    return (np.ascontiguousarray(c[:, e].reshape(128, -1)), np.ascontiguousarray(s[:, e]))
def join(*qs):
    return (np.concatenate([q[0] for q in qs], axis=1), np.concatenate([q[1] for q in qs], axis=1))
def put(q, e, v):
    c, s = q[0].reshape(128, -1, 4).copy(), q[1].copy(); c[:, e] = v[0].reshape(128, -1, 4); s[:, e] = v[1]
    return (c.reshape(128, -1), s)
def pk(c, s):
    return (np.ascontiguousarray(c), mx_ref.live(s))
def emit(q):
    return q[0], q[1]
def packed(v, rng):
    q = [mx_ref.quantize(np.ascontiguousarray(v[r])) for r in range(N)]
    return np.stack([a for a, b in q]), np.stack([mx_ref.plane(b, rng) for a, b in q])
def values_of_codes():
    e, c = np.zeros((128, 128, 4), np.float32), np.zeros((128, 2, 4), np.uint8)
    e[np.arange(128), np.arange(128), 0] = 1
    c[:127, :, 0] = np.arange(256).reshape(2, 128).T[:127]
    return mx_ref.matmul(mx_ref.quantize(e.reshape(128, 512).astype(BF)), (c.reshape(128, 8), np.full((16, 2), 127, np.uint8))).T.reshape(-1).astype(np.float64)
CODE_VALUE, SCALE_VALUE = values_of_codes(), 2.0 ** (np.arange(256) - 127.0)
def decode(q):
    return (CODE_VALUE[q[0]].reshape(16, 8, -1, 4) * SCALE_VALUE[q[1]][:, None, :, None] + 0.0).reshape(128, -1).astype(np.float32)
def f(rng, *shape):
    return mx_ref.flush((rng.standard_normal(shape, dtype=np.float32) * np.exp2(rng.integers(-2, 3, shape[:-1] + (1,)))).astype(BF))
def wide(rng, *shape, cols=0):
    v = rng.standard_normal(shape, dtype=np.float32) * np.exp2(rng.integers(-12, 13, shape)).astype(np.float32)
    if cols: v *= np.repeat(np.exp2(rng.integers(-cols, cols + 1, shape[:-2] + (1, shape[-1] // 4))) * (rng.random(shape[:-2] + (1, shape[-1] // 4)) > 0.0625), 4, axis=-1).astype(np.float32)
    return mx_ref.flush(v.astype(BF))
C, R = 320, 3
STEP = [1, 2, 4]
DOUBLINGS = 9
def order(p):
    return np.argsort(-(p + np.float32(0.0)), axis=1, kind="stable")
def mates(o):
    m = np.zeros_like(o)
    np.put_along_axis(m, o, np.ascontiguousarray(o.reshape(8, -1, 2)[:, :, ::-1]).reshape(8, -1), axis=1)
    return m
def at(a, e):
    return np.take_along_axis(a, e, axis=1)
def big(v):
    v = v.astype(np.float32)
    v[np.abs(v) < np.float32(2.0 ** -16)] = 0
    return v.astype(BF)
def same(u):
    return np.stack([u.reshape(128, 512)] * N)
def numbers_of(rng):
    return {"x": big(f(rng, N, 128, 4 * C)), "u": same(np.array(f(rng, 128, 512))), "v": np.array(f(rng, N, 128, 512))}
def weights(rng, w):
    c, p = packed(w, rng)
    return {"wc": c, "ws": p}
def still(rng):
    return weights(rng, np.zeros((N, 128, 2048), BF))
def ring(rng):
    v = np.concatenate([rng.permutation(C), C + rng.permutation(C)]).reshape(C, 2)[rng.permutation(C)].reshape(-1)
    a, b = np.zeros(2 * C, int), np.zeros(2 * C, int)
    a[v[v < C]] = np.arange(C)
    a[v[v >= C]] = np.arange(C)
    b[np.roll(v, -1).reshape(C, 2)[rng.permutation(C)].reshape(-1)] = np.arange(2 * C)
    return a, b
def digits(s):
    return (((s[:, None] >> np.arange(12)) & 1) * 2.0 ** (np.arange(12) - 23.0)).reshape(-1, 3, 4).transpose(1, 0, 2)
def setup_inputs(rng):
    return {**numbers_of(rng), **weights(rng, big(f(rng, N, 128, 2048)))}
def setup_inputs_ties(rng):
    d = numbers_of(rng)
    e = rng.permutation(N)
    x = d["x"].reshape(N, 8, 16, C, 4)
    a = x[0][:, :8, :3].copy()
    a[:, :, 2] = 0
    for r in range(N):
        k = np.zeros(C, int) if r == e[0] else rng.permutation(C) % 3
        x[r][:, :8] = a[:, :, k]
    x[e[1]] = 0
    u = d["u"][0].reshape(8, 16, 128, 4).copy()
    u[:, 8:, ::8] = 0
    g = 16 * rng.permutation(8)
    u[:, :, g[:2]] = 0
    u[:, :, g[2:4] + 8] = 0
    u[:, :, [g[4], g[4] + 8]] = 0
    return {"x": x.reshape(N, 128, 4 * C), "u": same(u), "v": d["v"], **weights(rng, big(f(rng, N, 128, 2048)))}
def setup_inputs_near(rng):
    d = numbers_of(rng)
    x = d["x"].astype(np.float32).reshape(N, 8, 16, C, 4)
    o = rng.permutation(8)
    c = np.array([1.0, -1.0, 1.0, -1.0, 1.0, -1.0, 0.0, 0.0])[o]
    k = np.array([1.0, 1.0, 1.0, 1.0, 2.0 ** -30, 2.0 ** -30, 2.0 ** -30, -2.0 ** -30])[o].astype(np.float32).astype(BF)
    x[:, :, 0] = 0
    x[:, :, 0, :, 0] = c[None, :, None]
    x[:, :, 14:] = rng.integers(4, 8, (N, 8, 2, C, 4)) * rng.choice([-1.0, 1.0], (N, 8, 2, C, 4)) * 2.0 ** -20
    for i in range(0, N, 2):
        for g in range(8):
            a, b = ring(rng)
            for s in range(2):
                x[i + s, g, 8:11] = digits(a[C * s:C * s + C])
                x[i + s, g, 11:14] = digits(b[C * s:C * s + C])
    u = d["u"][0].reshape(128, 128, 4).copy()
    u[:, ::8] = 0
    for g in range(8):
        h = 16 * g
        u[h, h, 0] = k[g]
        u[h, h + 8, 0] = k[g]
        u[h + 8:h + 11, h] = k[g]
        u[h + 11:h + 14, h + 8] = k[g]
    return {"x": x.reshape(N, 128, 4 * C).astype(BF), "u": same(u), "v": d["v"], **still(rng)}
def setup_inputs_huge(rng):
    d = numbers_of(rng)
    c = np.ones((N, C))
    for i, k in enumerate(rng.permutation(N // 2) % 3):
        if k == 1: c[2 * i + int(rng.integers(2))] = -1
        if k == 2:
            for s in range(2): c[2 * i + s] = rng.permutation(C) % 2 * 2.0 - 1.0
    x = 2.0 ** 30 * (0.6 + 0.4 * rng.random((N, 128, C, 4))) * c[:, None, :, None]
    g = np.stack([rng.permutation(8) % 2, rng.permutation(8) % 2], axis=1).reshape(16) * 2.0 - 1.0
    u = d["u"][0].reshape(128, 128, 4).copy()
    u[:, ::8] = (2.0 ** 30 * (1 - 0.25 * rng.random((128, 16, 4))) * g[None, :, None]).astype(np.float32).astype(BF)
    return {"x": x.astype(np.float32).reshape(N, 128, 4 * C).astype(BF), "u": same(u), "v": d["v"], **still(rng)}
def setup_inputs_spread(rng):
    d = setup_inputs(rng)
    d["x"] = big(wide(rng, N, 128, 4 * C, cols=6))
    return d
def check_inputs(d):
    b = []
    for k in ("x", "u", "v"):
        a = np.abs(d[k].astype(np.float32))
        if not (np.isfinite(a).all() and ((a == 0) | (a >= 2.0 ** -30) & (a <= 2.0 ** 30)).all()): b.append("a value of " + k)
    if (d["u"] != d["u"][:1]).any(): b.append("u differs between ranks")
    if ((d["wc"] & 127) == 127).any(): b.append("a code of wc is no number")
    a = np.zeros((128, 4, 4), np.float32)
    a[:, 1] = 2.0 ** -30
    a[:, 2] = 2.0 ** 30
    e = emit(mx_ref.quantize(a.reshape(128, 16).astype(BF)))[1][0]
    s = np.stack([mx_ref.live(p) for p in d["ws"]])
    if not ((s == e[0]) | (s >= e[1]) & (s <= e[2])).all(): b.append("a scale of ws")
    return b
def reference(x, u, v, wc, ws):
    qu = mx_ref.quantize(u[0])
    lay = [pk(wc[r], ws[r]) for r in range(N)]
    now = [x[r] for r in range(N)]
    for t in range(R):
        num, s, sent, reds = [], [], [], [None] * N
        for r in range(N):
            q = mx_ref.quantize(now[r])
            num.append(decode(q).astype(BF))
            s.append(mx_ref.matmul(qu, q))
        own = [mates(order(s[r][::16])) for r in range(N)]
        for lo in range(N):
            hi = lo ^ STEP[t]
            if lo < hi:
                a = np.concatenate([own[lo], C + own[hi]], axis=1)
                b = mates(order(np.concatenate([s[lo][8::16], s[hi][8::16]], axis=1)))
                to = at(b, a)
                low = np.tile(np.arange(2 * C), (8, 1))
                for i in range(DOUBLINGS):
                    low = np.minimum(low, at(low, to))
                    to = at(to, to)
                blue = low > at(low, a)
                reds[lo] = np.argsort(blue[:, :C], axis=1, kind="stable")[:, :C // 2]
                reds[hi] = np.argsort(blue[:, C:], axis=1, kind="stable")[:, :C // 2]
        for r in range(N):
            one = gcols(num[r], reds[r]).astype(np.float32)
            two = gcols(num[r], at(own[r], reds[r])).astype(np.float32)
            sent.append(mx_ref.quantize(((one + two) * np.float32(0.5)).astype(BF)))
        for r in range(N):
            e = np.tile(np.arange(C), (8, 1))
            np.put_along_axis(e, reds[r], np.tile(C + np.arange(C // 2), (8, 1)), axis=1)
            came = decode(sent[r ^ STEP[t]]).astype(BF)
            z = mx_ref.quantize(gcols(np.concatenate([num[r], came], axis=1), e))
            d = decode(z).reshape(128, C, 4)
            now[r] = tile([d[:, :, b] + np.maximum(mx_ref.matmul(pick(lay[r], np.arange(128 * b, 128 * b + 128)), z), np.float32(0.0)) * np.float32(0.03125) for b in range(4)])
    y, ol = np.zeros((N, 128, C), np.float32), np.zeros((N, 8, C // 2), np.float32)
    oc, osc = np.zeros((N, 128, 4 * C), np.uint8), np.zeros((N, 16, C), np.uint8)
    for r in range(N):
        q = mx_ref.quantize(now[r])
        y[r] = mx_ref.matmul(mx_ref.quantize(v[r]), q)
        ol[r] = reds[r]
        oc[r], osc[r] = emit(q)
    return {"y": y, "ol": ol, "oc": oc, "osc": osc}

@@ -1,0 +1,617 @@
+from concourse.mybir import dt, AluOpType as ALU, ActivationFunctionType as AF
+
+C, R = 320, 3
+F32, BF, I32, U16, U8, MX, F16 = "float32", "bfloat16", "int32", "uint16", "uint8", "float8_e4m3fn_x4", "float16"
+SCRATCH = {"ps": ("psum", [128, 4096], F32)}
+for _n, _w, _t in [
+    ("x0", 1280, BF), ("xa", 1280, BF), ("ut", 512, BF), ("vt", 512, BF), ("uq", 128, MX), ("us", 128, U8), ("up", 512, MX), ("ups", 512, U8),
+    ("vq", 128, MX), ("vs", 128, U8), ("wq", 512, MX), ("wp", 512, U8), ("one", 512, BF), ("et", 2048, BF), ("eq", 512, MX), ("es", 512, U8),
+    ("bq", 160, MX), ("bs", 160, U8), ("zq", 320, MX), ("zs", 320, U8), ("bt", 640, BF), ("yt", 1280, BF), ("dw", 1920, BF), ("dp", 1280, BF),
+    ("tm", 640, F32), ("rl", 1280, F32), ("ysb", 320, F32), ("er", 160, F32),
+    ("xt", 1280, F32), ("fl", 9600, BF), ("sg", 9600, BF), ("so", 6400, BF), ("ac", 120, F32), ("eqf", 1280, BF), ("eqs", 1280, BF), ("eqm", 320, BF),
+    ("cf", 3200, BF), ("pf", 1616, F16), ("x1", 320, F16), ("x2", 320, F16), ("cu", 352, F32),
+    ("ck", 120, F32), ("ce", 40, F32), ("d1", 50, F32), ("p1", 20, F32), ("ra", 40, I32), ("rt", 80, I32), ("rb", 20, I32), ("ba", 20, I32),
+    ("rau", 40, U16), ("bau", 40, U16), ("sa", 320, BF), ("cn", 320, BF), ("j1", 320, F32), ("j3", 320, F32), ("eb", 320, F32), ("enc", 320, BF), ("lo", 320, BF),
+    ("sc1", 640, BF), ("sc2", 640, BF), ("xs", 640, BF), ("st", 640, BF), ("oa", 640, BF), ("wa", 704, BF), ("w0", 704, BF), ("w1", 704, BF),
+    ("yy", 320, BF), ("an", 320, BF), ("la", 32, U16), ("li", 64, U16), ("ex", 128, F32), ("e2", 64, F32), ("e3", 32, F32), ("obu", 32, U16),
+    ("e4", 64, F32), ("e5", 32, F32), ("lnu", 32, U16), ("xc", 704, BF),
+    ("fg", 64, F32), ("mm", 20, F32), ("stb", 640, BF), ("bw", 640, BF), ("wb", 352, BF), ("wb2", 352, BF), ("xb", 704, BF), ("rn", 320, BF), ("pm", 320, BF),
+    ("pr", 128, F32), ("a1", 128, F32), ("jj", 192, F32), ("ysu", 32, U16), ("se", 496, BF), ("lu", 80, U16),
+    ("tbl", 640, BF), ("zz", 640, BF), ("ti", 2560, BF), ("pi", 8, I32), ("ui", 32, I32), ("ul", 32, U16), ("cc", 64, F32), ("ci", 72, F32), ("cl", 72, U16),
+    ("ia", 60, F32),
+]:
+    SCRATCH[_n] = ("sbuf", [128, _w], _t)
+for _t in range(R + 1):
+    SCRATCH["tq%d" % _t] = ("sbuf", [128, C], MX)
+    SCRATCH["ts%d" % _t] = ("sbuf", [128, C], U8)
+for _t in range(R):
+    SCRATCH["lq%d" % _t] = ("sbuf", [128, C], MX)
+    SCRATCH["ls%d" % _t] = ("sbuf", [128, C], U8)
+    SCRATCH["sn%d" % _t] = ("sbuf", [128, 180], F32)
+SEMAPHORES = (["cv", "cs", "cp", "cg", "dx", "dx2", "du", "dv", "dwq", "dwp", "dtb", "dsa", "dz", "dout", "sent"]
+              + ["a%s%d" % (k, t) for k in "qrsn" for t in range(R)])
+
+NS = [(4, 4, 4, 4), (5, 4, 4, 4), (5, 4, 4, 4)]
+
+
+def rank_program(g, core, T, topo):
+    rank = T.rank_of(core)
+    if rank is None:
+        return
+    Q = {"v": g.vector, "s": g.scalar, "p": g.tensor, "g": g, "y": g.sync}
+    total = {}
+    seen = {q: {} for q in Q}
+    log = {}
+
+    def A(name, lo=0, hi=None, step=1, rows=None):
+        hi = SCRATCH[name][1][1] if hi is None else hi
+        cols = slice(lo, hi) if step == 1 else slice(lo, hi, step)
+        ap = T[name][(slice(None) if rows is None else rows), cols]
+        if name == "ps":
+            m = ((1 << ((hi - 1) // 512 + 1)) - 1) ^ ((1 << (lo // 512)) - 1)
+        elif step == 1:
+            m = ((1 << hi) - 1) ^ ((1 << lo) - 1)
+        else:
+            m = sum(1 << c for c in range(lo, hi, step))
+        return (ap, [(name, m)])
+
+    def ind(win, off, word=False):
+        ap = win[0].bitcast(dt.uint32) if word else win[0]
+        return (ap.indirect(off[0]), win[1] + off[1])
+
+    def wait(q, tok):
+        if seen[q].get(tok[0], 0) < tok[1]:
+            Q[q].wait_ge(T.sem[tok[0]], tok[1])
+            seen[q][tok[0]] = tok[1]
+
+    def order(q, reads, writes):
+        need = {}
+        for regs, w in ((reads, False), (writes, True)):
+            for name, m in regs:
+                for e in log.get(name, []):
+                    if e[0] & m and (w or e[2] or (name == "ps" and e[3] != q)) and not (q == "p" and e[3] == "p"):
+                        need[e[1][0]] = max(need.get(e[1][0], 0), e[1][1])
+        for s in need:
+            wait(q, (s, need[s]))
+
+    def note(q, tok, reads, writes):
+        for name, m in writes:
+            log[name] = [[e[0] & ~m] + e[1:] for e in log.get(name, []) if e[0] & ~m] + [[m, tok, True, q]]
+        for name, m in reads:
+            log[name] = [e for e in log.get(name, []) if e[2] or e[3] != q or e[1][0] != tok[0] or e[0] & ~m] + [[m, tok, False, q]]
+
+    def op(q, fn, outs, ins, lists=()):
+        reads = [r for a in ins if isinstance(a, tuple) for r in a[1]] + list(lists)
+        writes = [r for a in outs for r in a[1] if r not in lists]
+        order(q, reads, writes)
+        s = "c" + q
+        if q == "g":
+            wait(q, (s, total.get(s, 0)))
+        total[s] = total.get(s, 0) + 1
+        fn().then_inc(T.sem[s], 1)
+        note(q, (s, total[s]), reads, writes)
+
+    def x(a):
+        return a[0] if isinstance(a, tuple) else a
+
+    def dma(q, out, in_, sem, last=None):
+        reads = in_[1] if isinstance(in_, tuple) else []
+        writes = out[1] if isinstance(out, tuple) else []
+        keep = {n: log.get(n, []) for n, m in writes}
+        for n, m in writes:
+            log[n] = [e for e in log.get(n, []) if e[1][0] != sem]
+        order(q, reads, writes)
+        for n in keep:
+            log[n] = keep[n]
+        total[sem] = total.get(sem, 0) + 16
+        Q[q].dma_start(x(out), x(in_)).then_inc(T.sem[sem], 16)
+        note(q, (sem, last or total[sem]), reads, writes)
+
+    def send(dst, out, in_, sem):
+        order("g", in_[1], [])
+        rid, pid = topo.addr(dst)[0:2]
+        g.remote_dma(out[0], in_[0], T.sem[sem], T.sem["sent"], pid, rid, topo.mask(core, dst))
+        total["sent"] = total.get("sent", 0) + len(topo.engines(core, dst))
+        total[sem] = len(topo.engines(dst, core))
+        note("r", (sem, total[sem]), [], out[1])
+
+    def u8(a):
+        return (a[0].bitcast(dt.uint8), a[1])
+
+    def cp(out, in_, q="v"):
+        if q == "v":
+            op("v", lambda: g.vector.tensor_copy(out[0], in_[0]), [out], [in_])
+        else:
+            act(out, in_, AF.Copy)
+
+    def scat(win, off, in_):
+        o = ind(win, off)
+        op("v", lambda: g.vector.tensor_copy(o[0], in_[0]), [o], [in_], lists=off[1])
+
+    def tt(out, a, b, o):
+        op("v", lambda: g.vector.tensor_tensor(out[0], a[0], b[0], o), [out], [a, b])
+
+    def ts(out, a, s1, o0, s2=None, o1=None):
+        if o1 is None:
+            op("v", lambda: g.vector.tensor_scalar(out[0], a[0], x(s1), None, o0), [out], [a, s1])
+        else:
+            op("v", lambda: g.vector.tensor_scalar(out[0], a[0], x(s1), x(s2), o0, o1), [out], [a, s1, s2])
+
+    def scan(out, d0, d1, o0, o1=ALU.add):
+        op("v", lambda: g.vector.tensor_tensor_scan(out[0], d0[0], d1[0], 0.0, o0, o1), [out], [d0, d1])
+
+    def tr(out, in_):
+        op("v", lambda: g.vector.transpose(out[0], in_[0]), [out], [in_])
+
+    def fill(out, v):
+        op("v", lambda: g.vector.memset(out[0], v), [out], [])
+
+    def act(out, in_, f, scale=None, bias=None, acc=None):
+        k = {}
+        if scale is not None:
+            k["scale"] = x(scale)
+        if bias is not None:
+            k["bias"] = x(bias)
+        if acc is not None:
+            k["accum_out"] = acc[0]
+        op("s", lambda: g.scalar.activation(out[0], in_[0], f, **k), [out] + ([acc] if acc else []), [in_, scale, bias])
+
+    def lin(out, in_, scale, bias):
+        act(out, in_, AF.Identity, scale, bias)
+
+    def iota(out, pat, base=0, cm=0, flt=True):
+        if flt:
+            op("g", lambda: g.iota(out[0], pat, base, cm, allow_small_or_imprecise_dtypes=True), [out], [])
+        else:
+            op("g", lambda: g.iota(out[0], pat, base, cm), [out], [])
+
+    def sel(out, in_, pat, o, base, cm):
+        op("g", lambda: g.affine_select(out[0], in_[0], pat, o, 0.0, base, cm), [out], [in_])
+
+    def quant(q, s, in_):
+        op("v", lambda: g.vector.quantize_mx(q[0], s[0], in_[0]), [q, s], [in_])
+
+    def mm(bank, wq, ws, c0, xq, xs, lo=0, hi=C):
+        out, a, b, c, d = A("ps", 512 * bank, 512 * bank + hi - lo), A(wq, c0, c0 + 128), A(ws, c0, c0 + 128), A(xq, lo, hi), A(xs, lo, hi)
+        op("p", lambda: g.tensor.matmul_mx(out[0], a[0], b[0], c[0], d[0], True, True), [out], [a, b, c, d])
+
+    def P(bank, lo=0, hi=C):
+        return A("ps", 512 * bank + lo, 512 * bank + hi)
+
+    def K(i, j=None):
+        return A("cc", i, (i if j is None else j - 1) + 1)
+
+    def L(i, j):
+        return A("cl", i, j)
+
+    add, sub, mul, mn = ALU.add, ALU.subtract, ALU.mult, ALU.min
+    band, shr = ALU.bitwise_and, ALU.arith_shift_right
+    parts = [rank ^ (1 << t) for t in range(R)]
+    hs = [1 if rank > p else 0 for p in parts]
+    H = C // 2
+
+    def send_t(t, half):
+        dst = T.cores[parts[t]]
+        send(dst, u8(A("lq%d" % t, H * half, H * half + H)), u8(A("tq%d" % t, H * half, H * half + H)), "a%s%d" % ("qr"[half], t))
+        if half:
+            send(dst, A("ls%d" % t), A("ts%d" % t), "as%d" % t)
+
+    def runs(kind, t):
+        out = []
+        for half in range(2):
+            n = NS[t]["ab".index(kind) + (0 if half == hs[t] else 2)]
+            if n:
+                out.append((10 * half, 10 * half + n, "s", half))
+            if n < 10:
+                out.append((10 * half + n, 10 * half + 10, "v", half))
+        return out
+
+    def count_constants(t):
+        for k, kind in enumerate("ab"):
+            for c0, c1, q, half in runs(kind, t):
+                iota(A("ck", 40 * t + 20 * k + c0, 40 * t + 20 * k + c1), [[32 if q == "s" else 0, c1 - c0]],
+                     320 * half + (32 * (c0 % 10) + 32 if q == "s" else 160))
+
+    def lists(pairs, singles=()):
+        for c0, k, b in pairs:
+            lin(A("ci", c0, c0 + 2), K(k, k + 2), 1.0, float(b))
+        for c0, k, b in singles:
+            lin(A("ci", c0, c0 + 1), K(k), 1.0, float(b))
+
+    def tie_mask(a):
+        rows = slice(32 * a, 32 * a + 32)
+        sel(A("eqm", rows=rows), A("one", 0, 320, rows=rows), [[0, 10], [-1, 32]], ALU.not_equal, 0, 1)
+
+    def pick_u(hh):
+        o_, l_ = A("up", 256 * hh, 256 * hh + 256), A("ul", 16 * hh, 16 * hh + 16)
+        i_ = ind(A("uq"), l_, True)
+        op("v", lambda: g.vector.tensor_copy(o_[0].bitcast(dt.uint32), i_[0]), [o_], [i_])
+        cp(A("ups", 256 * hh, 256 * hh + 256), ind(A("us"), l_), "s")
+
+    dma("y", A("x0", 0, 640), T.x[:, 0:640], "dx")
+    dma("s", A("ut"), T.u[:], "du")
+    dma("y", A("x0", 640, 1280), T.x[:, 640:1280], "dx2")
+    dma("y", u8(A("wq")), T.wc[:], "dwq")
+    dma("y", A("wp"), T.ws[:], "dwp")
+    dma("y", A("vt"), T.v[:], "dv")
+    iota(A("pi", 0, 1), [[0, 1]], 0, 1, False)
+    iota(A("ui"), [[8, 4], [32, 4], [0, 2]], 0, 0, False)
+    iota(A("ia", 0, 20), [[16, 10], [0, 2]])
+    iota(A("ia", 20, 40), [[0, 10], [1, 2]])
+    fill(A("one"), 1.0)
+    tie_mask(0)
+    tie_mask(1)
+    p0, i4, r = A("pi", 0, 1), K(0), K(1)
+    ts(A("pi", 1, 2), p0, 15, band)
+    ts(A("pi", 2, 3), p0, 4, shr, 1, band)
+    ts(A("pi", 3, 4), p0, 1, band)
+    ts(A("pi", 4, 5), p0, 1, shr, 7, band)
+    cp(A("ul"), A("ui"))
+    cp(K(0, 4), A("pi", 1, 5))
+    fill(A("zz"), 0.0)
+    zero = [A(w) for w in ("cn", "sc1", "st", "tbl", "sc2", "stb", "se")]
+    zero += [A(w, c, c + 16) for w in ("wa", "xb", "w0", "w1", "wb", "wb2", "xc") for c in (0, 336)]
+    for a in zero:
+        dma("y", a, A("zz", 0, bin(a[1][0][1]).count("1")), "dz", 16 * len(zero))
+    tt(K(4), K(2), r, ALU.not_equal)
+    for k, v in ((23, 1.0), (24, 3.0), (25, 5.0), (26, 4.0), (19, 10.0), (20, 12.0)):
+        ts(K(k), i4, v, ALU.is_equal)
+    ts(K(27), i4, 1.0, ALU.not_equal)
+    ts(K(28), i4, 9.0, mn)
+    ts(K(15), i4, 32.0, mul, 512.0, add)
+    for k, src, a, b in ((5, r, -32.0, 368.0), (7, K(3), 32.0, 16.0), (14, i4, 32.0, 0.0), (11, r, 16.0, 0.0), (12, r, 17.0, 0.0), (13, r, -16.0, 0.0),
+                         (16, r, -704.0, 368.0), (18, r, -1.0, 1.0), (22, r, 368.0, 16.0), (29, r, -704.0, 336.0), (30, r, -352.0, -16.0), (49, r, -320.0, 0.0),
+                         (34, i4, 1.0, 0.0), (35, i4, 1.0, 16.0), (36, K(28), 1.0, 84.0), (37, K(28), 1.0, 100.0), (38, K(28), 1.0, 52.0),
+                         (9, K(4), K(5), K(7)), (33, K(24), 1.0, 1.0), (6, K(26), 1.0, K(25)), (48, K(19), 1.0, K(20)), (17, r, 496.0, K(35)),
+                         (31, K(23), K(29), K(22)), (8, K(6), -1.0e6, 1.0e6), (50, K(48), K(49), 0.0), (32, K(24), K(30), K(31))):
+        lin(K(k), src, a, b)
+    for half in range(2):
+        quant(A("tq0", H * half, H * half + H), A("ts0", H * half, H * half + H), A("x0", 640 * half, 640 * half + 640))
+        send_t(0, half)
+        if half == 0:
+            quant(A("uq"), A("us"), A("ut"))
+    pick_u(hs[0])
+    ts(K(15), K(15), 608.0, mn)
+    ts(K(10), K(9), 256.0, add, 672.0, mn)
+    for k, src, b in ((40, K(9, 11), K(11)), (42, K(9, 11), K(12)), (44, K(9, 11), K(13)), (46, K(14, 16), r)):
+        lin(K(k, k + 2), src, 1.0, b)
+    lists(((4, 42, 6), (6, 40, 9)))
+    tie_mask(2)
+    tie_mask(3)
+    iota(A("j3"), [[16, 20], [0, 16]])
+    iota(A("eb"), [[0, 5], [32, 4], [1, 16]], 128)
+    iota(A("lo"), [[0, 20], [1, 16]])
+    count_constants(0)
+
+    def mid_constants():
+        ts(A("sa"), A("j3"), K(33), mul, K(32), add)
+        for k in range(5):
+            ts(A("enc", 64 * k, 64 * k + 64), A("eb", 64 * k, 64 * k + 64), K(11), add, float(2 ** k), mul)
+        cp(L(4, 8), A("ci", 4, 8))
+        for d, kd, s, ks in (("cn", 12, "sa", 3), ("sa", 2, "lo", 2), ("sa", 8, "enc", 8), ("cn", 5, "enc", 5), ("cn", 13, "lo", 13)):
+            dma("y", A(d, rows=slice(kd, 128, 16)), A(s, rows=slice(ks, 128, 16)), "dsa", 80)
+
+    def late_constants():
+        low = slice(0, 32)
+        iota(A("pf", 4, 810, 805), [[0, 2]])
+        iota(A("cu", 0, 32), [[0, 32]])
+        for k, base, d in ((0, 16, 368), (1, 352, -336)):
+            for e in range(2):
+                iota(A("ti", 640 * k + e, 640 * k + 640, 2, rows=low), [[16, 10], [d, 2], [0, 16]], base + 160 * (1 - e))
+        iota(A("ti", 1280, 1920, rows=low), [[0, 20], [1, 16], [0, 2]])
+        for e in range(2):
+            iota(A("ti", 1920 + e, 2560, 2, rows=low), [[16, 20], [0, 16]], 320 * e)
+        for k in range(4):
+            dma("y", A("tbl", rows=slice(k, 128, 16)), A("ti", 640 * k, 640 * k + 640, rows=slice(0, 8)), "dtb", 64)
+        for b in range(4):
+            sel(A("et", 512 * b, 512 * b + 512), A("one"), [[-1, 512]], ALU.is_equal, b, 4)
+        iota(A("jj", 0, 64), [[0, 2], [16, 32]])
+        for k in range(R):
+            iota(A("sn%d" % k, 20, 32), [[0, 12]])
+        iota(A("j1"), [[1, 320]])
+        count_constants(1)
+        count_constants(2)
+
+    def own(w, xb="xb"):
+        tr(A(xb, 16, 336), A(w, 16, 336))
+
+    def shifted(w, xb="xb"):
+        tr(A(xb, 352, 704), A(w, 0, 352))
+
+    def other(w, lo=0, hi=352):
+        tr(A(w, 352 + lo, 352 + hi), A("xb", lo, hi))
+
+    for t in range(R):
+        h = hs[t]
+        tq, tsc, lq, ls, sn = "tq%d" % t, "ts%d" % t, "lq%d" % t, "ls%d" % t, "sn%d" % t
+        if t:
+            iota(A("sc1"), [[0, 640]])
+            iota(A("sc2"), [[0, 640]])
+        pend = {"v": [], "s": []}
+        cnt = {"v": 0, "s": 0}
+
+        def flush(q, keep=0):
+            while len(pend[q]) > keep:
+                pend[q].pop(0)()
+
+        def unit(q, kind, c):
+            tau, key, n = (0 if kind == "a" else 1), c // 10, 32 * (c % 10) + 32
+            slot = 20 * "abx".index(kind) + c
+            thr = A("xt", 640 * tau + 32 * c, 640 * tau + 32 * c + 1)
+            f0 = C * (cnt[q] % 30)
+            cnt[q] += 1
+            if kind == "x":
+                f = A("cf", c, 3200, 10)
+                act(f, P(7), AF.Sign, -1.0, thr)
+                pend[q].append(lambda: act(f, f, AF.Relu, -1.0, None, A("ac", slot, slot + 1)))
+            elif q == "v":
+                ts(A("fl", f0, f0 + n), P(2 * tau + key, 0, n), thr, ALU.is_ge, 0.5, sub)
+                if n < C:
+                    ts(A("fl", f0 + n, f0 + C), P(2 * tau + key, n, C), thr, ALU.is_gt, 0.5, sub)
+                pend[q].append(lambda: scan(A("so", 160 * slot, 160 * slot + 160), A("fl", f0, f0 + 160), A("fl", f0 + 160, f0 + C), add))
+            else:
+                act(A("sg", f0, f0 + C), P(4 + 2 * tau + key), AF.Sign, -1.0, thr)
+
+                def second():
+                    act(A("sg", f0, f0 + n), A("sg", f0, f0 + n), AF.Relu, None, None, A("ac", 60 + slot, 61 + slot))
+                    act(A("sg", f0 + n, f0 + C), A("sg", f0 + n, f0 + C), AF.Relu, -1.0, None, A("ac", slot, slot + 1))
+                pend[q].append(second)
+            flush(q, 1)
+
+        def listed(q, kind, half):
+            return [(q, kind, c) for c0, c1, qq, hf in runs(kind, t) if qq == q and hf == half for c in range(c0, c1)]
+
+        def units(q, kind, half):
+            for u in listed(q, kind, half):
+                unit(*u)
+
+        def scores(half, q_, s_):
+            for tau in range(2):
+                for e in range(2):
+                    mm(4 * e + 2 * tau + half, "up", "ups", 128 * (2 * h + tau), q_, s_)
+            for tau in range(2):
+                tr(A("xt", 640 * tau + C * half, 640 * tau + C * half + C), P(2 * tau + half))
+
+        def ties(tau, half):
+            c0 = 640 * tau + C * half
+            k0 = 20 * tau + 10 * half
+            tt(A("eqf", c0, c0 + C), P(2 * tau + half), A("xt", c0, c0 + C), ALU.is_equal)
+            flush("v")
+            pend["v"].append(lambda: scan(A("eqs", c0, c0 + C), A("eqm"), A("eqf", c0, c0 + C), mul))
+            return lambda: tt(A("ce", k0, k0 + 10), A("ck", 40 * t + k0, 40 * t + k0 + 10), A("eqs", c0 + 31, c0 + C, 32), sub)
+
+        def ends(slot0, c0, c1):
+            return A("so", 160 * (slot0 + c0) + 159, 160 * (slot0 + c1), 160)
+
+        def same(kind, out):
+            k0 = 0 if kind == "a" else 20
+            for c0, c1, q, half in runs(kind, t):
+                if q == "s":
+                    tt(A("d1", k0 + c0, k0 + c1), A("ac", k0 + c0, k0 + c1), A("ac", 60 + k0 + c0, 60 + k0 + c1), sub)
+            for c0, c1, q, half in sorted(runs(kind, t), key=lambda u: u[2] == "s"):
+                tt(A(out, c0, c1), ends(k0, c0, c1) if q == "v" else A("d1", k0 + c0, k0 + c1), A("ce", k0 + c0, k0 + c1), add)
+
+        scores(h, tq, tsc)
+        units("s", "a", h)
+        units("s", "b", h)
+        units("v", "a", h)
+        mine = listed("v", "b", h)
+        for u in mine[:-2]:
+            unit(*u)
+        f1 = ties(0, h)
+        unit(*mine[-2])
+        f2 = ties(1, h)
+        unit(*mine[-1])
+        f1()
+        if t == 0:
+            mid_constants()
+            late_constants()
+        scores(1 - h, lq, ls)
+        units("s", "a", 1 - h)
+        flush("s")
+        f3 = ties(0, 1 - h)
+        units("v", "a", 1 - h)
+        f2()
+        f3()
+        f4 = ties(1, 1 - h)
+        for c in range(10):
+            unit("s", "x", c)
+        units("s", "b", 1 - h)
+        flush("s")
+        if t == 0:
+            lin(A("ia", 40, 60), A("ia", 20, 40), K(16), K(17))
+            lists(((0, 42, 0), (2, 40, 2), (28, 46, 0), (30, 14, 2), (32, 46, 16), (34, 14, 18)))
+        rest = listed("v", "b", 1 - h)
+
+        def gap():
+            if rest:
+                unit(*rest.pop(0))
+
+        flush("v")
+        same("a", "ra")
+        f4()
+        cp(A("rau", 0, 20), A("ra", 0, 20))
+        ts(A("rt", 0, 20), A("ra", 0, 20), 1, band)
+        gap()
+        scat(A("sc1"), A("rau", 0, 20), A("sa"))
+        ts(A("rt", 20, 40), A("rt", 0, 20), -2.0, mul, 1.0, add)
+        tr(A("xs"), A("sc1"))
+        tt(A("ra", 20, 40), A("ra", 0, 20), A("rt", 20, 40), add)
+        for ks, kd in ((8, 4), (0, 6), (1, 7), (2, 9), (3, 10)):
+            for hh in range(2):
+                tt(A("st", kd + 16 * hh, 640, 32), A("xs", ks, 640, 32), A("xs", 16 + ks, 640, 32), add)
+        cp(A("rau", 20, 40), A("ra", 20, 40))
+        tr(A("oa"), A("st"))
+        gap()
+        tt(A("wa", 16, 336), ind(A("oa"), A("rau", 20, 40)), A("cn"), add)
+        gap()
+        own("wa")
+        shifted("wa")
+        other("wa")
+        cp(A("ex", 0, 64), ind(A("xb"), L(4, 8)))
+        gap()
+        tt(A("e3", 0, 20), A("ex", 0, 20), A("ex", 32, 52), add)
+        while rest:
+            gap()
+        flush("v")
+        for k in range(2):
+            scan(A("pf", 805 * k + 5, 805 * k + 805), A("cf", 1600 * k, 1600 * k + 1600, 2), A("cf", 1600 * k + 1, 1600 * k + 1600, 2), add)
+        cp(A("la", 0, 20), A("e3", 0, 20))
+        for k in range(2):
+            tr(A("x1", 160 * k, 160 * k + 160), A("pf", 805 * k + 9, 805 * k + 805, 5))
+            tr(A("x2", 160 * k, 160 * k + 160), A("pf", 805 * k + 4, 805 * k + 800, 5))
+        if t == 0:
+            tt(A("ci", 36, 56), A("ia", 40, 60), A("ia", 0, 20), add)
+        scan(A("cu", 32, 352), A("x1"), A("x2"), add, sub)
+        if t == 0:
+            quant(A("eq"), A("es"), A("et"))
+        same("b", "p1")
+        tt(A("d1", 40, 50), A("cu", 63, 352, 32), A("cu", 31, 320, 32), sub)
+        tt(A("rb", 0, 10), A("p1", 0, 10), A("ac", 40, 50), add)
+        tt(A("rb", 10, 20), A("p1", 10, 20), A("d1", 40, 50), sub)
+        for b in range(4):
+            mm(4 + b, "eq", "es", 128 * b, lq, ls)
+        for b in range(4):
+            mm(b, "eq", "es", 128 * b, tq, tsc)
+        if t == 0:
+            cp(L(0, 4), A("ci", 0, 4))
+            cp(L(28, 56), A("ci", 28, 56))
+        cp(A("bau", 20, 40), A("rb"))
+        ts(A("rt", 0, 20), A("rb"), 1, band)
+        ts(A("rt", 20, 40), A("rb"), 1, shr)
+        tt(A("w0", 16, 336), ind(A("tbl"), A("bau", 20, 40)), A("wa", 16, 336), add)
+        ts(A("rt", 40, 60), A("rt", 0, 20), 320.0, mul)
+        own("w0")
+        tt(A("ba"), A("rt", 40, 60), A("rt", 20, 40), add)
+        other("w0")
+        cp(A("bau", 0, 20), A("ba"))
+        cp(A("w1", 16, 336), ind(A("w0"), A("la", 0, 20)), "s")
+        scat(A("sc2"), A("bau", 0, 20), A("sa"))
+        cp(A("wb", 16, 336), ind(A("w0"), L(36, 56)), "s")
+        lin(A("an"), ind(A("wa"), L(36, 56)), 1.0, K(50))
+        tr(A("xs"), A("sc2"))
+        own("w1")
+        cp(A("ex"), ind(A("xs"), L(28, 36)))
+        other("w1", 0, 192)
+        tt(A("e2"), A("ex", 0, 64), A("ex", 64, 128), add)
+        other("w1", 192, 352)
+        tt(A("e3", 0, 20), A("e2", 0, 20), A("e2", 32, 52), add)
+        cp(A("obu", 0, 20), A("e3", 0, 20))
+        cp(A("w0", 16, 336), ind(A("w1"), A("obu", 0, 20)))
+
+        def first_round(s):
+            if s == 0:
+                lists(((68, 40, 3), (70, 40, 2), (8, 40, 4), (10, 40, 5), (12, 40, 0), (14, 44, 16), (16, 40, 1), (18, 44, 17)))
+            if s == 1:
+                lists((), ((20, 40, 12), (21, 40, 10), (22, 44, 28), (23, 44, 26), (24, 40, 13), (25, 40, 9), (26, 44, 29), (27, 44, 25)))
+            if s in (2, 3):
+                for j, d in enumerate((116.0, 116.0, 52.0, 52.0, 116.0, 116.0)):
+                    lin(A("ci", 44 + 6 * s + j, 45 + 6 * s + j), K(18) if s == 3 else r, d, K(34 + j % 5))
+            if s == 4:
+                lin(A("pm"), A("one", 0, 320), K(27), 0.0)
+            if s == 5:
+                lin(A("jj", 64, 128), A("jj", 0, 64), 1.0, K(35))
+                lin(A("jj", 128, 192), A("jj", 64, 128), 1.0, 144.0)
+                lin(A("jj", 64, 128), A("jj", 64, 128), 1.0, 145.0)
+
+        fillers = [lambda: own("wb", "xc"), lambda: shifted("wb", "xc"),
+                   lambda: cp(L(56, 72), A("ci", 56, 72)) if t == 0 else None, lambda: cp(A("e4"), ind(A("xc"), L(68, 72))),
+                   lambda: tt(A("e5", 0, 20), A("e4", 0, 20), A("e4", 32, 52), add), lambda: cp(A("lnu", 0, 20), A("e5", 0, 20)),
+                   lambda: cp(L(8, 28), A("ci", 8, 28)) if t == 0 else None]
+        for s in range(8):
+            cur, nxt, l0 = "w%d" % (s % 2), "w%d" % (1 - s % 2), 32 * (min(s, 6) % 2)
+            lin(A("yy"), A(cur, 16, 336), K(6), K(8))
+            if s < 4:
+                act(A("dp", C * s, C * s + C), P(4 + s), AF.Copy, 0.5)
+            else:
+                cp(A("dw", 480 * (s - 4) + 160, 480 * (s - 4) + 480), P(s - 4), "s")
+            if t == 0:
+                first_round(s)
+            own(cur)
+            if s < 7:
+                shifted(cur)
+                other(cur, 0, 192)
+                cp(A("ex", 0, 64), ind(A("xb"), L(0, 4)))
+                other(cur, 192, 352)
+                tt(A("e3", 0, 20), A("ex", 0, 20), A("ex", 32, 52), add)
+                if t or s > 2:
+                    for k in range(2 if t == 0 else 1):
+                        if fillers:
+                            fillers.pop(0)()
+                cp(A("li", l0, l0 + 20), A("e3", 0, 20))
+            else:
+                other(cur)
+            tt(A(nxt, 16, 336), ind(A(cur), A("li", l0, l0 + 20)), A("yy"), mn)
+        own("w0")
+        shifted("w0")
+        cp(A("fg"), ind(A("xb"), L(8, 12)))
+        tt(A("mm", 0, 10), A("fg", 0, 10), A("fg", 42, 52), mn)
+        tt(A("mm", 10, 20), A("fg", 32, 42), A("fg", 10, 20), mn)
+        for k in (0, 1, 16, 17):
+            tt(A("stb", k, 320, 32), A("mm", 0, 10), A("mm", 10, 20), ALU.is_lt)
+            tt(A("stb", 320 + k, 640, 32), A("mm", 0, 10), A("mm", 10, 20), ALU.is_gt)
+        tr(A("bw"), A("stb"))
+        cp(A("rn"), ind(A("bw"), A("lnu", 0, 20)))
+        scan(A("wb2", 16, 336), A("pm"), A("rn"), mul)
+        own("wb2")
+        shifted("wb2")
+        cp(A("pr"), ind(A("xb"), L(12, 20)))
+        tt(A("a1", 0, 20), A("pr", 0, 20), A("jj", 64, 84), sub)
+        tt(A("a1", 32, 52), A("pr", 32, 52), A("jj", 96, 116), sub)
+        tt(A("a1", 64, 84), A("a1", 0, 20), A("pr", 64, 84), mul)
+        tt(A("a1", 96, 116), A("a1", 32, 52), A("pr", 96, 116), mul)
+        tt(A(sn, 0, 20), A("a1", 64, 84), A("jj", 128, 148), add)
+        tt(A(sn, 32, 52), A("a1", 96, 116), A("jj", 160, 180), add)
+        cp(A("ysu", 0, 20), A(sn, 0, 20))
+        scat(A("se", 16, 496), A("ysu", 0, 20), A("an"))
+        tr(A("xb", 16, 176), A("se", 16, 176))
+        tr(A("xb", 352, 544), A("se", 0, 192))
+        cp(A("ex"), ind(A("xb"), L(20, 28)))
+        tt(A(sn, 52, 116), A("ex", 0, 64), A("ex", 64, 128), add)
+        w = 62 if t == R - 1 else 46
+        send(T.cores[parts[t]], A(sn, 116, 116 + w), A(sn, 32, 32 + w), "an%d" % t)
+        if t == 0:
+            quant(A("vq"), A("vs"), A("vt"))
+            if len(set(hs)) == 2:
+                pick_u(1 - h)
+        k = 5 if t == R - 1 else 4
+        cp(A("lu", 0, 16 * k), ind(A(sn, 0, 116 + w), L(56 + 6 * h, 56 + 6 * h + k)))
+        for b in range(4):
+            win = A("dp", C * b, C * b + C)
+            cp(A("tm", 160 * b, 160 * b + 160), ind(win, A("lu", 32, 42)), "s")
+            tt(A("bt", b, 640, 4), ind(win, A("lu", 48, 58)), A("tm", 160 * b, 160 * b + 160), add)
+        quant(A("bq"), A("bs"), A("bt"))
+        for b in range(4):
+            mm(b, "eq", "es", 128 * b, "bq", "bs", 0, H)
+        for b in range(4):
+            cp(A("dw", 480 * b, 480 * b + 160), P(b, 0, H), "vs"[b % 2])
+        for half in range(2):
+            c0, e0 = H * half, 640 * half
+            for b in range(4):
+                cp(A("yt", e0 + b, e0 + 640, 4), ind(A("dw", 480 * b, 480 * b + 480), A("lu", 10 * half, 10 * half + 10)), "vs"[b % 2])
+            quant(A("zq", c0, c0 + H), A("zs", c0, c0 + H), A("yt", e0, e0 + 640))
+        for half in range(2):
+            c0, e0, nq, ns = H * half, 640 * half, "tq%d" % (t + 1), "ts%d" % (t + 1)
+            for b in range(4):
+                mm(4 + b, "wq", "wp", 128 * b, "zq", "zs", c0, c0 + H)
+                mm(b, "eq", "es", 128 * b, "zq", "zs", c0, c0 + H)
+            for b in range(4):
+                rl = A("rl", C * b + c0, C * b + c0 + H)
+                act(rl, P(4 + b, 0, H), AF.Relu, 0.03125)
+                tt(A("xa", e0 + b, e0 + 640, 4), P(b, 0, H), rl, add)
+            quant(A(nq, c0, c0 + H), A(ns, c0, c0 + H), A("xa", e0, e0 + 640))
+            if t + 1 < R:
+                send_t(t + 1, half)
+            else:
+                dma("y", T.oc[:, 4 * c0:4 * c0 + 640], u8(A(nq, c0, c0 + H)), "dout")
+                if half == 0:
+                    cp(A("er"), ind(A("j1"), A("lu", 64, 74)), "s")
+                    dma("y", T.ol[:], A("er", rows=slice(0, 128, 16)), "dout")
+
+    mm(0, "vq", "vs", 0, "tq3", "ts3")
+    for k in range(4):
+        dma("s", T.osc[4 * k:4 * k + 4, :], A("ts3", rows=slice(32 * k, 32 * k + 4)), "dout")
+    cp(A("ysb"), P(0))
+    dma("y", T.y[:], A("ysb"), "dout")
+    for s in total:
+        wait("g", (s, total[s]))

@@ -5,18 +5,18 @@ F32, BF, I32, U16, U8, MX, F16 = "float32", "bfloat16", "int32", "uint16", "uint
 SCRATCH = {"ps": ("psum", [128, 4096], F32)}
 for _n, _w, _t in [
     ("x0", 1280, BF), ("xa", 1280, BF), ("ut", 512, BF), ("vt", 512, BF), ("uq", 128, MX), ("us", 128, U8), ("up", 512, MX), ("ups", 512, U8),
-    ("vq", 128, MX), ("vs", 128, U8), ("wq", 512, MX), ("wp", 512, U8), ("one", 512, BF), ("et", 2048, BF), ("eq", 512, MX), ("es", 512, U8),
+    ("vq", 128, MX), ("vs", 128, U8), ("wq", 512, MX), ("wp", 512, U8), ("one", 528, BF), ("e0", 528, BF), ("et", 2048, BF), ("eq", 512, MX), ("es", 512, U8),
     ("bq", 160, MX), ("bs", 160, U8), ("zq", 320, MX), ("zs", 320, U8), ("bt", 640, BF), ("yt", 1280, BF), ("dw", 1920, BF), ("dp", 1280, BF),
     ("tm", 640, F32), ("rl", 1280, F32), ("ysb", 320, F32), ("er", 160, F32),
     ("xt", 1280, F32), ("fl", 9600, BF), ("sg", 9600, BF), ("so", 6400, BF), ("ac", 120, F32), ("eqf", 1280, BF), ("eqs", 1280, BF), ("eqm", 320, BF),
     ("cf", 3200, BF), ("pf", 1616, F16), ("x1", 320, F16), ("x2", 320, F16), ("cu", 352, F32),
-    ("ck", 120, F32), ("ce", 40, F32), ("d1", 50, F32), ("p1", 20, F32), ("ra", 40, I32), ("rt", 80, I32), ("rb", 20, I32), ("ba", 20, I32),
+    ("ck", 120, F32), ("ce", 40, F32), ("d1", 40, F32), ("ra", 40, I32), ("rt", 80, I32), ("rb", 20, I32), ("ba", 20, I32),
     ("rau", 40, U16), ("bau", 40, U16), ("sa", 320, BF), ("cn", 320, BF), ("j1", 320, F32), ("j3", 320, F32), ("eb", 320, F32), ("enc", 320, BF), ("lo", 320, BF),
     ("sc1", 640, BF), ("sc2", 640, BF), ("xs", 640, BF), ("st", 640, BF), ("oa", 640, BF), ("wa", 704, BF), ("w0", 704, BF), ("w1", 704, BF),
     ("yy", 320, BF), ("an", 320, BF), ("la", 32, U16), ("li", 64, U16), ("ex", 128, F32), ("e2", 64, F32), ("e3", 32, F32), ("obu", 32, U16),
     ("e4", 64, F32), ("e5", 32, F32), ("lnu", 32, U16), ("xc", 704, BF),
-    ("fg", 64, F32), ("mm", 20, F32), ("stb", 640, BF), ("bw", 640, BF), ("wb", 352, BF), ("wb2", 352, BF), ("xb", 704, BF), ("rn", 320, BF), ("pm", 320, BF),
-    ("pr", 128, F32), ("a1", 128, F32), ("jj", 192, F32), ("ysu", 32, U16), ("se", 496, BF), ("lu", 80, U16),
+    ("fg", 64, F32), ("mm", 20, F32), ("stb", 640, BF), ("bw", 640, BF), ("wb", 352, BF), ("wb2", 352, BF), ("xb", 704, BF), ("rn", 320, BF), ("pm", 336, BF),
+    ("jj", 192, F32), ("ysu", 32, U16), ("se", 496, BF), ("lu", 80, U16),
     ("tbl", 640, BF), ("zz", 640, BF), ("ti", 2560, BF), ("pi", 8, I32), ("ui", 32, I32), ("ul", 32, U16), ("cc", 64, F32), ("ci", 72, F32), ("cl", 72, U16),
     ("ia", 60, F32),
 ]:
@@ -28,7 +28,7 @@ for _t in range(R):
     SCRATCH["lq%d" % _t] = ("sbuf", [128, C], MX)
     SCRATCH["ls%d" % _t] = ("sbuf", [128, C], U8)
     SCRATCH["sn%d" % _t] = ("sbuf", [128, 180], F32)
-SEMAPHORES = (["cv", "cs", "cp", "cg", "dx", "dx2", "du", "dv", "dwq", "dwp", "dtb", "dsa", "dz", "dout", "sent"]
+SEMAPHORES = (["cv", "cs", "cp", "cg", "dx", "dx2", "du", "dv", "dwq", "dwp", "dtb", "dsa", "det", "dz", "dout", "sent"]
               + ["a%s%d" % (k, t) for k in "qrsn" for t in range(R)])
 
 NS = [(4, 4, 4, 4), (5, 4, 4, 4), (5, 4, 4, 4)]
@@ -137,8 +137,8 @@ def rank_program(g, core, T, topo):
         else:
             op("v", lambda: g.vector.tensor_scalar(out[0], a[0], x(s1), x(s2), o0, o1), [out], [a, s1, s2])
 
-    def scan(out, d0, d1, o0, o1=ALU.add):
-        op("v", lambda: g.vector.tensor_tensor_scan(out[0], d0[0], d1[0], 0.0, o0, o1), [out], [d0, d1])
+    def scan(out, d0, d1, o0, o1=ALU.add, first=0.0):
+        op("v", lambda: g.vector.tensor_tensor_scan(out[0], d0[0], d1[0], first, o0, o1), [out], [d0, d1])
 
     def tr(out, in_):
         op("v", lambda: g.vector.transpose(out[0], in_[0]), [out], [in_])
@@ -250,13 +250,12 @@ def rank_program(g, core, T, topo):
     cp(K(0, 4), A("pi", 1, 5))
     fill(A("zz"), 0.0)
     zero = [A(w) for w in ("cn", "sc1", "st", "tbl", "sc2", "stb", "se")]
-    zero += [A(w, c, c + 16) for w in ("wa", "xb", "w0", "w1", "wb", "wb2", "xc") for c in (0, 336)]
+    zero += [A(w, c, c + 16) for w in ("wa", "xb", "w0", "w1", "wb", "wb2", "xc") for c in (0, 336)] + [A("pm", 0, 16)]
     for a in zero:
         dma("y", a, A("zz", 0, bin(a[1][0][1]).count("1")), "dz", 16 * len(zero))
     tt(K(4), K(2), r, ALU.not_equal)
     for k, v in ((23, 1.0), (24, 3.0), (25, 5.0), (26, 4.0), (19, 10.0), (20, 12.0)):
         ts(K(k), i4, v, ALU.is_equal)
-    ts(K(27), i4, 1.0, ALU.not_equal)
     ts(K(28), i4, 9.0, mn)
     ts(K(15), i4, 32.0, mul, 512.0, add)
     for k, src, a, b in ((5, r, -32.0, 368.0), (7, K(3), 32.0, 16.0), (14, i4, 32.0, 0.0), (11, r, 16.0, 0.0), (12, r, 17.0, 0.0), (13, r, -16.0, 0.0),
@@ -303,11 +302,10 @@ def rank_program(g, core, T, topo):
             iota(A("ti", 1920 + e, 2560, 2, rows=low), [[16, 20], [0, 16]], 320 * e)
         for k in range(4):
             dma("y", A("tbl", rows=slice(k, 128, 16)), A("ti", 640 * k, 640 * k + 640, rows=slice(0, 8)), "dtb", 64)
+        sel(A("e0"), A("one"), [[-1, 528]], ALU.is_equal, 3, 4)
         for b in range(4):
-            sel(A("et", 512 * b, 512 * b + 512), A("one"), [[-1, 512]], ALU.is_equal, b, 4)
+            dma("y", A("et", 512 * b, 512 * b + 512), A("e0", 3 - b, 515 - b), "det", 64)
         iota(A("jj", 0, 64), [[0, 2], [16, 32]])
-        for k in range(R):
-            iota(A("sn%d" % k, 20, 32), [[0, 12]])
         iota(A("j1"), [[1, 320]])
         count_constants(1)
         count_constants(2)
@@ -366,8 +364,8 @@ def rank_program(g, core, T, topo):
                 unit(*u)
 
         def scores(half, q_, s_):
-            for tau in range(2):
-                for e in range(2):
+            for e in range(2):
+                for tau in range(2):
                     mm(4 * e + 2 * tau + half, "up", "ups", 128 * (2 * h + tau), q_, s_)
             for tau in range(2):
                 tr(A("xt", 640 * tau + C * half, 640 * tau + C * half + C), P(2 * tau + half))
@@ -383,13 +381,17 @@ def rank_program(g, core, T, topo):
         def ends(slot0, c0, c1):
             return A("so", 160 * (slot0 + c0) + 159, 160 * (slot0 + c1), 160)
 
-        def same(kind, out):
+        def differences(kind):
             k0 = 0 if kind == "a" else 20
             for c0, c1, q, half in runs(kind, t):
                 if q == "s":
                     tt(A("d1", k0 + c0, k0 + c1), A("ac", k0 + c0, k0 + c1), A("ac", 60 + k0 + c0, 60 + k0 + c1), sub)
+
+        def places(kind, out, halves):
+            k0 = 0 if kind == "a" else 20
             for c0, c1, q, half in sorted(runs(kind, t), key=lambda u: u[2] == "s"):
-                tt(A(out, c0, c1), ends(k0, c0, c1) if q == "v" else A("d1", k0 + c0, k0 + c1), A("ce", k0 + c0, k0 + c1), add)
+                if half in halves:
+                    tt(A(out, c0, c1), ends(k0, c0, c1) if q == "v" else A("d1", k0 + c0, k0 + c1), A("ce", k0 + c0, k0 + c1), add)
 
         scores(h, tq, tsc)
         units("s", "a", h)
@@ -402,17 +404,21 @@ def rank_program(g, core, T, topo):
         unit(*mine[-2])
         f2 = ties(1, h)
         unit(*mine[-1])
-        f1()
-        if t == 0:
-            mid_constants()
-            late_constants()
         scores(1 - h, lq, ls)
         units("s", "a", 1 - h)
         flush("s")
         f3 = ties(0, 1 - h)
-        units("v", "a", 1 - h)
+        theirs = listed("v", "a", 1 - h)
+        unit(*theirs[0])
+        if t == 0:
+            mid_constants()
+            late_constants()
+        for u in theirs[1:-1]:
+            unit(*u)
+        f1()
         f2()
         f3()
+        unit(*theirs[-1])
         f4 = ties(1, 1 - h)
         for c in range(10):
             unit("s", "x", c)
@@ -427,20 +433,25 @@ def rank_program(g, core, T, topo):
             if rest:
                 unit(*rest.pop(0))
 
-        flush("v")
-        same("a", "ra")
-        f4()
+        gap()
+        differences("a")
+        places("a", "ra", (0, 1))
+        gap()
         cp(A("rau", 0, 20), A("ra", 0, 20))
         ts(A("rt", 0, 20), A("ra", 0, 20), 1, band)
-        gap()
+        f4()
+        flush("v")
         scat(A("sc1"), A("rau", 0, 20), A("sa"))
         ts(A("rt", 20, 40), A("rt", 0, 20), -2.0, mul, 1.0, add)
+        gap()
         tr(A("xs"), A("sc1"))
         tt(A("ra", 20, 40), A("ra", 0, 20), A("rt", 20, 40), add)
+        flush("v")
         for ks, kd in ((8, 4), (0, 6), (1, 7), (2, 9), (3, 10)):
             for hh in range(2):
                 tt(A("st", kd + 16 * hh, 640, 32), A("xs", ks, 640, 32), A("xs", 16 + ks, 640, 32), add)
         cp(A("rau", 20, 40), A("ra", 20, 40))
+        gap()
         tr(A("oa"), A("st"))
         gap()
         tt(A("wa", 16, 336), ind(A("oa"), A("rau", 20, 40)), A("cn"), add)
@@ -449,30 +460,25 @@ def rank_program(g, core, T, topo):
         shifted("wa")
         other("wa")
         cp(A("ex", 0, 64), ind(A("xb"), L(4, 8)))
-        gap()
-        tt(A("e3", 0, 20), A("ex", 0, 20), A("ex", 32, 52), add)
         while rest:
             gap()
         flush("v")
         for k in range(2):
             scan(A("pf", 805 * k + 5, 805 * k + 805), A("cf", 1600 * k, 1600 * k + 1600, 2), A("cf", 1600 * k + 1, 1600 * k + 1600, 2), add)
-        cp(A("la", 0, 20), A("e3", 0, 20))
+        tt(A("e3", 0, 20), A("ex", 0, 20), A("ex", 32, 52), add)
         for k in range(2):
             tr(A("x1", 160 * k, 160 * k + 160), A("pf", 805 * k + 9, 805 * k + 805, 5))
             tr(A("x2", 160 * k, 160 * k + 160), A("pf", 805 * k + 4, 805 * k + 800, 5))
         if t == 0:
             tt(A("ci", 36, 56), A("ia", 40, 60), A("ia", 0, 20), add)
+        cp(A("la", 0, 20), A("e3", 0, 20))
+        tt(A("ce", 20, 30), A("ce", 20, 30), A("ac", 40, 50), add)
         scan(A("cu", 32, 352), A("x1"), A("x2"), add, sub)
-        if t == 0:
-            quant(A("eq"), A("es"), A("et"))
-        same("b", "p1")
-        tt(A("d1", 40, 50), A("cu", 63, 352, 32), A("cu", 31, 320, 32), sub)
-        tt(A("rb", 0, 10), A("p1", 0, 10), A("ac", 40, 50), add)
-        tt(A("rb", 10, 20), A("p1", 10, 20), A("d1", 40, 50), sub)
-        for b in range(4):
-            mm(4 + b, "eq", "es", 128 * b, lq, ls)
-        for b in range(4):
-            mm(b, "eq", "es", 128 * b, tq, tsc)
+        differences("b")
+        tt(A("ce", 30, 40), A("ce", 30, 40), A("cu", 63, 352, 32), sub)
+        places("b", "rb", (0,))
+        tt(A("ce", 30, 40), A("ce", 30, 40), A("cu", 31, 320, 32), add)
+        places("b", "rb", (1,))
         if t == 0:
             cp(L(0, 4), A("ci", 0, 4))
             cp(L(28, 56), A("ci", 28, 56))
@@ -487,32 +493,34 @@ def rank_program(g, core, T, topo):
         cp(A("bau", 0, 20), A("ba"))
         cp(A("w1", 16, 336), ind(A("w0"), A("la", 0, 20)), "s")
         scat(A("sc2"), A("bau", 0, 20), A("sa"))
+        if t == 0:
+            quant(A("eq"), A("es"), A("et"))
+        for b in range(4):
+            mm(4 + b, "eq", "es", 128 * b, lq, ls)
+        for b in range(4):
+            mm(b, "eq", "es", 128 * b, tq, tsc)
         cp(A("wb", 16, 336), ind(A("w0"), L(36, 56)), "s")
         lin(A("an"), ind(A("wa"), L(36, 56)), 1.0, K(50))
         tr(A("xs"), A("sc2"))
         own("w1")
         cp(A("ex"), ind(A("xs"), L(28, 36)))
-        other("w1", 0, 192)
+        other("w1")
         tt(A("e2"), A("ex", 0, 64), A("ex", 64, 128), add)
-        other("w1", 192, 352)
         tt(A("e3", 0, 20), A("e2", 0, 20), A("e2", 32, 52), add)
         cp(A("obu", 0, 20), A("e3", 0, 20))
         cp(A("w0", 16, 336), ind(A("w1"), A("obu", 0, 20)))
 
         def first_round(s):
             if s == 0:
-                lists(((68, 40, 3), (70, 40, 2), (8, 40, 4), (10, 40, 5), (12, 40, 0), (14, 44, 16), (16, 40, 1), (18, 44, 17)))
+                lists(((68, 40, 3), (70, 40, 2), (8, 40, 4), (10, 40, 5), (12, 40, 0), (14, 44, 16), (16, 40, 0), (18, 40, 0)))
             if s == 1:
                 lists((), ((20, 40, 12), (21, 40, 10), (22, 44, 28), (23, 44, 26), (24, 40, 13), (25, 40, 9), (26, 44, 29), (27, 44, 25)))
             if s in (2, 3):
                 for j, d in enumerate((116.0, 116.0, 52.0, 52.0, 116.0, 116.0)):
                     lin(A("ci", 44 + 6 * s + j, 45 + 6 * s + j), K(18) if s == 3 else r, d, K(34 + j % 5))
-            if s == 4:
-                lin(A("pm"), A("one", 0, 320), K(27), 0.0)
             if s == 5:
                 lin(A("jj", 64, 128), A("jj", 0, 64), 1.0, K(35))
                 lin(A("jj", 128, 192), A("jj", 64, 128), 1.0, 144.0)
-                lin(A("jj", 64, 128), A("jj", 64, 128), 1.0, 145.0)
 
         fillers = [lambda: own("wb", "xc"), lambda: shifted("wb", "xc"),
                    lambda: cp(L(56, 72), A("ci", 56, 72)) if t == 0 else None, lambda: cp(A("e4"), ind(A("xc"), L(68, 72))),
@@ -547,21 +555,16 @@ def rank_program(g, core, T, topo):
         cp(A("fg"), ind(A("xb"), L(8, 12)))
         tt(A("mm", 0, 10), A("fg", 0, 10), A("fg", 42, 52), mn)
         tt(A("mm", 10, 20), A("fg", 32, 42), A("fg", 10, 20), mn)
-        for k in (0, 1, 16, 17):
+        for k in (0, 16):
             tt(A("stb", k, 320, 32), A("mm", 0, 10), A("mm", 10, 20), ALU.is_lt)
             tt(A("stb", 320 + k, 640, 32), A("mm", 0, 10), A("mm", 10, 20), ALU.is_gt)
         tr(A("bw"), A("stb"))
-        cp(A("rn"), ind(A("bw"), A("lnu", 0, 20)))
-        scan(A("wb2", 16, 336), A("pm"), A("rn"), mul)
+        ts(A("rn"), ind(A("bw"), A("lnu", 0, 20)), -511.0, mul, 512.0, add)
+        lin(A("pm", 16, 336), ind(A("bw"), A("lnu", 0, 20)), 512.0, -512.0)
+        scan(A("wb2", 16, 336), A("pm", 15, 335), A("rn"), add, add, -1.0)
         own("wb2")
         shifted("wb2")
-        cp(A("pr"), ind(A("xb"), L(12, 20)))
-        tt(A("a1", 0, 20), A("pr", 0, 20), A("jj", 64, 84), sub)
-        tt(A("a1", 32, 52), A("pr", 32, 52), A("jj", 96, 116), sub)
-        tt(A("a1", 64, 84), A("a1", 0, 20), A("pr", 64, 84), mul)
-        tt(A("a1", 96, 116), A("a1", 32, 52), A("pr", 96, 116), mul)
-        tt(A(sn, 0, 20), A("a1", 64, 84), A("jj", 128, 148), add)
-        tt(A(sn, 32, 52), A("a1", 96, 116), A("jj", 160, 180), add)
+        tt(A(sn, 0, 64), ind(A("xb"), L(12, 16)), A("jj", 128, 192), mn)
         cp(A("ysu", 0, 20), A(sn, 0, 20))
         scat(A("se", 16, 496), A("ysu", 0, 20), A("an"))
         tr(A("xb", 16, 176), A("se", 16, 176))
@@ -576,10 +579,10 @@ def rank_program(g, core, T, topo):
                 pick_u(1 - h)
         k = 5 if t == R - 1 else 4
         cp(A("lu", 0, 16 * k), ind(A(sn, 0, 116 + w), L(56 + 6 * h, 56 + 6 * h + k)))
+        for b in (3, 0, 1, 2):
+            cp(A("tm", 160 * b, 160 * b + 160), ind(A("dp", C * b, C * b + C), A("lu", 32, 42)), "v" if b == 3 else "s")
         for b in range(4):
-            win = A("dp", C * b, C * b + C)
-            cp(A("tm", 160 * b, 160 * b + 160), ind(win, A("lu", 32, 42)), "s")
-            tt(A("bt", b, 640, 4), ind(win, A("lu", 48, 58)), A("tm", 160 * b, 160 * b + 160), add)
+            tt(A("bt", b, 640, 4), ind(A("dp", C * b, C * b + C), A("lu", 48, 58)), A("tm", 160 * b, 160 * b + 160), add)
         quant(A("bq"), A("bs"), A("bt"))
         for b in range(4):
             mm(b, "eq", "es", 128 * b, "bq", "bs", 0, H)
@@ -594,6 +597,7 @@ def rank_program(g, core, T, topo):
             c0, e0, nq, ns = H * half, 640 * half, "tq%d" % (t + 1), "ts%d" % (t + 1)
             for b in range(4):
                 mm(4 + b, "wq", "wp", 128 * b, "zq", "zs", c0, c0 + H)
+            for b in range(4):
                 mm(b, "eq", "es", 128 * b, "zq", "zs", c0, c0 + H)
             for b in range(4):
                 rl = A("rl", C * b + c0, C * b + c0 + H)
@@ -608,10 +612,11 @@ def rank_program(g, core, T, topo):
                     cp(A("er"), ind(A("j1"), A("lu", 64, 74)), "s")
                     dma("y", T.ol[:], A("er", rows=slice(0, 128, 16)), "dout")
 
-    mm(0, "vq", "vs", 0, "tq3", "ts3")
+    for half in range(2):
+        mm(4 + half, "vq", "vs", 0, "tq3", "ts3", H * half, H * half + H)
+        cp(A("ysb", H * half, H * half + H), P(4 + half, 0, H), "sv"[half])
+        dma("sy"[half], T.y[:, H * half:H * half + H], A("ysb", H * half, H * half + H), "dout")
     for k in range(4):
         dma("s", T.osc[4 * k:4 * k + 4, :], A("ts3", rows=slice(32 * k, 32 * k + 4)), "dout")
-    cp(A("ysb"), P(0))
-    dma("y", T.y[:], A("ysb"), "dout")
     for s in total:
         wait("g", (s, total[s]))

@@ -12,13 +12,13 @@ for _n, _w, _t in [
     ("cf", 3200, BF), ("pf", 1616, F16), ("x1", 320, F16), ("x2", 320, F16), ("cu", 352, F32),
     ("ck", 120, F32), ("ce", 40, F32), ("d1", 40, F32), ("ra", 40, I32), ("rt", 80, I32), ("rb", 20, I32), ("ba", 20, I32),
     ("rau", 40, U16), ("bau", 40, U16), ("sa", 320, BF), ("cn", 320, BF), ("j1", 320, F32), ("j3", 320, F32), ("eb", 320, F32), ("enc", 320, BF), ("lo", 320, BF),
-    ("sc1", 640, BF), ("sc2", 640, BF), ("xs", 640, BF), ("st", 640, BF), ("oa", 640, BF), ("wa", 704, BF), ("w0", 704, BF), ("w1", 704, BF),
-    ("yy", 320, BF), ("an", 320, BF), ("la", 32, U16), ("li", 64, U16), ("ex", 128, F32), ("e2", 64, F32), ("e3", 32, F32), ("obu", 32, U16),
+    ("sc1", 640, BF), ("sc2", 640, BF), ("xs", 640, BF), ("st", 640, BF), ("oa", 640, BF), ("wa", 704, BF), ("w0", 896, BF), ("w1", 896, BF),
+    ("yy", 320, BF), ("kx", 640, BF), ("tl", 40, F32), ("tlu", 40, U16), ("la", 32, U16), ("li", 64, U16), ("ex", 128, F32), ("e3", 32, F32), ("obu", 32, U16),
     ("e4", 64, F32), ("e5", 32, F32), ("lnu", 32, U16), ("xc", 704, BF),
     ("fg", 64, F32), ("mm", 20, F32), ("stb", 640, BF), ("bw", 640, BF), ("wb", 352, BF), ("wb2", 352, BF), ("xb", 704, BF), ("rn", 320, BF), ("pm", 336, BF),
     ("jj", 192, F32), ("ysu", 32, U16), ("se", 496, BF), ("lu", 80, U16),
-    ("tbl", 640, BF), ("zz", 640, BF), ("ti", 2560, BF), ("pi", 8, I32), ("ui", 32, I32), ("ul", 32, U16), ("cc", 64, F32), ("ci", 72, F32), ("cl", 72, U16),
-    ("ia", 60, F32),
+    ("tbl", 640, BF), ("zz", 640, BF), ("ti", 1312, BF), ("pi", 8, I32), ("ui", 32, I32), ("ul", 32, U16), ("cc", 64, F32), ("ci", 72, F32), ("cl", 72, U16),
+    ("ia", 160, F32),
 ]:
     SCRATCH[_n] = ("sbuf", [128, _w], _t)
 for _t in range(R + 1):
@@ -249,20 +249,21 @@ def rank_program(g, core, T, topo):
     cp(A("ul"), A("ui"))
     cp(K(0, 4), A("pi", 1, 5))
     fill(A("zz"), 0.0)
-    zero = [A(w) for w in ("cn", "sc1", "st", "tbl", "sc2", "stb", "se")]
-    zero += [A(w, c, c + 16) for w in ("wa", "xb", "w0", "w1", "wb", "wb2", "xc") for c in (0, 336)] + [A("pm", 0, 16)]
+    zero = [A(w) for w in ("cn", "sc1", "st", "kx", "sc2", "stb", "se")]
+    zero += [A(w, c, c + 16) for w in ("wa", "xb", "wb", "wb2", "xc") for c in (0, 336)] + [A("pm", 0, 16)]
+    zero += [A(w, c, c + 448) for w in ("w0", "w1") for c in (0, 448)]
     for a in zero:
         dma("y", a, A("zz", 0, bin(a[1][0][1]).count("1")), "dz", 16 * len(zero))
     tt(K(4), K(2), r, ALU.not_equal)
-    for k, v in ((23, 1.0), (24, 3.0), (25, 5.0), (26, 4.0), (19, 10.0), (20, 12.0)):
+    for k, v in ((25, 5.0), (26, 4.0), (19, 10.0), (20, 12.0)):
         ts(K(k), i4, v, ALU.is_equal)
     ts(K(28), i4, 9.0, mn)
     ts(K(15), i4, 32.0, mul, 512.0, add)
     for k, src, a, b in ((5, r, -32.0, 368.0), (7, K(3), 32.0, 16.0), (14, i4, 32.0, 0.0), (11, r, 16.0, 0.0), (12, r, 17.0, 0.0), (13, r, -16.0, 0.0),
-                         (16, r, -704.0, 368.0), (18, r, -1.0, 1.0), (22, r, 368.0, 16.0), (29, r, -704.0, 336.0), (30, r, -352.0, -16.0), (49, r, -320.0, 0.0),
+                         (16, r, 128.0, 32.0), (18, r, -1.0, 1.0), (22, K(2), -160.0, 160.0), (29, r, -2.0, 1.0), (30, r, 32.0, 240.0), (49, r, -320.0, 0.0),
                          (34, i4, 1.0, 0.0), (35, i4, 1.0, 16.0), (36, K(28), 1.0, 84.0), (37, K(28), 1.0, 100.0), (38, K(28), 1.0, 52.0),
-                         (9, K(4), K(5), K(7)), (33, K(24), 1.0, 1.0), (6, K(26), 1.0, K(25)), (48, K(19), 1.0, K(20)), (17, r, 496.0, K(35)),
-                         (31, K(23), K(29), K(22)), (8, K(6), -1.0e6, 1.0e6), (50, K(48), K(49), 0.0), (32, K(24), K(30), K(31))):
+                         (9, K(4), K(5), K(7)), (6, K(26), 1.0, K(25)), (48, K(19), 1.0, K(20)), (17, i4, 1.0, K(16)),
+                         (31, K(3), 1.0, K(22)), (8, K(6), -1.0e6, 1.0e6), (50, K(48), K(49), 0.0)):
         lin(K(k), src, a, b)
     for half in range(2):
         quant(A("tq0", H * half, H * half + H), A("ts0", H * half, H * half + H), A("x0", 640 * half, 640 * half + 640))
@@ -274,34 +275,43 @@ def rank_program(g, core, T, topo):
     ts(K(10), K(9), 256.0, add, 672.0, mn)
     for k, src, b in ((40, K(9, 11), K(11)), (42, K(9, 11), K(12)), (44, K(9, 11), K(13)), (46, K(14, 16), r)):
         lin(K(k, k + 2), src, 1.0, b)
-    lists(((4, 42, 6), (6, 40, 9)))
+    lists(((4, 42, 6),))
     tie_mask(2)
     tie_mask(3)
     iota(A("j3"), [[16, 20], [0, 16]])
     iota(A("eb"), [[0, 5], [32, 4], [1, 16]], 128)
     iota(A("lo"), [[0, 20], [1, 16]])
+    low = slice(0, 32)
+    iota(A("ti", 0, 128, rows=low), [[2, 128]], -512)
+    iota(A("ti", 128, 288, rows=low), [[1, 160]], 96)
+    iota(A("ti", 288, 352, rows=low), [[2, 64]], 256)
+    iota(A("ti", 352, 672, rows=low), [[1, 320]], -240)
     count_constants(0)
 
     def mid_constants():
-        ts(A("sa"), A("j3"), K(33), mul, K(32), add)
+        ts(A("sa"), A("j3"), 2.0, mul, K(11), add)
         for k in range(5):
             ts(A("enc", 64 * k, 64 * k + 64), A("eb", 64 * k, 64 * k + 64), K(11), add, float(2 ** k), mul)
-        cp(L(4, 8), A("ci", 4, 8))
+        cp(L(4, 6), A("ci", 4, 6))
         for d, kd, s, ks in (("cn", 12, "sa", 3), ("sa", 2, "lo", 2), ("sa", 8, "enc", 8), ("cn", 5, "enc", 5), ("cn", 13, "lo", 13)):
-            dma("y", A(d, rows=slice(kd, 128, 16)), A(s, rows=slice(ks, 128, 16)), "dsa", 80)
+            dma("y", A(d, rows=slice(kd, 128, 16)), A(s, rows=slice(ks, 128, 16)), "dsa", 144)
+        for k in range(2):
+            for hh in range(2):
+                c0 = 352 if k == hh else 32 * (1 - k)
+                dma("y", A("sa", rows=slice(k + 16 * hh, 128, 32)), A("ti", c0, c0 + 320, rows=slice(0, 4)), "dsa", 144)
 
     def late_constants():
-        low = slice(0, 32)
         iota(A("pf", 4, 810, 805), [[0, 2]])
         iota(A("cu", 0, 32), [[0, 32]])
-        for k, base, d in ((0, 16, 368), (1, 352, -336)):
-            for e in range(2):
-                iota(A("ti", 640 * k + e, 640 * k + 640, 2, rows=low), [[16, 10], [d, 2], [0, 16]], base + 160 * (1 - e))
-        iota(A("ti", 1280, 1920, rows=low), [[0, 20], [1, 16], [0, 2]])
-        for e in range(2):
-            iota(A("ti", 1920 + e, 2560, 2, rows=low), [[16, 20], [0, 16]], 320 * e)
-        for k in range(4):
-            dma("y", A("tbl", rows=slice(k, 128, 16)), A("ti", 640 * k, 640 * k + 640, rows=slice(0, 8)), "dtb", 64)
+        iota(A("tl"), [[16, 10], [320, 2], [8, 2]])
+        for hh in range(2):
+            iota(A("ti", 672 + 320 * hh, 992 + 320 * hh, rows=low), [[-320, 2], [32, 10], [0, 16]], 320 + 16 * hh)
+        for hh in range(2):
+            for k in range(2):
+                c0 = 352 if k == hh else 32 * (1 - k)
+                dma("y", A("kx", 320 * hh, 320 * hh + 320, rows=slice(k, 128, 16)), A("ti", c0, c0 + 320, rows=slice(0, 8)), "dtb", 112)
+            dma("y", A("kx", 320 * hh, 320 * hh + 320, rows=slice(2, 128, 16)), A("lo", rows=slice(0, 8)), "dtb", 112)
+        dma("y", A("kx", rows=slice(3, 128, 16)), A("ti", 672, 1312, rows=slice(0, 8)), "dtb", 112)
         sel(A("e0"), A("one"), [[-1, 528]], ALU.is_equal, 3, 4)
         for b in range(4):
             dma("y", A("et", 512 * b, 512 * b + 512), A("e0", 3 - b, 515 - b), "det", 64)
@@ -310,14 +320,35 @@ def rank_program(g, core, T, topo):
         count_constants(1)
         count_constants(2)
 
+    def O(w, pad=0):
+        c0 = 272 if w in ("w0", "w1") else 16
+        return A(w, c0 - pad, c0 + 320 + pad)
+
+    def natural_list():
+        i_, a_, b_, m_ = A("ia", 40, 60), A("ia", 60, 80), A("ia", 80, 100), A("ia", 100, 120)
+        ts(A("tlu"), A("tl"), K(31), add)
+        ts(i_, A("ia", 0, 20), K(17), add)
+        ts(m_, A("ia", 20, 40), K(29), mul, r, add)
+        ts(a_, i_, 128.0, ALU.is_lt)
+        ts(b_, i_, 288.0, sub, 0.0, ALU.max)
+        ts(A("ia", 120, 140), i_, 480.0, sub)
+        ts(A("ia", 140, 160), i_, K(30), add)
+        tt(a_, a_, A("ia", 120, 140), mul)
+        ts(b_, b_, K(30), sub, 480.0, add)
+        tt(a_, a_, b_, add)
+        tt(a_, a_, m_, mul)
+        tt(A("ci", 36, 56), a_, A("ia", 140, 160), add)
+
     def own(w, xb="xb"):
-        tr(A(xb, 16, 336), A(w, 16, 336))
+        tr(A(xb, 16, 336), O(w))
 
     def shifted(w, xb="xb"):
-        tr(A(xb, 352, 704), A(w, 0, 352))
+        tr(A(xb, 352, 704), O(w, 16))
 
-    def other(w, lo=0, hi=352):
-        tr(A(w, 352 + lo, 352 + hi), A("xb", lo, hi))
+    def other(w):
+        tr(A(w, 608, 768), A("xb", 128, 288))
+        tr(A(w, 0, 256, 2), A("xb", 0, 128))
+        tr(A(w, 768, 896, 2), A("xb", 288, 352))
 
     for t in range(R):
         h = hs[t]
@@ -422,11 +453,13 @@ def rank_program(g, core, T, topo):
         f4 = ties(1, 1 - h)
         for c in range(10):
             unit("s", "x", c)
+        if t == 0:
+            natural_list()
+            cp(A("tbl"), ind(A("kx"), A("tlu")), "s")
         units("s", "b", 1 - h)
         flush("s")
         if t == 0:
-            lin(A("ia", 40, 60), A("ia", 20, 40), K(16), K(17))
-            lists(((0, 42, 0), (2, 40, 2), (28, 46, 0), (30, 14, 2), (32, 46, 16), (34, 14, 18)))
+            lists(((0, 42, 0), (28, 46, 0), (30, 46, 16)))
         rest = listed("v", "b", 1 - h)
 
         def gap():
@@ -458,20 +491,15 @@ def rank_program(g, core, T, topo):
         gap()
         own("wa")
         shifted("wa")
-        other("wa")
-        cp(A("ex", 0, 64), ind(A("xb"), L(4, 8)))
         while rest:
             gap()
         flush("v")
         for k in range(2):
             scan(A("pf", 805 * k + 5, 805 * k + 805), A("cf", 1600 * k, 1600 * k + 1600, 2), A("cf", 1600 * k + 1, 1600 * k + 1600, 2), add)
-        tt(A("e3", 0, 20), A("ex", 0, 20), A("ex", 32, 52), add)
+        ts(A("la"), ind(A("xb"), L(4, 6)), 512.0, add)
         for k in range(2):
             tr(A("x1", 160 * k, 160 * k + 160), A("pf", 805 * k + 9, 805 * k + 805, 5))
             tr(A("x2", 160 * k, 160 * k + 160), A("pf", 805 * k + 4, 805 * k + 800, 5))
-        if t == 0:
-            tt(A("ci", 36, 56), A("ia", 40, 60), A("ia", 0, 20), add)
-        cp(A("la", 0, 20), A("e3", 0, 20))
         tt(A("ce", 20, 30), A("ce", 20, 30), A("ac", 40, 50), add)
         scan(A("cu", 32, 352), A("x1"), A("x2"), add, sub)
         differences("b")
@@ -480,18 +508,19 @@ def rank_program(g, core, T, topo):
         tt(A("ce", 30, 40), A("ce", 30, 40), A("cu", 31, 320, 32), add)
         places("b", "rb", (1,))
         if t == 0:
-            cp(L(0, 4), A("ci", 0, 4))
-            cp(L(28, 56), A("ci", 28, 56))
+            cp(L(0, 2), A("ci", 0, 2))
+            cp(L(28, 32), A("ci", 28, 32))
+            cp(L(36, 56), A("ci", 36, 56))
         cp(A("bau", 20, 40), A("rb"))
         ts(A("rt", 0, 20), A("rb"), 1, band)
         ts(A("rt", 20, 40), A("rb"), 1, shr)
-        tt(A("w0", 16, 336), ind(A("tbl"), A("bau", 20, 40)), A("wa", 16, 336), add)
+        tt(O("w0"), ind(A("tbl"), A("bau", 20, 40)), A("wa", 16, 336), add)
         ts(A("rt", 40, 60), A("rt", 0, 20), 320.0, mul)
         own("w0")
         tt(A("ba"), A("rt", 40, 60), A("rt", 20, 40), add)
         other("w0")
         cp(A("bau", 0, 20), A("ba"))
-        cp(A("w1", 16, 336), ind(A("w0"), A("la", 0, 20)), "s")
+        cp(O("w1"), ind(A("w0"), A("la", 0, 20)), "s")
         scat(A("sc2"), A("bau", 0, 20), A("sa"))
         if t == 0:
             quant(A("eq"), A("es"), A("et"))
@@ -499,16 +528,18 @@ def rank_program(g, core, T, topo):
             mm(4 + b, "eq", "es", 128 * b, lq, ls)
         for b in range(4):
             mm(b, "eq", "es", 128 * b, tq, tsc)
-        cp(A("wb", 16, 336), ind(A("w0"), L(36, 56)), "s")
-        lin(A("an"), ind(A("wa"), L(36, 56)), 1.0, K(50))
-        tr(A("xs"), A("sc2"))
+        lin(O("wb"), ind(A("w0"), L(36, 56)), 1.0, K(50))
         own("w1")
-        cp(A("ex"), ind(A("xs"), L(28, 36)))
+        tr(A("xs"), A("sc2"))
         other("w1")
-        tt(A("e2"), A("ex", 0, 64), A("ex", 64, 128), add)
-        tt(A("e3", 0, 20), A("e2", 0, 20), A("e2", 32, 52), add)
-        cp(A("obu", 0, 20), A("e3", 0, 20))
-        cp(A("w0", 16, 336), ind(A("w1"), A("obu", 0, 20)))
+        cp(A("ex", 0, 64), ind(A("xs"), L(28, 32)))
+        if t:
+            own("wb", "xc")
+        tt(A("e3", 0, 20), A("ex", 0, 20), A("ex", 32, 52), add)
+        if t:
+            shifted("wb", "xc")
+        ts(A("obu", 0, 20), A("e3", 0, 20), 512.0, add)
+        cp(O("w0"), ind(A("w1"), A("obu", 0, 20)))
 
         def first_round(s):
             if s == 0:
@@ -522,13 +553,15 @@ def rank_program(g, core, T, topo):
                 lin(A("jj", 64, 128), A("jj", 0, 64), 1.0, K(35))
                 lin(A("jj", 128, 192), A("jj", 64, 128), 1.0, 144.0)
 
-        fillers = [lambda: own("wb", "xc"), lambda: shifted("wb", "xc"),
-                   lambda: cp(L(56, 72), A("ci", 56, 72)) if t == 0 else None, lambda: cp(A("e4"), ind(A("xc"), L(68, 72))),
-                   lambda: tt(A("e5", 0, 20), A("e4", 0, 20), A("e4", 32, 52), add), lambda: cp(A("lnu", 0, 20), A("e5", 0, 20)),
-                   lambda: cp(L(8, 28), A("ci", 8, 28)) if t == 0 else None]
+        fillers = [lambda: cp(A("e4"), ind(A("xc"), L(68, 72))),
+                   lambda: tt(A("e5", 0, 20), A("e4", 0, 20), A("e4", 32, 52), add), lambda: cp(A("lnu", 0, 20), A("e5", 0, 20))]
+        if t == 0:
+            fillers = ([lambda: own("wb", "xc"), lambda: shifted("wb", "xc"), lambda: None, lambda: None, lambda: cp(L(56, 72), A("ci", 56, 72))]
+                       + fillers[0:1] + [lambda: (fillers_last[0](), cp(L(8, 28), A("ci", 8, 28)))])
+            fillers_last = [lambda: tt(A("e5", 0, 20), A("e4", 0, 20), A("e4", 32, 52), add)]
         for s in range(8):
             cur, nxt, l0 = "w%d" % (s % 2), "w%d" % (1 - s % 2), 32 * (min(s, 6) % 2)
-            lin(A("yy"), A(cur, 16, 336), K(6), K(8))
+            lin(A("yy"), O(cur), K(6), K(8))
             if s < 4:
                 act(A("dp", C * s, C * s + C), P(4 + s), AF.Copy, 0.5)
             else:
@@ -538,18 +571,15 @@ def rank_program(g, core, T, topo):
             own(cur)
             if s < 7:
                 shifted(cur)
-                other(cur, 0, 192)
-                cp(A("ex", 0, 64), ind(A("xb"), L(0, 4)))
-                other(cur, 192, 352)
-                tt(A("e3", 0, 20), A("ex", 0, 20), A("ex", 32, 52), add)
-                if t or s > 2:
-                    for k in range(2 if t == 0 else 1):
-                        if fillers:
-                            fillers.pop(0)()
-                cp(A("li", l0, l0 + 20), A("e3", 0, 20))
-            else:
                 other(cur)
-            tt(A(nxt, 16, 336), ind(A(cur), A("li", l0, l0 + 20)), A("yy"), mn)
+                ts(A("li", l0, l0 + 32), ind(A("xb"), L(0, 2)), 512.0, add)
+                if fillers:
+                    fillers.pop(0)()
+            else:
+                if t == 0:
+                    cp(A("lnu", 0, 20), A("e5", 0, 20))
+                other(cur)
+            tt(O(nxt), ind(A(cur), A("li", l0, l0 + 20)), A("yy"), mn)
         own("w0")
         shifted("w0")
         cp(A("fg"), ind(A("xb"), L(8, 12)))
@@ -566,7 +596,7 @@ def rank_program(g, core, T, topo):
         shifted("wb2")
         tt(A(sn, 0, 64), ind(A("xb"), L(12, 16)), A("jj", 128, 192), mn)
         cp(A("ysu", 0, 20), A(sn, 0, 20))
-        scat(A("se", 16, 496), A("ysu", 0, 20), A("an"))
+        scat(A("se", 16, 496), A("ysu", 0, 20), O("wb"))
         tr(A("xb", 16, 176), A("se", 16, 176))
         tr(A("xb", 352, 544), A("se", 0, 192))
         cp(A("ex"), ind(A("xb"), L(20, 28)))

@@ -6,19 +6,18 @@ SCRATCH = {"ps": ("psum", [128, 4096], F32)}
 for _n, _w, _t in [
     ("x0", 1280, BF), ("xa", 1280, BF), ("ut", 512, BF), ("vt", 512, BF), ("uq", 128, MX), ("us", 128, U8), ("up", 512, MX), ("ups", 512, U8),
     ("vq", 128, MX), ("vs", 128, U8), ("wq", 512, MX), ("wp", 512, U8), ("one", 528, BF), ("e0", 528, BF), ("et", 2048, BF), ("eq", 512, MX), ("es", 512, U8),
-    ("bq", 160, MX), ("bs", 160, U8), ("zq", 320, MX), ("zs", 320, U8), ("bt", 640, BF), ("yt", 1280, BF), ("dw", 1920, BF), ("dp", 1280, BF),
-    ("tm", 640, F32), ("rl", 1280, F32), ("ysb", 320, F32), ("er", 160, F32),
-    ("xt", 1280, F32), ("fl", 9600, BF), ("sg", 9600, BF), ("so", 6400, BF), ("ac", 120, F32), ("eqf", 1280, BF), ("eqs", 1280, BF), ("eqm", 320, BF),
+    ("bq", 160, MX), ("bs", 160, U8), ("zq", 320, MX), ("zs", 320, U8), ("bt", 640, BF), ("bu", 640, BF), ("yt", 1280, BF), ("dw", 1920, BF), ("dp", 1280, BF),
+    ("rl", 1280, F32), ("ysb", 320, F32), ("er", 160, F32),
+    ("xt", 1280, F32), ("fl", 6400, BF), ("sg", 6400, BF), ("so", 8000, F16), ("ac", 120, F32), ("eqf", 1280, BF), ("eqs", 1280, BF), ("eqm", 320, BF),
     ("cf", 3200, BF), ("pf", 1616, F16), ("x1", 320, F16), ("x2", 320, F16), ("cu", 352, F32),
-    ("ck", 120, F32), ("ce", 40, F32), ("d1", 40, F32), ("ra", 40, I32), ("rt", 80, I32), ("rb", 20, I32), ("ba", 20, I32),
-    ("rau", 40, U16), ("bau", 40, U16), ("sa", 320, BF), ("cn", 320, BF), ("j1", 320, F32), ("j3", 320, F32), ("eb", 320, F32), ("enc", 320, BF), ("lo", 320, BF),
-    ("sc1", 640, BF), ("sc2", 640, BF), ("xs", 640, BF), ("st", 640, BF), ("oa", 640, BF), ("wa", 704, BF), ("w0", 896, BF), ("w1", 896, BF),
-    ("yy", 320, BF), ("kx", 640, BF), ("tl", 40, F32), ("tlu", 40, U16), ("la", 32, U16), ("li", 64, U16), ("ex", 128, F32), ("e3", 32, F32), ("obu", 32, U16),
-    ("e4", 64, F32), ("e5", 32, F32), ("lnu", 32, U16), ("xc", 704, BF),
-    ("fg", 64, F32), ("mm", 20, F32), ("stb", 640, BF), ("bw", 640, BF), ("wb", 352, BF), ("wb2", 352, BF), ("xb", 704, BF), ("rn", 320, BF), ("pm", 336, BF),
-    ("jj", 192, F32), ("ysu", 32, U16), ("se", 496, BF), ("lu", 80, U16),
-    ("tbl", 640, BF), ("zz", 640, BF), ("ti", 1312, BF), ("pi", 8, I32), ("ui", 32, I32), ("ul", 32, U16), ("cc", 64, F32), ("ci", 72, F32), ("cl", 72, U16),
-    ("ia", 160, F32),
+    ("ck", 60, F32), ("ce", 40, F32), ("d1", 40, F32), ("pb", 40, F32), ("rb", 20, F32), ("ii", 20, I32),
+    ("zl", 32, U16), ("xl", 20, U16), ("bl", 20, U16), ("az", 32, U16), ("mu", 32, U16), ("li", 64, U16), ("yl", 64, U16), ("lu", 32, U16), ("ou", 32, U16),
+    ("sa", 320, BF), ("sb", 320, BF), ("j1", 320, F32), ("sc1", 320, BF), ("xd", 384, BF), ("oa", 704, BF), ("wa", 320, BF), ("wi", 320, BF), ("xw", 544, BF),
+    ("s2", 320, BF), ("pr", 320, BF), ("sc2", 640, BF), ("xs", 640, BF), ("st", 640, BF), ("ob", 640, BF), ("w0", 1056, BF), ("w1", 1056, BF),
+    ("yy", 320, BF), ("yz", 320, BF), ("o2", 320, BF), ("xb", 704, BF), ("xc", 704, BF), ("mm", 60, F32), ("stb", 640, BF), ("bw", 656, BF),
+    ("wb", 352, BF), ("wb2", 352, BF), ("jj", 128, F32), ("yp", 64, F32), ("se", 816, BF), ("oe", 96, BF),
+    ("zz", 704, BF), ("ti", 1920, BF), ("pi", 8, I32), ("ui", 32, I32), ("ul", 32, U16), ("cc", 64, F32), ("ci", 20, F32), ("cl", 20, U16),
+    ("rp", 8, F32), ("tl", 40, F32), ("tlu", 20, U16), ("s3", 320, F32),
 ]:
     SCRATCH[_n] = ("sbuf", [128, _w], _t)
 for _t in range(R + 1):
@@ -27,11 +26,15 @@ for _t in range(R + 1):
 for _t in range(R):
     SCRATCH["lq%d" % _t] = ("sbuf", [128, C], MX)
     SCRATCH["ls%d" % _t] = ("sbuf", [128, C], U8)
-    SCRATCH["sn%d" % _t] = ("sbuf", [128, 180], F32)
-SEMAPHORES = (["cv", "cs", "cp", "cg", "dx", "dx2", "du", "dv", "dwq", "dwp", "dtb", "dsa", "det", "dz", "dout", "sent"]
-              + ["a%s%d" % (k, t) for k in "qrsn" for t in range(R)])
+    SCRATCH["th%d" % _t] = ("sbuf", [128, 64], F32)
+    SCRATCH["rw%d" % _t] = ("sbuf", [128, 64], F32)
+    SCRATCH["ml%d" % _t] = ("sbuf", [128, 128], BF)
+    SCRATCH["sn%d" % _t] = ("sbuf", [128, 96], BF)
+SEMAPHORES = (["cv", "cs", "cp", "cg", "dx", "dx2", "du", "dv", "dwq", "dwp", "dsa", "dyz", "det", "dz", "dout", "sent", "dacc", "ao"]
+              + ["%s%d" % (k, t) for k in ("aq", "as", "an", "at", "ar", "ac", "am", "d1", "d2", "d3", "d4") for t in range(R)])
 
-NS = [(4, 4, 4, 4), (5, 4, 4, 4), (5, 4, 4, 4)]
+NS = (5, 5, 4, 5, 6)
+BIG = 1.0e6
 
 
 def rank_program(g, core, T, topo):
@@ -94,26 +97,30 @@ def rank_program(g, core, T, topo):
     def x(a):
         return a[0] if isinstance(a, tuple) else a
 
-    def dma(q, out, in_, sem, last=None):
+    def dma(q, out, in_, sem, last=None, adds=False):
         reads = in_[1] if isinstance(in_, tuple) else []
         writes = out[1] if isinstance(out, tuple) else []
         keep = {n: log.get(n, []) for n, m in writes}
         for n, m in writes:
-            log[n] = [e for e in log.get(n, []) if e[1][0] != sem]
+            log[n] = [e for e in log.get(n, []) if e[1][0] != sem or adds]
         order(q, reads, writes)
         for n in keep:
             log[n] = keep[n]
         total[sem] = total.get(sem, 0) + 16
-        Q[q].dma_start(x(out), x(in_)).then_inc(T.sem[sem], 16)
+        if adds:
+            Q[q].dma_start(x(out), x(in_), accum_op=ALU.add).then_inc(T.sem[sem], 16)
+        else:
+            Q[q].dma_start(x(out), x(in_)).then_inc(T.sem[sem], 16)
         note(q, (sem, last or total[sem]), reads, writes)
 
-    def send(dst, out, in_, sem):
+    def send(dst, out, in_, sem, here=None, parts=1):
+        here = here or out
         order("g", in_[1], [])
         rid, pid = topo.addr(dst)[0:2]
         g.remote_dma(out[0], in_[0], T.sem[sem], T.sem["sent"], pid, rid, topo.mask(core, dst))
         total["sent"] = total.get("sent", 0) + len(topo.engines(core, dst))
-        total[sem] = len(topo.engines(dst, core))
-        note("r", (sem, total[sem]), [], out[1])
+        total[sem] = parts * len(topo.engines(dst, core))
+        note("r", (sem, total[sem]), [], here[1])
 
     def u8(a):
         return (a[0].bitcast(dt.uint8), a[1])
@@ -181,42 +188,19 @@ def rank_program(g, core, T, topo):
     def K(i, j=None):
         return A("cc", i, (i if j is None else j - 1) + 1)
 
-    def L(i, j):
-        return A("cl", i, j)
-
-    add, sub, mul, mn = ALU.add, ALU.subtract, ALU.mult, ALU.min
+    add, sub, mul, mn, mx = ALU.add, ALU.subtract, ALU.mult, ALU.min, ALU.max
     band, shr = ALU.bitwise_and, ALU.arith_shift_right
     parts = [rank ^ (1 << t) for t in range(R)]
     hs = [1 if rank > p else 0 for p in parts]
     H = C // 2
 
-    def send_t(t, half):
-        dst = T.cores[parts[t]]
-        send(dst, u8(A("lq%d" % t, H * half, H * half + H)), u8(A("tq%d" % t, H * half, H * half + H)), "a%s%d" % ("qr"[half], t))
-        if half:
-            send(dst, A("ls%d" % t), A("ts%d" % t), "as%d" % t)
+    LISTS = [("next", 32, ((16, 369), (384, 33))), ("turn", 32, ((18, 19), (34, 35))), ("own", 32, ((16, 368), (384, 32))), ("far", 32, ((32, 352), (400, 16))),
+             ("zm", 1, ((0, 40), (24, 12))), ("mm0", 2, ((1, 97), (65, 33))), ("mm1", 2, ((32, 64), (96, 0))),
+             ("mg0", 2, ((0, 64), (1, 65))), ("mg1", 2, ((64, 0), (65, 1))), ("ol", 2, (((32, 64), (33, 65)), ((64, 32), (65, 33)))[hs[R - 1]])]
 
-    def runs(kind, t):
-        out = []
-        for half in range(2):
-            n = NS[t]["ab".index(kind) + (0 if half == hs[t] else 2)]
-            if n:
-                out.append((10 * half, 10 * half + n, "s", half))
-            if n < 10:
-                out.append((10 * half + n, 10 * half + 10, "v", half))
-        return out
-
-    def count_constants(t):
-        for k, kind in enumerate("ab"):
-            for c0, c1, q, half in runs(kind, t):
-                iota(A("ck", 40 * t + 20 * k + c0, 40 * t + 20 * k + c1), [[32 if q == "s" else 0, c1 - c0]],
-                     320 * half + (32 * (c0 % 10) + 32 if q == "s" else 160))
-
-    def lists(pairs, singles=()):
-        for c0, k, b in pairs:
-            lin(A("ci", c0, c0 + 2), K(k, k + 2), 1.0, float(b))
-        for c0, k, b in singles:
-            lin(A("ci", c0, c0 + 1), K(k), 1.0, float(b))
+    def L(name, k=1):
+        i = [e[0] for e in LISTS].index(name)
+        return A("cl", 2 * i, 2 * i + 2 * k)
 
     def tie_mask(a):
         rows = slice(32 * a, 32 * a + 32)
@@ -228,134 +212,122 @@ def rank_program(g, core, T, topo):
         op("v", lambda: g.vector.tensor_copy(o_[0].bitcast(dt.uint32), i_[0]), [o_], [i_])
         cp(A("ups", 256 * hh, 256 * hh + 256), ind(A("us"), l_), "s")
 
-    dma("y", A("x0", 0, 640), T.x[:, 0:640], "dx")
     dma("s", A("ut"), T.u[:], "du")
+    dma("y", A("x0", 0, 640), T.x[:, 0:640], "dx")
     dma("y", A("x0", 640, 1280), T.x[:, 640:1280], "dx2")
+    iota(A("pi", 0, 1), [[0, 1]], 0, 1, False)
+    iota(A("ui"), [[8, 4], [32, 4], [0, 2]], 0, 0, False)
+    fill(A("one"), 1.0)
+    iota(A("rp", 0, 2), [[8, 2]])
+    tie_mask(0)
+    tie_mask(1)
+    p0 = A("pi", 0, 1)
+    i4, run, hq, par, p5, both = K(0), K(1), K(2), K(3), K(4), K(5)
+    ts(A("pi", 1, 2), p0, 15, band)
+    ts(A("pi", 2, 3), p0, 4, shr, 1, band)
+    ts(A("pi", 3, 4), p0, 1, shr, 7, band)
+    ts(A("pi", 4, 5), p0, 1, band)
+    ts(A("pi", 5, 6), p0, 31, band)
+    cp(A("ul"), A("ui"))
+    fill(A("zz"), 0.0)
+    cp(K(0, 5), A("pi", 1, 6))
+    for t in range(R):
+        fill(A("rw%d" % t, 24, 64), 0.0)
+        fill(A("rw%d" % t, 12 * hs[t] + 8, 12 * hs[t] + 12), 0.0)
+        fill(A("sn%d" % t, 64, 96), 0.0)
+        fill(A("ml%d" % t), 0.0)
+    tt(both, par, run, mul)
+    ts(K(6), i4, 5.0, ALU.is_equal)
+    ts(K(7), i4, 6.0, ALU.is_equal)
+    fill(A("st"), BIG)
+    fill(A("yz"), BIG)
+    fill(A("xd"), 0.0)
+    fill(A("w0"), 0.0)
+    fill(A("w1"), 0.0)
+    keep_, big_, base_ = K(8), K(9), K(10)
+    lin(keep_, K(6), 1.0, K(7))
+    lin(base_, run, -64.0, 560.0)
+    lin(K(11), run, 320.0, 0.0)
+    lin(K(12), run, -384.0, 384.0)
+    for level in range(5):
+        for i, (name, step, b) in enumerate(LISTS):
+            k0, k1 = K(20 + i), K(30 + i)
+            if level == 0:
+                lin(k0, hq, float(step), float(b[0][0]))
+            elif level == 4:
+                lin(A("ci", 2 * i, 2 * i + 2), A("rp", 0, 2), float(step), k1)
+            else:
+                src, f = ((par, b[1][0] - b[0][0]), (run, b[0][1] - b[0][0]), (both, b[1][1] - b[1][0] - b[0][1] + b[0][0]))[level - 1]
+                lin(*((k1, src, float(f), k0) if level % 2 else (k0, src, float(f), k1)))
+    lin(big_, keep_, -BIG, BIG)
+    quant(A("uq"), A("us"), A("ut"))
+    pick_u(1 - hs[0])
+    for half in range(2):
+        quant(A("tq0", H * half, H * half + H), A("ts0", H * half, H * half + H), A("x0", 640 * half, 640 * half + 640))
+    pick_u(hs[0])
     dma("y", u8(A("wq")), T.wc[:], "dwq")
     dma("y", A("wp"), T.ws[:], "dwp")
     dma("y", A("vt"), T.v[:], "dv")
-    iota(A("pi", 0, 1), [[0, 1]], 0, 1, False)
-    iota(A("ui"), [[8, 4], [32, 4], [0, 2]], 0, 0, False)
-    iota(A("ia", 0, 20), [[16, 10], [0, 2]])
-    iota(A("ia", 20, 40), [[0, 10], [1, 2]])
-    fill(A("one"), 1.0)
-    tie_mask(0)
-    tie_mask(1)
-    p0, i4, r = A("pi", 0, 1), K(0), K(1)
-    ts(A("pi", 1, 2), p0, 15, band)
-    ts(A("pi", 2, 3), p0, 4, shr, 1, band)
-    ts(A("pi", 3, 4), p0, 1, band)
-    ts(A("pi", 4, 5), p0, 1, shr, 7, band)
-    cp(A("ul"), A("ui"))
-    cp(K(0, 4), A("pi", 1, 5))
-    fill(A("zz"), 0.0)
-    zero = [A(w) for w in ("cn", "sc1", "st", "kx", "sc2", "stb", "se")]
-    zero += [A(w, c, c + 16) for w in ("wa", "xb", "wb", "wb2", "xc") for c in (0, 336)] + [A("pm", 0, 16)]
-    zero += [A(w, c, c + 448) for w in ("w0", "w1") for c in (0, 448)]
+    zero = [A(w) for w in ("xw", "xb", "xc", "stb", "oe")] + [A("bw", 320, 336), A("se", 0, 176), A("se", 496, 816)]
+    zero += [A(w, c, c + 16) for w in ("wb", "wb2") for c in (0, 336)]
     for a in zero:
         dma("y", a, A("zz", 0, bin(a[1][0][1]).count("1")), "dz", 16 * len(zero))
-    tt(K(4), K(2), r, ALU.not_equal)
-    for k, v in ((25, 5.0), (26, 4.0), (19, 10.0), (20, 12.0)):
-        ts(K(k), i4, v, ALU.is_equal)
-    ts(K(28), i4, 9.0, mn)
-    ts(K(15), i4, 32.0, mul, 512.0, add)
-    for k, src, a, b in ((5, r, -32.0, 368.0), (7, K(3), 32.0, 16.0), (14, i4, 32.0, 0.0), (11, r, 16.0, 0.0), (12, r, 17.0, 0.0), (13, r, -16.0, 0.0),
-                         (16, r, 128.0, 32.0), (18, r, -1.0, 1.0), (22, K(2), -160.0, 160.0), (29, r, -2.0, 1.0), (30, r, 32.0, 240.0), (49, r, -320.0, 0.0),
-                         (34, i4, 1.0, 0.0), (35, i4, 1.0, 16.0), (36, K(28), 1.0, 84.0), (37, K(28), 1.0, 100.0), (38, K(28), 1.0, 52.0),
-                         (9, K(4), K(5), K(7)), (6, K(26), 1.0, K(25)), (48, K(19), 1.0, K(20)), (17, i4, 1.0, K(16)),
-                         (31, K(3), 1.0, K(22)), (8, K(6), -1.0e6, 1.0e6), (50, K(48), K(49), 0.0)):
-        lin(K(k), src, a, b)
-    for half in range(2):
-        quant(A("tq0", H * half, H * half + H), A("ts0", H * half, H * half + H), A("x0", 640 * half, 640 * half + 640))
-        send_t(0, half)
-        if half == 0:
-            quant(A("uq"), A("us"), A("ut"))
-    pick_u(hs[0])
-    ts(K(15), K(15), 608.0, mn)
-    ts(K(10), K(9), 256.0, add, 672.0, mn)
-    for k, src, b in ((40, K(9, 11), K(11)), (42, K(9, 11), K(12)), (44, K(9, 11), K(13)), (46, K(14, 16), r)):
-        lin(K(k, k + 2), src, 1.0, b)
-    lists(((4, 42, 6),))
     tie_mask(2)
     tie_mask(3)
-    iota(A("j3"), [[16, 20], [0, 16]])
-    iota(A("eb"), [[0, 5], [32, 4], [1, 16]], 128)
-    iota(A("lo"), [[0, 20], [1, 16]])
-    low = slice(0, 32)
-    iota(A("ti", 0, 128, rows=low), [[2, 128]], -512)
-    iota(A("ti", 128, 288, rows=low), [[1, 160]], 96)
-    iota(A("ti", 288, 352, rows=low), [[2, 64]], 256)
-    iota(A("ti", 352, 672, rows=low), [[1, 320]], -240)
-    count_constants(0)
+    for k in range(6):
+        n, lift = NS[(0, 1, 2, 3, 2, 3)[k]], 320 * (k // 4)
+        iota(A("ck", 10 * k, 10 * k + n), [[32, n]], 32 + lift)
+        iota(A("ck", 10 * k + n, 10 * k + 10), [[0, 10 - n]], 160 + lift)
 
-    def mid_constants():
-        ts(A("sa"), A("j3"), 2.0, mul, K(11), add)
+    def early_constants():
+        iota(A("tl", 0, 20), [[32, 10], [320, 2]])
+        for c0, n, step, base in ((0, 320, 1, -160), (320, 160, 2, -496), (480, 160, 2, 176), (640, 192, 2, -496), (832, 128, 2, 240), (960, 320, 1, -96)):
+            iota(A("ti", c0, c0 + n), [[step, n]], base)
         for k in range(5):
-            ts(A("enc", 64 * k, 64 * k + 64), A("eb", 64 * k, 64 * k + 64), K(11), add, float(2 ** k), mul)
-        cp(L(4, 6), A("ci", 4, 6))
-        for d, kd, s, ks in (("cn", 12, "sa", 3), ("sa", 2, "lo", 2), ("sa", 8, "enc", 8), ("cn", 5, "enc", 5), ("cn", 13, "lo", 13)):
-            dma("y", A(d, rows=slice(kd, 128, 16)), A(s, rows=slice(ks, 128, 16)), "dsa", 144)
-        for k in range(2):
-            for hh in range(2):
-                c0 = 352 if k == hh else 32 * (1 - k)
-                dma("y", A("sa", rows=slice(k + 16 * hh, 128, 32)), A("ti", c0, c0 + 320, rows=slice(0, 4)), "dsa", 144)
-
-    def late_constants():
+            iota(A("ti", 1280 + 128 * k, 1408 + 128 * k), [[2 ** k, 128]], 128 * 2 ** k)
+        iota(A("s3"), [[32, 10], [0, 32]], -160)
         iota(A("pf", 4, 810, 805), [[0, 2]])
         iota(A("cu", 0, 32), [[0, 32]])
-        iota(A("tl"), [[16, 10], [320, 2], [8, 2]])
+
+    def table_constants():
+        cp(A("sa"), ind(A("ti", 0, 640), A("tlu")), "s")
+        cp(A("sb"), ind(A("ti", 640, 1280), A("tlu")), "s")
+        lin(A("s2"), A("s3"), 1.0, p5)
+        low = slice(0, 4)
         for hh in range(2):
-            iota(A("ti", 672 + 320 * hh, 992 + 320 * hh, rows=low), [[-320, 2], [32, 10], [0, 16]], 320 + 16 * hh)
-        for hh in range(2):
-            for k in range(2):
-                c0 = 352 if k == hh else 32 * (1 - k)
-                dma("y", A("kx", 320 * hh, 320 * hh + 320, rows=slice(k, 128, 16)), A("ti", c0, c0 + 320, rows=slice(0, 8)), "dtb", 112)
-            dma("y", A("kx", 320 * hh, 320 * hh + 320, rows=slice(2, 128, 16)), A("lo", rows=slice(0, 8)), "dtb", 112)
-        dma("y", A("kx", rows=slice(3, 128, 16)), A("ti", 672, 1312, rows=slice(0, 8)), "dtb", 112)
+            for r_, c0 in ((0, 320 * hh), (1, 640 + 320 * hh), (6, 1280 + 320 * hh)):
+                dma("y", A("sa", rows=slice(r_ + 16 * hh, 128, 32)), A("ti", c0, c0 + 320, rows=low), "dsa", 128)
+            dma("y", A("yz", rows=slice(5 + 16 * hh, 128, 32)), A("ti", 1280 + 320 * hh, 1600 + 320 * hh, rows=low), "dyz", 32)
+        dma("y", A("sa", rows=slice(7, 128, 16)), A("ti", 0, 320, rows=slice(0, 8)), "dsa", 128)
+        dma("y", A("sa", rows=slice(3, 128, 16)), A("sb", rows=slice(3, 128, 16)), "dsa", 128)
+
+    def late_constants():
         sel(A("e0"), A("one"), [[-1, 528]], ALU.is_equal, 3, 4)
         for b in range(4):
             dma("y", A("et", 512 * b, 512 * b + 512), A("e0", 3 - b, 515 - b), "det", 64)
-        iota(A("jj", 0, 64), [[0, 2], [16, 32]])
+        iota(A("jj", 0, 64), [[320, 2], [16, 32]], 160)
+        iota(A("se", 176, 496), [[1, 320]], -80)
         iota(A("j1"), [[1, 320]])
-        count_constants(1)
-        count_constants(2)
 
     def O(w, pad=0):
-        c0 = 272 if w in ("w0", "w1") else 16
+        c0 = 400 if w in ("w0", "w1") else 16
         return A(w, c0 - pad, c0 + 320 + pad)
 
-    def natural_list():
-        i_, a_, b_, m_ = A("ia", 40, 60), A("ia", 60, 80), A("ia", 80, 100), A("ia", 100, 120)
-        ts(A("tlu"), A("tl"), K(31), add)
-        ts(i_, A("ia", 0, 20), K(17), add)
-        ts(m_, A("ia", 20, 40), K(29), mul, r, add)
-        ts(a_, i_, 128.0, ALU.is_lt)
-        ts(b_, i_, 288.0, sub, 0.0, ALU.max)
-        ts(A("ia", 120, 140), i_, 480.0, sub)
-        ts(A("ia", 140, 160), i_, K(30), add)
-        tt(a_, a_, A("ia", 120, 140), mul)
-        ts(b_, b_, K(30), sub, 480.0, add)
-        tt(a_, a_, b_, add)
-        tt(a_, a_, m_, mul)
-        tt(A("ci", 36, 56), a_, A("ia", 140, 160), add)
+    def own(w, xb="xb", back=0):
+        tr(A(xb, 16 - back, 336 - back), O(w))
 
-    def own(w, xb="xb"):
-        tr(A(xb, 16, 336), O(w))
-
-    def shifted(w, xb="xb"):
-        tr(A(xb, 352, 704), O(w, 16))
+    def shifted(w, xb="xb", back=0):
+        tr(A(xb, 352 - back, 704 - back), O(w, 16))
 
     def other(w):
-        tr(A(w, 608, 768), A("xb", 128, 288))
-        tr(A(w, 0, 256, 2), A("xb", 0, 128))
-        tr(A(w, 768, 896, 2), A("xb", 288, 352))
+        tr(A(w, 0, 384, 2), A("xb", 0, 192))
+        tr(A(w, 736, 1056, 2), A("xb", 192, 352))
 
     for t in range(R):
         h = hs[t]
-        tq, tsc, lq, ls, sn = "tq%d" % t, "ts%d" % t, "lq%d" % t, "ls%d" % t, "sn%d" % t
-        if t:
-            iota(A("sc1"), [[0, 640]])
-            iota(A("sc2"), [[0, 640]])
+        tq, tsc, lq, ls = "tq%d" % t, "ts%d" % t, "lq%d" % t, "ls%d" % t
+        th, rw, ml, sn = "th%d" % t, "rw%d" % t, "ml%d" % t, "sn%d" % t
+        dst = T.cores[parts[t]]
         pend = {"v": [], "s": []}
         cnt = {"v": 0, "s": 0}
 
@@ -363,23 +335,26 @@ def rank_program(g, core, T, topo):
             while len(pend[q]) > keep:
                 pend[q].pop(0)()
 
-        def unit(q, kind, c):
-            tau, key, n = (0 if kind == "a" else 1), c // 10, 32 * (c % 10) + 32
-            slot = 20 * "abx".index(kind) + c
-            thr = A("xt", 640 * tau + 32 * c, 640 * tau + 32 * c + 1)
-            f0 = C * (cnt[q] % 30)
+        def unit(q, k, c):
+            n, slot = 32 * c + 32, 10 * k + c
+            thr = A("xt", C * k + 32 * c, C * k + 32 * c + 1) if k < 4 else A(th, 16 + c, 17 + c)
+            f0 = C * (cnt[q] % 20)
             cnt[q] += 1
-            if kind == "x":
+            if k == 4:
                 f = A("cf", c, 3200, 10)
-                act(f, P(7), AF.Sign, -1.0, thr)
-                pend[q].append(lambda: act(f, f, AF.Relu, -1.0, None, A("ac", slot, slot + 1)))
+                if q == "s":
+                    act(f, P(7), AF.Sign, -1.0, thr)
+                    pend[q].append(lambda: act(f, f, AF.Relu, 1.0 - 2.0 * h, None, A("ac", slot, slot + 1)))
+                else:
+                    ts(f, P(3), thr, ALU.is_gt if h else ALU.is_lt)
+                    pend[q].append(lambda: scan(A("so", 160 * slot, 160 * slot + 160), A("cf", c, 1600, 10), A("cf", 1600 + c, 3200, 10), add))
             elif q == "v":
-                ts(A("fl", f0, f0 + n), P(2 * tau + key, 0, n), thr, ALU.is_ge, 0.5, sub)
+                ts(A("fl", f0, f0 + n), P(k, 0, n), thr, ALU.is_ge, 0.5, sub)
                 if n < C:
-                    ts(A("fl", f0 + n, f0 + C), P(2 * tau + key, n, C), thr, ALU.is_gt, 0.5, sub)
+                    ts(A("fl", f0 + n, f0 + C), P(k, n, C), thr, ALU.is_gt, 0.5, sub)
                 pend[q].append(lambda: scan(A("so", 160 * slot, 160 * slot + 160), A("fl", f0, f0 + 160), A("fl", f0 + 160, f0 + C), add))
             else:
-                act(A("sg", f0, f0 + C), P(4 + 2 * tau + key), AF.Sign, -1.0, thr)
+                act(A("sg", f0, f0 + C), P(4 + k), AF.Sign, -1.0, thr)
 
                 def second():
                     act(A("sg", f0, f0 + n), A("sg", f0, f0 + n), AF.Relu, None, None, A("ac", 60 + slot, 61 + slot))
@@ -387,237 +362,234 @@ def rank_program(g, core, T, topo):
                 pend[q].append(second)
             flush(q, 1)
 
-        def listed(q, kind, half):
-            return [(q, kind, c) for c0, c1, qq, hf in runs(kind, t) if qq == q and hf == half for c in range(c0, c1)]
+        def units(q, k):
+            return [(q, k, c) for c in (range(NS[k]) if q == "s" else range(NS[k], 10))]
 
-        def units(q, kind, half):
-            for u in listed(q, kind, half):
+        def run_units(us):
+            for u in us:
                 unit(*u)
 
-        def scores(half, q_, s_):
-            for e in range(2):
-                for tau in range(2):
-                    mm(4 * e + 2 * tau + half, "up", "ups", 128 * (2 * h + tau), q_, s_)
-            for tau in range(2):
-                tr(A("xt", 640 * tau + C * half, 640 * tau + C * half + C), P(2 * tau + half))
+        def thresholds(k):
+            tr(A("xt", C * k, C * k + C), P(k))
 
-        def ties(tau, half):
-            c0 = 640 * tau + C * half
-            k0 = 20 * tau + 10 * half
-            tt(A("eqf", c0, c0 + C), P(2 * tau + half), A("xt", c0, c0 + C), ALU.is_equal)
+        def ties(k):
+            c0, k0 = C * k, 10 * k
+            tt(A("eqf", c0, c0 + C), P(k), A("xt", c0, c0 + C), ALU.is_equal)
             flush("v")
             pend["v"].append(lambda: scan(A("eqs", c0, c0 + C), A("eqm"), A("eqf", c0, c0 + C), mul))
-            return lambda: tt(A("ce", k0, k0 + 10), A("ck", 40 * t + k0, 40 * t + k0 + 10), A("eqs", c0 + 31, c0 + C, 32), sub)
 
-        def ends(slot0, c0, c1):
-            return A("so", 160 * (slot0 + c0) + 159, 160 * (slot0 + c1), 160)
+        def tie_sums(k):
+            k1 = 10 * (k + 2 * h if k > 1 else k)
+            tt(A("ce", 10 * k, 10 * k + 10), A("ck", k1, k1 + 10), A("eqs", C * k + 31, C * k + C, 32), sub)
 
-        def differences(kind):
-            k0 = 0 if kind == "a" else 20
-            for c0, c1, q, half in runs(kind, t):
-                if q == "s":
-                    tt(A("d1", k0 + c0, k0 + c1), A("ac", k0 + c0, k0 + c1), A("ac", 60 + k0 + c0, 60 + k0 + c1), sub)
+        def ends(k, c0, c1):
+            return A("so", 160 * (10 * k + c0) + 159, 160 * (10 * k + c1), 160)
 
-        def places(kind, out, halves):
-            k0 = 0 if kind == "a" else 20
-            for c0, c1, q, half in sorted(runs(kind, t), key=lambda u: u[2] == "s"):
-                if half in halves:
-                    tt(A(out, c0, c1), ends(k0, c0, c1) if q == "v" else A("d1", k0 + c0, k0 + c1), A("ce", k0 + c0, k0 + c1), add)
+        def differences(k):
+            k0 = 10 * k
+            tt(A("d1", k0, k0 + NS[k]), A("ac", k0, k0 + NS[k]), A("ac", 60 + k0, 60 + k0 + NS[k]), sub)
 
-        scores(h, tq, tsc)
-        units("s", "a", h)
-        units("s", "b", h)
-        units("v", "a", h)
-        mine = listed("v", "b", h)
-        for u in mine[:-2]:
-            unit(*u)
-        f1 = ties(0, h)
-        unit(*mine[-2])
-        f2 = ties(1, h)
-        unit(*mine[-1])
-        scores(1 - h, lq, ls)
-        units("s", "a", 1 - h)
-        flush("s")
-        f3 = ties(0, 1 - h)
-        theirs = listed("v", "a", 1 - h)
-        unit(*theirs[0])
+        def places(k, name, c0):
+            k0, n = 10 * k, NS[k]
+            tt(A(name, c0 + n, c0 + 10), ends(k, n, 10), A("ce", k0 + n, k0 + 10), add)
+            tt(A(name, c0, c0 + n), A("d1", k0, k0 + n), A("ce", k0, k0 + n), add)
+
+        def self_count(k, between=()):
+            us, between = units("v", k), list(between)
+            ties(k)
+            for u in us:
+                unit(*u)
+                if between:
+                    between.pop(0)()
+            for f in between:
+                f()
+            tie_sums(k)
+
+        for k in range(4):
+            for e in range(2):
+                mm(4 * e + k, "up", "ups", 128 * (2 * (h if k % 2 else 1 - h) + k // 2), tq, tsc)
+        thresholds(0)
+        thresholds(2)
+        thresholds(1)
+        cp(A(th, 0, 10), A("xt", 2 * C, 3 * C, 32))
+        send(dst, A(th, 16, 26), A(th, 0, 10), "at%d" % t)
         if t == 0:
-            mid_constants()
+            early_constants()
+        iota(A("sc2"), [[0, 640]])
+        run_units(units("s", 0) + units("s", 1))
+        self_count(0)
+        flush("s")
+        mine = units("v", 1)
+        ties(1)
+        unit(*mine[0])
+        differences(0)
+        unit(*mine[1])
+        places(0, rw, 52)
+        send(dst, A(rw, 12 * h, 12 * h + 12), A(rw, 52, 64), "ar%d" % t, A(rw, 12 - 12 * h, 24 - 12 * h))
+        run_units(mine[2:])
+        tie_sums(1)
+        thresholds(3)
+        if t == 0:
+            ts(A("cl"), A("ci"), 703.0, mn)
+            ts(A("tlu"), A("tl", 0, 20), p5, add)
+            table_constants()
+        run_units(units("s", 2))
+        flush("s")
+        self_count(2, [lambda: differences(1), lambda: places(1, rw, 12 * h)])
+        dma("y", A(rw, 24, 34, rows=slice(0, 112)), A(rw, 0, 10, rows=slice(16, 128)), "d1%d" % t)
+        dma("y", A(rw, 40, 50, rows=slice(16, 128)), A(rw, 12, 22, rows=slice(0, 112)), "d2%d" % t)
+        run_units(units("s", 4))
+        flush("s")
+        cross = units("v", 4)
+        unit(*cross[0])
+        differences(2)
+        unit(*cross[1])
+        places(2, th, 32)
+        send(dst, A(th, 48, 58), A(th, 32, 42), "ac%d" % t)
+        for half in range(2):
+            send(dst, u8(A(lq, H * half, H * half + H)), u8(A(tq, H * half, H * half + H)), "aq%d" % t, None, 2)
+        send(dst, A(ls), A(tsc), "as%d" % t)
+        if t == 0:
             late_constants()
-        for u in theirs[1:-1]:
-            unit(*u)
-        f1()
-        f2()
-        f3()
-        unit(*theirs[-1])
-        f4 = ties(1, 1 - h)
-        for c in range(10):
-            unit("s", "x", c)
-        if t == 0:
-            natural_list()
-            cp(A("tbl"), ind(A("kx"), A("tlu")), "s")
-        units("s", "b", 1 - h)
-        flush("s")
-        if t == 0:
-            lists(((0, 42, 0), (28, 46, 0), (30, 46, 16)))
-        rest = listed("v", "b", 1 - h)
+        run_units(cross[2:])
+        rest = units("v", 3)
+        srest = units("s", 3)
 
         def gap():
             if rest:
                 unit(*rest.pop(0))
 
-        gap()
-        differences("a")
-        places("a", "ra", (0, 1))
-        gap()
-        cp(A("rau", 0, 20), A("ra", 0, 20))
-        ts(A("rt", 0, 20), A("ra", 0, 20), 1, band)
-        f4()
+        run_units(srest[:3])
+        cp(A("zl"), ind(A(rw), L("zm")))
+        for k in range(2):
+            ts(A("xl", k, 20, 2), A(rw, 12 * k, 12 * k + 10), K(11 + k), add)
+            ts(A("ii", 10 * k, 10 * k + 10), A(rw, 12 * k, 12 * k + 10), 0.5, mul, 0.25, sub)
         flush("v")
-        scat(A("sc1"), A("rau", 0, 20), A("sa"))
-        ts(A("rt", 20, 40), A("rt", 0, 20), -2.0, mul, 1.0, add)
-        gap()
-        tr(A("xs"), A("sc1"))
-        tt(A("ra", 20, 40), A("ra", 0, 20), A("rt", 20, 40), add)
+        scat(A("sc1"), A("zl", 0, 20), A("sa"))
+        for k in range(2):
+            ts(A("s2", 24 - 16 * k, 320, 32), A("ii", 10 * k, 10 * k + 10), 240.0, sub)
+        for e in range(2):
+            tr(A("xd", 16 + 192 * e, 176 + 192 * e), A("sc1", e, 320, 2))
+        ties(3)
+        for e in range(2):
+            cp(A("xd", 21 + 192 * e, 176 + 192 * e, 16), A("xd", 214 - 192 * e, 368 - 192 * e, 16))
+        cp(A(ml, 0, 22), A("xd", 23, 368, 16))
+        send(dst, A(ml, 32, 54), A(ml, 0, 22), "am%d" % t)
+        up, down = (slice(0, 112), slice(16, 128)), (slice(16, 128), slice(0, 112))
+        for c0, s0, way, sem in ((64, 0, (up, down)[h], "d3%d" % t), (96, 32, (down, up)[h], "d4%d" % t)):
+            dma("y", A(ml, c0, c0 + 22, rows=way[0]), A(ml, s0, s0 + 22, rows=way[1]), sem)
         flush("v")
-        for ks, kd in ((8, 4), (0, 6), (1, 7), (2, 9), (3, 10)):
-            for hh in range(2):
-                tt(A("st", kd + 16 * hh, 640, 32), A("xs", ks, 640, 32), A("xs", 16 + ks, 640, 32), add)
-        cp(A("rau", 20, 40), A("ra", 20, 40))
-        gap()
-        tr(A("oa"), A("st"))
-        gap()
-        tt(A("wa", 16, 336), ind(A("oa"), A("rau", 20, 40)), A("cn"), add)
-        gap()
-        own("wa")
-        shifted("wa")
-        while rest:
-            gap()
-        flush("v")
+        for e in range(2):
+            tr(A("oa", 1 - e, 320, 2), A("xd", 16 + 192 * e, 176 + 192 * e))
+            tr(A("oa", 321 - e, 704, 2), A("xd", 192 * e, 192 + 192 * e))
+        flush("s")
+        cp(A("wa"), ind(A("oa"), A("xl")), "s")
+        run_units(srest[3:])
+        flush("s")
+        lin(A("wi"), A("wa"), keep_, big_)
+        tie_sums(3)
         for k in range(2):
             scan(A("pf", 805 * k + 5, 805 * k + 805), A("cf", 1600 * k, 1600 * k + 1600, 2), A("cf", 1600 * k + 1, 1600 * k + 1600, 2), add)
-        ts(A("la"), ind(A("xb"), L(4, 6)), 512.0, add)
+        gap()
         for k in range(2):
             tr(A("x1", 160 * k, 160 * k + 160), A("pf", 805 * k + 9, 805 * k + 805, 5))
             tr(A("x2", 160 * k, 160 * k + 160), A("pf", 805 * k + 4, 805 * k + 800, 5))
-        tt(A("ce", 20, 30), A("ce", 20, 30), A("ac", 40, 50), add)
+        gap()
         scan(A("cu", 32, 352), A("x1"), A("x2"), add, sub)
-        differences("b")
-        tt(A("ce", 30, 40), A("ce", 30, 40), A("cu", 63, 352, 32), sub)
-        places("b", "rb", (0,))
-        tt(A("ce", 30, 40), A("ce", 30, 40), A("cu", 31, 320, 32), add)
-        places("b", "rb", (1,))
-        if t == 0:
-            cp(L(0, 2), A("ci", 0, 2))
-            cp(L(28, 32), A("ci", 28, 32))
-            cp(L(36, 56), A("ci", 36, 56))
-        cp(A("bau", 20, 40), A("rb"))
-        ts(A("rt", 0, 20), A("rb"), 1, band)
-        ts(A("rt", 20, 40), A("rb"), 1, shr)
-        tt(O("w0"), ind(A("tbl"), A("bau", 20, 40)), A("wa", 16, 336), add)
-        ts(A("rt", 40, 60), A("rt", 0, 20), 320.0, mul)
-        own("w0")
-        tt(A("ba"), A("rt", 40, 60), A("rt", 20, 40), add)
-        other("w0")
-        cp(A("bau", 0, 20), A("ba"))
-        cp(O("w1"), ind(A("w0"), A("la", 0, 20)), "s")
-        scat(A("sc2"), A("bau", 0, 20), A("sa"))
+        n4, far = NS[4], (sub, add)[h]
+        tt(A("rb", 1 - h, 2 * n4, 2), A(th, 48, 48 + n4), A("ac", 40, 40 + n4), far)
+        tt(A("rb", 1 - h + 2 * n4, 20, 2), A(th, 48 + n4, 58), ends(4, n4, 10), far)
+        gap()
+        tt(A("pb", 0, 10), A("cu", 63, 352, 32), A("cu", 31, 320, 32), sub)
+        gap()
+        tt(A("ce", 30, 40), A("ce", 30, 40), A("pb", 0, 10), (add, sub)[h])
+        while rest:
+            gap()
+        tr(A("pr"), A("s2"))
+        flush("v")
+        differences(3)
+        tr(A("xw", 18, 338), A("wa"))
+        n3 = NS[3]
+        tt(A("rb", h + 2 * n3, 20, 2), ends(3, n3, 10), A("ce", 30 + n3, 40), add)
+        tt(A("rb", h, 2 * n3, 2), A("d1", 30, 30 + n3), A("ce", 30, 30 + n3), add)
+        ts(A("az"), ind(A("xw"), L("turn")), base_, add)
+        cp(A("bl"), A("rb"))
+        scat(A("sc2"), A("bl"), A("wa"))
         if t == 0:
             quant(A("eq"), A("es"), A("et"))
+            lin(A("jj", 64, 128), A("jj", 0, 64), 1.0, i4)
+        for b in range(4):
+            mm(b, "eq", "es", 128 * b, tq, tsc)
         for b in range(4):
             mm(4 + b, "eq", "es", 128 * b, lq, ls)
         for b in range(4):
-            mm(b, "eq", "es", 128 * b, tq, tsc)
-        lin(O("wb"), ind(A("w0"), L(36, 56)), 1.0, K(50))
-        own("w1")
-        tr(A("xs"), A("sc2"))
-        other("w1")
-        cp(A("ex", 0, 64), ind(A("xs"), L(28, 32)))
-        if t:
-            own("wb", "xc")
-        tt(A("e3", 0, 20), A("ex", 0, 20), A("ex", 32, 52), add)
-        if t:
-            shifted("wb", "xc")
-        ts(A("obu", 0, 20), A("e3", 0, 20), 512.0, add)
-        cp(O("w0"), ind(A("w1"), A("obu", 0, 20)))
-
-        def first_round(s):
-            if s == 0:
-                lists(((68, 40, 3), (70, 40, 2), (8, 40, 4), (10, 40, 5), (12, 40, 0), (14, 44, 16), (16, 40, 0), (18, 40, 0)))
-            if s == 1:
-                lists((), ((20, 40, 12), (21, 40, 10), (22, 44, 28), (23, 44, 26), (24, 40, 13), (25, 40, 9), (26, 44, 29), (27, 44, 25)))
-            if s in (2, 3):
-                for j, d in enumerate((116.0, 116.0, 52.0, 52.0, 116.0, 116.0)):
-                    lin(A("ci", 44 + 6 * s + j, 45 + 6 * s + j), K(18) if s == 3 else r, d, K(34 + j % 5))
-            if s == 5:
-                lin(A("jj", 64, 128), A("jj", 0, 64), 1.0, K(35))
-                lin(A("jj", 128, 192), A("jj", 64, 128), 1.0, 144.0)
-
-        fillers = [lambda: cp(A("e4"), ind(A("xc"), L(68, 72))),
-                   lambda: tt(A("e5", 0, 20), A("e4", 0, 20), A("e4", 32, 52), add), lambda: cp(A("lnu", 0, 20), A("e5", 0, 20))]
-        if t == 0:
-            fillers = ([lambda: own("wb", "xc"), lambda: shifted("wb", "xc"), lambda: None, lambda: None, lambda: cp(L(56, 72), A("ci", 56, 72))]
-                       + fillers[0:1] + [lambda: (fillers_last[0](), cp(L(8, 28), A("ci", 8, 28)))])
-            fillers_last = [lambda: tt(A("e5", 0, 20), A("e4", 0, 20), A("e4", 32, 52), add)]
+            cp(A("dw", 480 * b + 160, 480 * b + 480), P(b), "s")
+        for b in range(4):
+            act(A("dp", C * b, C * b + C), P(4 + b), AF.Copy, 0.5)
+        for e in range(2):
+            tr(A("xs", C * e, C * e + C), A("sc2", e, 640, 2))
+        for ks, kd in ((0, 0), (1, 1), (2, 2), (3, 3), (5, 6)):
+            for hh in range(2):
+                tt(A("st", kd + 16 * hh, 640, 32), A("xs", ks, 640, 32), A("xs", 16 + ks, 640, 32), add)
+        for e in range(2):
+            tr(A("ob", 1 - e, 640, 2), A("st", C * e, C * e + C))
+        tt(O("w0"), ind(A("ob"), A("bl")), A("wi"), mn)
+        halves = [(lambda b, e: lambda: cp(A(("bt", "bu")[e], b, 640, 4), ind(A("dp", C * b, C * b + C), A("mu", 12 * e, 12 * e + 10)), "s"))(b, e)
+                  for b in range(4) for e in range(2)]
         for s in range(8):
-            cur, nxt, l0 = "w%d" % (s % 2), "w%d" % (1 - s % 2), 32 * (min(s, 6) % 2)
-            lin(A("yy"), O(cur), K(6), K(8))
-            if s < 4:
-                act(A("dp", C * s, C * s + C), P(4 + s), AF.Copy, 0.5)
-            else:
-                cp(A("dw", 480 * (s - 4) + 160, 480 * (s - 4) + 480), P(s - 4), "s")
-            if t == 0:
-                first_round(s)
+            cur, nxt = "w%d" % (s % 2), "w%d" % (1 - s % 2)
+            l0 = 32 * (min(s, 6) % 2)
+            if s:
+                lin(A("yy"), O(cur), keep_, big_)
             own(cur)
-            if s < 7:
+            if s == 0:
+                ts(A("mu"), ind(A(ml), L("mm%d" % h)), 160.0, add)
+            if 0 < s < 7:
                 shifted(cur)
-                other(cur)
-                ts(A("li", l0, l0 + 32), ind(A("xb"), L(0, 2)), 512.0, add)
-                if fillers:
-                    fillers.pop(0)()
+            other(cur)
+            if s < 7:
+                ts(A("li", l0, l0 + 32), ind(A("xb"), L("next" if s else "turn")), base_, add)
             else:
-                if t == 0:
-                    cp(A("lnu", 0, 20), A("e5", 0, 20))
-                other(cur)
-            tt(O(nxt), ind(A(cur), A("li", l0, l0 + 20)), A("yy"), mn)
+                cp(A("o2"), ind(A(cur), A("az", 0, 20)), "s")
+            if s < 4:
+                halves.pop(0)()
+                halves.pop(0)()
+            if s == 4:
+                dma("g", A("bt"), A("bu"), "dacc", None, True)
+            tt(O(nxt), ind(A(cur), A("li", l0, l0 + 20)), A("yy" if s else "yz"), mn)
         own("w0")
-        shifted("w0")
-        cp(A("fg"), ind(A("xb"), L(8, 12)))
-        tt(A("mm", 0, 10), A("fg", 0, 10), A("fg", 42, 52), mn)
-        tt(A("mm", 10, 20), A("fg", 32, 42), A("fg", 10, 20), mn)
-        for k in (0, 16):
-            tt(A("stb", k, 320, 32), A("mm", 0, 10), A("mm", 10, 20), ALU.is_lt)
-            tt(A("stb", 320 + k, 640, 32), A("mm", 0, 10), A("mm", 10, 20), ALU.is_gt)
-        tr(A("bw"), A("stb"))
-        ts(A("rn"), ind(A("bw"), A("lnu", 0, 20)), -511.0, mul, 512.0, add)
-        lin(A("pm", 16, 336), ind(A("bw"), A("lnu", 0, 20)), 512.0, -512.0)
-        scan(A("wb2", 16, 336), A("pm", 15, 335), A("rn"), add, add, -1.0)
+        tr(A("xc", 16, 336), A("o2"))
+        tt(A("mm", 0, 20), A("xb", 21, 336, 16), A("xc", 22, 336, 16), mn)
+        tt(A("mm", 20, 40), A("xb", 22, 336, 16), A("xc", 21, 336, 16), mn)
+        tt(A("mm", 40, 60), A("mm", 20, 40), A("mm", 0, 20), sub)
+        ts(A("stb", 0, 320, 16), A("mm", 40, 60), -1024.0, mul, 1.0, mx)
+        ts(A("stb", 320, 640, 16), A("mm", 40, 60), 1024.0, mul, 0.0, mn)
+        tr(A("bw", 0, 320), A("stb", 0, 320))
+        tr(A("bw", 336, 656), A("stb", 320, 640))
+        scan(O("wb2"), A("bw", 335, 655), A("bw", 0, 320), add, add, -1.0)
         own("wb2")
         shifted("wb2")
-        tt(A(sn, 0, 64), ind(A("xb"), L(12, 16)), A("jj", 128, 192), mn)
-        cp(A("ysu", 0, 20), A(sn, 0, 20))
-        scat(A("se", 16, 496), A("ysu", 0, 20), O("wb"))
-        tr(A("xb", 16, 176), A("se", 16, 176))
-        tr(A("xb", 352, 544), A("se", 0, 192))
-        cp(A("ex"), ind(A("xb"), L(20, 28)))
-        tt(A(sn, 52, 116), A("ex", 0, 64), A("ex", 64, 128), add)
-        w = 62 if t == R - 1 else 46
-        send(T.cores[parts[t]], A(sn, 116, 116 + w), A(sn, 32, 32 + w), "an%d" % t)
-        if t == 0:
-            quant(A("vq"), A("vs"), A("vt"))
-            if len(set(hs)) == 2:
-                pick_u(1 - h)
-        k = 5 if t == R - 1 else 4
-        cp(A("lu", 0, 16 * k), ind(A(sn, 0, 116 + w), L(56 + 6 * h, 56 + 6 * h + k)))
-        for b in (3, 0, 1, 2):
-            cp(A("tm", 160 * b, 160 * b + 160), ind(A("dp", C * b, C * b + C), A("lu", 32, 42)), "v" if b == 3 else "s")
-        for b in range(4):
-            tt(A("bt", b, 640, 4), ind(A("dp", C * b, C * b + C), A("lu", 48, 58)), A("tm", 160 * b, 160 * b + 160), add)
+        tt(A("yp"), ind(A("xb"), L("own", 2)), A("jj", 64, 128), mn)
+        cp(A("yl"), A("yp"))
+        scat(A("se", 16, 816), A("yl", 32, 52), A("pr"))
+        cp(O("wb"), ind(A("se", 16, 496), A("yl", 0, 20)))
+        own("wb", "xb", 8)
+        shifted("wb", "xb", 8)
+        cp(A(sn, 0, 64), ind(A("xb"), L("own", 2)))
+        send(dst, A(sn, 64, 84), A(sn, 32, 52), "an%d" % t)
         quant(A("bq"), A("bs"), A("bt"))
         for b in range(4):
             mm(b, "eq", "es", 128 * b, "bq", "bs", 0, H)
         for b in range(4):
-            cp(A("dw", 480 * b, 480 * b + 160), P(b, 0, H), "vs"[b % 2])
+            cp(A("dw", 480 * b, 480 * b + 160), P(b, 0, H), "s")
+        if t == 0:
+            quant(A("vq"), A("vs"), A("vt"))
+        if t == R - 1:
+            tr(A("xc", 7, 167), A("se", 16, 176))
+            tr(A("xc", 343, 535), A("se", 0, 192))
+            cp(A("oe", 0, 64), ind(A("xc"), L("own", 2)))
+            send(dst, A("oe", 64, 74), A("oe", 0, 10), "ao")
+        ts(A("lu"), ind(A(sn), L("mg%d" % h)), 240.0, add)
         for half in range(2):
             c0, e0 = H * half, 640 * half
             for b in range(4):
@@ -634,12 +606,11 @@ def rank_program(g, core, T, topo):
                 act(rl, P(4 + b, 0, H), AF.Relu, 0.03125)
                 tt(A("xa", e0 + b, e0 + 640, 4), P(b, 0, H), rl, add)
             quant(A(nq, c0, c0 + H), A(ns, c0, c0 + H), A("xa", e0, e0 + 640))
-            if t + 1 < R:
-                send_t(t + 1, half)
-            else:
+            if t + 1 == R:
                 dma("y", T.oc[:, 4 * c0:4 * c0 + 640], u8(A(nq, c0, c0 + H)), "dout")
                 if half == 0:
-                    cp(A("er"), ind(A("j1"), A("lu", 64, 74)), "s")
+                    ts(A("ou"), ind(A("oe"), L("ol")), 160.0, add)
+                    cp(A("er"), ind(A("j1"), A("ou", 0, 10)), "s")
                     dma("y", T.ol[:], A("er", rows=slice(0, 128, 16)), "dout")
 
     for half in range(2):

@@ -12,12 +12,12 @@ for _n, _w, _t in [
     ("cf", 3200, BF), ("pf", 1616, F16), ("x1", 320, F16), ("x2", 320, F16), ("cu", 352, F32),
     ("ck", 60, F32), ("ce", 40, F32), ("d1", 40, F32), ("pb", 40, F32), ("rb", 20, F32), ("ii", 20, I32),
     ("zl", 32, U16), ("xl", 20, U16), ("bl", 20, U16), ("az", 32, U16), ("mu", 32, U16), ("li", 64, U16), ("yl", 64, U16), ("lu", 32, U16), ("ou", 32, U16),
-    ("sa", 320, BF), ("sb", 320, BF), ("j1", 320, F32), ("sc1", 320, BF), ("xd", 384, BF), ("oa", 704, BF), ("wa", 320, BF), ("wi", 320, BF), ("xw", 544, BF),
+    ("sa", 320, BF), ("sb", 320, BF), ("j1", 320, F32), ("sc1", 320, BF), ("xd", 384, BF), ("oa", 704, BF), ("wa", 320, BF), ("wi", 320, BF),
     ("s2", 320, BF), ("pr", 320, BF), ("sc2", 640, BF), ("xs", 640, BF), ("st", 640, BF), ("ob", 640, BF), ("w0", 1056, BF), ("w1", 1056, BF),
-    ("yy", 320, BF), ("yz", 320, BF), ("o2", 320, BF), ("xb", 704, BF), ("xc", 704, BF), ("mm", 60, F32), ("stb", 640, BF), ("bw", 656, BF),
+    ("yy", 320, BF), ("yz", 320, BF), ("o2", 320, BF), ("xb", 704, BF), ("xc", 352, BF), ("mm", 60, F32), ("stb", 640, BF), ("bw", 656, BF),
     ("wb", 352, BF), ("wb2", 352, BF), ("jj", 128, F32), ("yp", 64, F32), ("se", 816, BF), ("oe", 96, BF),
-    ("zz", 704, BF), ("ti", 1920, BF), ("pi", 8, I32), ("ui", 32, I32), ("ul", 32, U16), ("cc", 64, F32), ("ci", 20, F32), ("cl", 20, U16),
-    ("rp", 8, F32), ("tl", 40, F32), ("tlu", 20, U16), ("s3", 320, F32),
+    ("ti", 1920, BF), ("pi", 8, I32), ("ui", 32, I32), ("ul", 32, U16), ("cc", 64, F32), ("ci", 20, F32), ("cl", 20, U16),
+    ("tl", 40, F32), ("tlu", 20, U16), ("s3", 320, F32),
 ]:
     SCRATCH[_n] = ("sbuf", [128, _w], _t)
 for _t in range(R + 1):
@@ -30,7 +30,7 @@ for _t in range(R):
     SCRATCH["rw%d" % _t] = ("sbuf", [128, 64], F32)
     SCRATCH["ml%d" % _t] = ("sbuf", [128, 128], BF)
     SCRATCH["sn%d" % _t] = ("sbuf", [128, 96], BF)
-SEMAPHORES = (["cv", "cs", "cp", "cg", "dx", "dx2", "du", "dv", "dwq", "dwp", "dsa", "dyz", "det", "dz", "dout", "sent", "dacc", "ao"]
+SEMAPHORES = (["cv", "cs", "cp", "cg", "dx", "dx2", "du", "dv", "dwq", "dwp", "dsa", "dyz", "det", "dout", "sent", "dacc", "ao", "dm"]
               + ["%s%d" % (k, t) for k in ("aq", "as", "an", "at", "ar", "ac", "am", "d1", "d2", "d3", "d4") for t in range(R)])
 
 NS = (5, 5, 4, 5, 6)
@@ -172,6 +172,10 @@ def rank_program(g, core, T, topo):
         else:
             op("g", lambda: g.iota(out[0], pat, base, cm), [out], [])
 
+    def zero(*regions):
+        for a in regions:
+            iota(a, [[0, bin(a[1][0][1]).count("1")]])
+
     def sel(out, in_, pat, o, base, cm):
         op("g", lambda: g.affine_select(out[0], in_[0], pat, o, 0.0, base, cm), [out], [in_])
 
@@ -194,17 +198,13 @@ def rank_program(g, core, T, topo):
     hs = [1 if rank > p else 0 for p in parts]
     H = C // 2
 
-    LISTS = [("next", 32, ((16, 369), (384, 33))), ("turn", 32, ((18, 19), (34, 35))), ("own", 32, ((16, 368), (384, 32))), ("far", 32, ((32, 352), (400, 16))),
-             ("zm", 1, ((0, 40), (24, 12))), ("mm0", 2, ((1, 97), (65, 33))), ("mm1", 2, ((32, 64), (96, 0))),
+    LISTS = [("next", 32, ((16, 369), (384, 33))), ("turn", 32, ((18, 19), (34, 35))), ("zm", 1, ((0, 40), (24, 12))),
+             ("own", 32, ((16, 368), (384, 32))), ("far", 32, ((32, 352), (400, 16))), ("mm0", 2, ((1, 97), (65, 33))), ("mm1", 2, ((32, 64), (96, 0))),
              ("mg0", 2, ((0, 64), (1, 65))), ("mg1", 2, ((64, 0), (65, 1))), ("ol", 2, (((32, 64), (33, 65)), ((64, 32), (65, 33)))[hs[R - 1]])]
 
     def L(name, k=1):
         i = [e[0] for e in LISTS].index(name)
         return A("cl", 2 * i, 2 * i + 2 * k)
-
-    def tie_mask(a):
-        rows = slice(32 * a, 32 * a + 32)
-        sel(A("eqm", rows=rows), A("one", 0, 320, rows=rows), [[0, 10], [-1, 32]], ALU.not_equal, 0, 1)
 
     def pick_u(hh):
         o_, l_ = A("up", 256 * hh, 256 * hh + 256), A("ul", 16 * hh, 16 * hh + 16)
@@ -212,15 +212,22 @@ def rank_program(g, core, T, topo):
         op("v", lambda: g.vector.tensor_copy(o_[0].bitcast(dt.uint32), i_[0]), [o_], [i_])
         cp(A("ups", 256 * hh, 256 * hh + 256), ind(A("us"), l_), "s")
 
+    def send_t(t, half):
+        dst = T.cores[parts[t]]
+        send(dst, u8(A("lq%d" % t, H * half, H * half + H)), u8(A("tq%d" % t, H * half, H * half + H)), "aq%d" % t, None, 2)
+        if half:
+            send(dst, A("ls%d" % t), A("ts%d" % t), "as%d" % t)
+
     dma("s", A("ut"), T.u[:], "du")
     dma("y", A("x0", 0, 640), T.x[:, 0:640], "dx")
     dma("y", A("x0", 640, 1280), T.x[:, 640:1280], "dx2")
     iota(A("pi", 0, 1), [[0, 1]], 0, 1, False)
     iota(A("ui"), [[8, 4], [32, 4], [0, 2]], 0, 0, False)
+    iota(A("j1"), [[1, 320]])
     fill(A("one"), 1.0)
-    iota(A("rp", 0, 2), [[8, 2]])
-    tie_mask(0)
-    tie_mask(1)
+    sel(A("eqm", rows=slice(0, 32)), A("one", 0, 320, rows=slice(0, 32)), [[0, 10], [-1, 32]], ALU.not_equal, 0, 1)
+    for a in range(1, 4):
+        dma("y", A("eqm", rows=slice(32 * a, 32 * a + 32)), A("eqm", rows=slice(0, 32)), "dm", 48)
     p0 = A("pi", 0, 1)
     i4, run, hq, par, p5, both = K(0), K(1), K(2), K(3), K(4), K(5)
     ts(A("pi", 1, 2), p0, 15, band)
@@ -229,65 +236,58 @@ def rank_program(g, core, T, topo):
     ts(A("pi", 4, 5), p0, 1, band)
     ts(A("pi", 5, 6), p0, 31, band)
     cp(A("ul"), A("ui"))
-    fill(A("zz"), 0.0)
     cp(K(0, 5), A("pi", 1, 6))
-    for t in range(R):
-        fill(A("rw%d" % t, 24, 64), 0.0)
-        fill(A("rw%d" % t, 12 * hs[t] + 8, 12 * hs[t] + 12), 0.0)
-        fill(A("sn%d" % t, 64, 96), 0.0)
-        fill(A("ml%d" % t), 0.0)
+    fill(A("ck", 0, 40), 160.0)
+    fill(A("ck", 40, 60), 480.0)
     tt(both, par, run, mul)
     ts(K(6), i4, 5.0, ALU.is_equal)
     ts(K(7), i4, 6.0, ALU.is_equal)
+    for t in range(R):
+        fill(A("ml%d" % t), 0.0)
+        fill(A("rw%d" % t, 24, 64), 0.0)
+        fill(A("rw%d" % t, 12 * hs[t] + 8, 12 * hs[t] + 12), 0.0)
+    for c0, c1 in ((0, 16), (176, 208), (368, 384)):
+        fill(A("xd", c0, c1), 0.0)
+    fill(A("pf", 4, 810, 805), 0.0)
+    fill(A("cu", 0, 32), 0.0)
     fill(A("st"), BIG)
     fill(A("yz"), BIG)
-    fill(A("xd"), 0.0)
-    fill(A("w0"), 0.0)
-    fill(A("w1"), 0.0)
+    iota(A("tl", 0, 20), [[32, 10], [320, 2]])
+    for k in range(5):
+        iota(A("ti", 1280 + 128 * k, 1408 + 128 * k), [[2 ** k, 128]], 128 * 2 ** k)
+    iota(A("s3"), [[32, 10], [0, 32]], -160)
+    sel(A("e0"), A("one"), [[-1, 528]], ALU.is_equal, 3, 4)
     keep_, big_, base_ = K(8), K(9), K(10)
     lin(keep_, K(6), 1.0, K(7))
     lin(base_, run, -64.0, 560.0)
     lin(K(11), run, 320.0, 0.0)
     lin(K(12), run, -384.0, 384.0)
-    for level in range(5):
-        for i, (name, step, b) in enumerate(LISTS):
-            k0, k1 = K(20 + i), K(30 + i)
-            if level == 0:
-                lin(k0, hq, float(step), float(b[0][0]))
-            elif level == 4:
-                lin(A("ci", 2 * i, 2 * i + 2), A("rp", 0, 2), float(step), k1)
-            else:
-                src, f = ((par, b[1][0] - b[0][0]), (run, b[0][1] - b[0][0]), (both, b[1][1] - b[1][0] - b[0][1] + b[0][0]))[level - 1]
-                lin(*((k1, src, float(f), k0) if level % 2 else (k0, src, float(f), k1)))
+
+    def short_lists(i0, i1):
+        for level in range(5):
+            for i, (name, step, b) in list(enumerate(LISTS))[i0:i1]:
+                k0, k1 = K(20 + i), K(30 + i)
+                if level == 0:
+                    lin(k0, hq, float(step), float(b[0][0]))
+                elif level == 4:
+                    lin(A("ci", 2 * i, 2 * i + 2), A("j1", 0, 2), 8.0 * step, k1)
+                else:
+                    src, f = ((par, b[1][0] - b[0][0]), (run, b[0][1] - b[0][0]), (both, b[1][1] - b[1][0] - b[0][1] + b[0][0]))[level - 1]
+                    lin(*((k1, src, float(f), k0) if level % 2 else (k0, src, float(f), k1)))
+
+    for k in range(6):
+        n = NS[(0, 1, 2, 3, 2, 3)[k]]
+        lin(A("ck", 10 * k, 10 * k + n), A("j1", 0, n), 32.0, 32.0 + 320 * (k // 4))
+    for c0, n, step, base in ((0, 320, 1, -160), (320, 160, 2, -496), (480, 160, 2, 176), (640, 192, 2, -496), (832, 128, 2, 240), (960, 320, 1, -96)):
+        lin(A("ti", c0, c0 + n), A("j1", 0, n), float(step), float(base))
     lin(big_, keep_, -BIG, BIG)
+    short_lists(0, 3)
+    ts(A("tlu"), A("tl", 0, 20), p5, add)
     quant(A("uq"), A("us"), A("ut"))
     pick_u(1 - hs[0])
+    pick_u(hs[0])
     for half in range(2):
         quant(A("tq0", H * half, H * half + H), A("ts0", H * half, H * half + H), A("x0", 640 * half, 640 * half + 640))
-    pick_u(hs[0])
-    dma("y", u8(A("wq")), T.wc[:], "dwq")
-    dma("y", A("wp"), T.ws[:], "dwp")
-    dma("y", A("vt"), T.v[:], "dv")
-    zero = [A(w) for w in ("xw", "xb", "xc", "stb", "oe")] + [A("bw", 320, 336), A("se", 0, 176), A("se", 496, 816)]
-    zero += [A(w, c, c + 16) for w in ("wb", "wb2") for c in (0, 336)]
-    for a in zero:
-        dma("y", a, A("zz", 0, bin(a[1][0][1]).count("1")), "dz", 16 * len(zero))
-    tie_mask(2)
-    tie_mask(3)
-    for k in range(6):
-        n, lift = NS[(0, 1, 2, 3, 2, 3)[k]], 320 * (k // 4)
-        iota(A("ck", 10 * k, 10 * k + n), [[32, n]], 32 + lift)
-        iota(A("ck", 10 * k + n, 10 * k + 10), [[0, 10 - n]], 160 + lift)
-
-    def early_constants():
-        iota(A("tl", 0, 20), [[32, 10], [320, 2]])
-        for c0, n, step, base in ((0, 320, 1, -160), (320, 160, 2, -496), (480, 160, 2, 176), (640, 192, 2, -496), (832, 128, 2, 240), (960, 320, 1, -96)):
-            iota(A("ti", c0, c0 + n), [[step, n]], base)
-        for k in range(5):
-            iota(A("ti", 1280 + 128 * k, 1408 + 128 * k), [[2 ** k, 128]], 128 * 2 ** k)
-        iota(A("s3"), [[32, 10], [0, 32]], -160)
-        iota(A("pf", 4, 810, 805), [[0, 2]])
-        iota(A("cu", 0, 32), [[0, 32]])
 
     def table_constants():
         cp(A("sa"), ind(A("ti", 0, 640), A("tlu")), "s")
@@ -300,14 +300,18 @@ def rank_program(g, core, T, topo):
             dma("y", A("yz", rows=slice(5 + 16 * hh, 128, 32)), A("ti", 1280 + 320 * hh, 1600 + 320 * hh, rows=low), "dyz", 32)
         dma("y", A("sa", rows=slice(7, 128, 16)), A("ti", 0, 320, rows=slice(0, 8)), "dsa", 128)
         dma("y", A("sa", rows=slice(3, 128, 16)), A("sb", rows=slice(3, 128, 16)), "dsa", 128)
-
-    def late_constants():
-        sel(A("e0"), A("one"), [[-1, 528]], ALU.is_equal, 3, 4)
         for b in range(4):
             dma("y", A("et", 512 * b, 512 * b + 512), A("e0", 3 - b, 515 - b), "det", 64)
+
+    def late_constants():
+        zero(A("xb", 0, 16), A("xb", 336, 352))
+        for w in ("w0", "w1"):
+            zero(A(w, 1, 384, 2), A(w, 384, 400), A(w, 720, 736), A(w, 737, 1056, 2))
         iota(A("jj", 0, 64), [[320, 2], [16, 32]], 160)
         iota(A("se", 176, 496), [[1, 320]], -80)
-        iota(A("j1"), [[1, 320]])
+        zero(A("stb"), A("bw", 320, 336), A("se", 0, 176), A("se", 496, 816), A("oe", 80, 96))
+        zero(*[A(w, c, c + 16) for w in ("wb", "wb2") for c in (0, 336)])
+        zero(*[A("sn%d" % t, 88, 96) for t in range(R)])
 
     def O(w, pad=0):
         c0 = 400 if w in ("w0", "w1") else 16
@@ -373,7 +377,7 @@ def rank_program(g, core, T, topo):
             tr(A("xt", C * k, C * k + C), P(k))
 
         def ties(k):
-            c0, k0 = C * k, 10 * k
+            c0 = C * k
             tt(A("eqf", c0, c0 + C), P(k), A("xt", c0, c0 + C), ALU.is_equal)
             flush("v")
             pend["v"].append(lambda: scan(A("eqs", c0, c0 + C), A("eqm"), A("eqf", c0, c0 + C), mul))
@@ -405,19 +409,20 @@ def rank_program(g, core, T, topo):
                 f()
             tie_sums(k)
 
-        for k in range(4):
-            for e in range(2):
-                mm(4 * e + k, "up", "ups", 128 * (2 * (h if k % 2 else 1 - h) + k // 2), tq, tsc)
-        thresholds(0)
-        thresholds(2)
-        thresholds(1)
-        cp(A(th, 0, 10), A("xt", 2 * C, 3 * C, 32))
-        send(dst, A(th, 16, 26), A(th, 0, 10), "at%d" % t)
         if t == 0:
-            early_constants()
-        iota(A("sc2"), [[0, 640]])
-        run_units(units("s", 0) + units("s", 1))
-        self_count(0)
+            table_constants()
+        for bank in (0, 4, 2, 1, 5, 6, 3, 7):
+            k = bank % 4
+            mm(bank, "up", "ups", 128 * (2 * (h if k % 2 else 1 - h) + k // 2), tq, tsc)
+        thresholds(0)
+        run_units(units("s", 0))
+
+        def first_write():
+            cp(A(th, 0, 10), A("xt", 2 * C, 3 * C, 32))
+            send(dst, A(th, 16, 26), A(th, 0, 10), "at%d" % t)
+
+        self_count(0, [lambda: thresholds(2), lambda: thresholds(1), first_write])
+        run_units(units("s", 1))
         flush("s")
         mine = units("v", 1)
         ties(1)
@@ -426,32 +431,18 @@ def rank_program(g, core, T, topo):
         unit(*mine[1])
         places(0, rw, 52)
         send(dst, A(rw, 12 * h, 12 * h + 12), A(rw, 52, 64), "ar%d" % t, A(rw, 12 - 12 * h, 24 - 12 * h))
+        iota(A("sc2"), [[0, 640]])
         run_units(mine[2:])
         tie_sums(1)
         thresholds(3)
         if t == 0:
-            ts(A("cl"), A("ci"), 703.0, mn)
-            ts(A("tlu"), A("tl", 0, 20), p5, add)
-            table_constants()
+            ts(A("cl", 0, 2), A("ci", 0, 2), 703.0, mn)
+            ts(A("cl", 2, 6), A("ci", 2, 6), 351.0, mn)
         run_units(units("s", 2))
         flush("s")
         self_count(2, [lambda: differences(1), lambda: places(1, rw, 12 * h)])
         dma("y", A(rw, 24, 34, rows=slice(0, 112)), A(rw, 0, 10, rows=slice(16, 128)), "d1%d" % t)
         dma("y", A(rw, 40, 50, rows=slice(16, 128)), A(rw, 12, 22, rows=slice(0, 112)), "d2%d" % t)
-        run_units(units("s", 4))
-        flush("s")
-        cross = units("v", 4)
-        unit(*cross[0])
-        differences(2)
-        unit(*cross[1])
-        places(2, th, 32)
-        send(dst, A(th, 48, 58), A(th, 32, 42), "ac%d" % t)
-        for half in range(2):
-            send(dst, u8(A(lq, H * half, H * half + H)), u8(A(tq, H * half, H * half + H)), "aq%d" % t, None, 2)
-        send(dst, A(ls), A(tsc), "as%d" % t)
-        if t == 0:
-            late_constants()
-        run_units(cross[2:])
         rest = units("v", 3)
         srest = units("s", 3)
 
@@ -459,18 +450,28 @@ def rank_program(g, core, T, topo):
             if rest:
                 unit(*rest.pop(0))
 
-        run_units(srest[:3])
+        run_units(srest[:2])
+        ties(3)
+        differences(2)
+        gap()
+        places(2, th, 32)
+        send(dst, A(th, 48, 58), A(th, 32, 42), "ac%d" % t)
+        if t == 0:
+            zero(A("xc", 0, 18), A("xc", 336, 352))
+        gap()
+        gap()
+        run_units(units("s", 4))
+        flush("s")
+        run_units(units("v", 4))
+        run_units(srest[2:3])
         cp(A("zl"), ind(A(rw), L("zm")))
         for k in range(2):
             ts(A("xl", k, 20, 2), A(rw, 12 * k, 12 * k + 10), K(11 + k), add)
-            ts(A("ii", 10 * k, 10 * k + 10), A(rw, 12 * k, 12 * k + 10), 0.5, mul, 0.25, sub)
         flush("v")
         scat(A("sc1"), A("zl", 0, 20), A("sa"))
-        for k in range(2):
-            ts(A("s2", 24 - 16 * k, 320, 32), A("ii", 10 * k, 10 * k + 10), 240.0, sub)
         for e in range(2):
             tr(A("xd", 16 + 192 * e, 176 + 192 * e), A("sc1", e, 320, 2))
-        ties(3)
+        tie_sums(3)
         for e in range(2):
             cp(A("xd", 21 + 192 * e, 176 + 192 * e, 16), A("xd", 214 - 192 * e, 368 - 192 * e, 16))
         cp(A(ml, 0, 22), A("xd", 23, 368, 16))
@@ -478,6 +479,10 @@ def rank_program(g, core, T, topo):
         up, down = (slice(0, 112), slice(16, 128)), (slice(16, 128), slice(0, 112))
         for c0, s0, way, sem in ((64, 0, (up, down)[h], "d3%d" % t), (96, 32, (down, up)[h], "d4%d" % t)):
             dma("y", A(ml, c0, c0 + 22, rows=way[0]), A(ml, s0, s0 + 22, rows=way[1]), sem)
+            if t == 0 and s0 == 0:
+                send_t(0, 0)
+                send_t(0, 1)
+                late_constants()
         flush("v")
         for e in range(2):
             tr(A("oa", 1 - e, 320, 2), A("xd", 16 + 192 * e, 176 + 192 * e))
@@ -487,7 +492,6 @@ def rank_program(g, core, T, topo):
         run_units(srest[3:])
         flush("s")
         lin(A("wi"), A("wa"), keep_, big_)
-        tie_sums(3)
         for k in range(2):
             scan(A("pf", 805 * k + 5, 805 * k + 805), A("cf", 1600 * k, 1600 * k + 1600, 2), A("cf", 1600 * k + 1, 1600 * k + 1600, 2), add)
         gap()
@@ -505,19 +509,16 @@ def rank_program(g, core, T, topo):
         tt(A("ce", 30, 40), A("ce", 30, 40), A("pb", 0, 10), (add, sub)[h])
         while rest:
             gap()
-        tr(A("pr"), A("s2"))
-        flush("v")
         differences(3)
-        tr(A("xw", 18, 338), A("wa"))
+        flush("v")
         n3 = NS[3]
         tt(A("rb", h + 2 * n3, 20, 2), ends(3, n3, 10), A("ce", 30 + n3, 40), add)
         tt(A("rb", h, 2 * n3, 2), A("d1", 30, 30 + n3), A("ce", 30, 30 + n3), add)
-        ts(A("az"), ind(A("xw"), L("turn")), base_, add)
         cp(A("bl"), A("rb"))
         scat(A("sc2"), A("bl"), A("wa"))
         if t == 0:
             quant(A("eq"), A("es"), A("et"))
-            lin(A("jj", 64, 128), A("jj", 0, 64), 1.0, i4)
+            short_lists(3, len(LISTS))
         for b in range(4):
             mm(b, "eq", "es", 128 * b, tq, tsc)
         for b in range(4):
@@ -536,25 +537,39 @@ def rank_program(g, core, T, topo):
         tt(O("w0"), ind(A("ob"), A("bl")), A("wi"), mn)
         halves = [(lambda b, e: lambda: cp(A(("bt", "bu")[e], b, 640, 4), ind(A("dp", C * b, C * b + C), A("mu", 12 * e, 12 * e + 10)), "s"))(b, e)
                   for b in range(4) for e in range(2)]
+        fillers = [(lambda k: lambda: ts(A("ii", 10 * k, 10 * k + 10), A(rw, 12 * k, 12 * k + 10), 0.5, mul, 0.25, sub))(k) for k in range(2)]
+        fillers += [lambda: ts(A("cl", 6, 20), A("ci", 6, 20), 703.0, mn) if t == 0 else None, lambda: ts(A("mu"), ind(A(ml), L("mm%d" % h)), 160.0, add)]
+        fillers += [(lambda k: lambda: ts(A("s2", 24 - 16 * k, 320, 32), A("ii", 10 * k, 10 * k + 10), 240.0, sub))(k) for k in range(2)]
+        fillers += [lambda: tr(A("xc", 18, 338), A("wa")), lambda: tr(A("pr"), A("s2")), lambda: ts(A("az"), ind(A("xc"), L("turn")), base_, add)]
+
+        def filler():
+            if fillers:
+                fillers.pop(0)()
+
         for s in range(8):
             cur, nxt = "w%d" % (s % 2), "w%d" % (1 - s % 2)
             l0 = 32 * (min(s, 6) % 2)
             if s:
                 lin(A("yy"), O(cur), keep_, big_)
+            filler()
             own(cur)
-            if s == 0:
-                ts(A("mu"), ind(A(ml), L("mm%d" % h)), 160.0, add)
+            if s == 1 and t == 0:
+                dma("y", u8(A("wq")), T.wc[:], "dwq")
+                dma("y", A("wp"), T.ws[:], "dwp")
+                dma("y", A("vt"), T.v[:], "dv")
+                lin(A("jj", 64, 128), A("jj", 0, 64), 1.0, i4)
             if 0 < s < 7:
                 shifted(cur)
             other(cur)
             if s < 7:
-                ts(A("li", l0, l0 + 32), ind(A("xb"), L("next" if s else "turn")), base_, add)
+                ts(A("li", l0, l0 + 32), ind(A("xb", 0, 704 if s else 352), L("next" if s else "turn")), base_, add)
             else:
                 cp(A("o2"), ind(A(cur), A("az", 0, 20)), "s")
-            if s < 4:
+            filler()
+            if 2 <= s < 6:
                 halves.pop(0)()
                 halves.pop(0)()
-            if s == 4:
+            if s == 6:
                 dma("g", A("bt"), A("bu"), "dacc", None, True)
             tt(O(nxt), ind(A(cur), A("li", l0, l0 + 20)), A("yy" if s else "yz"), mn)
         own("w0")
@@ -576,7 +591,7 @@ def rank_program(g, core, T, topo):
         own("wb", "xb", 8)
         shifted("wb", "xb", 8)
         cp(A(sn, 0, 64), ind(A("xb"), L("own", 2)))
-        send(dst, A(sn, 64, 84), A(sn, 32, 52), "an%d" % t)
+        send(dst, A(sn, 64, 88), A(sn, 32, 56), "an%d" % t)
         quant(A("bq"), A("bs"), A("bt"))
         for b in range(4):
             mm(b, "eq", "es", 128 * b, "bq", "bs", 0, H)
@@ -585,16 +600,18 @@ def rank_program(g, core, T, topo):
         if t == 0:
             quant(A("vq"), A("vs"), A("vt"))
         if t == R - 1:
-            tr(A("xc", 7, 167), A("se", 16, 176))
-            tr(A("xc", 343, 535), A("se", 0, 192))
-            cp(A("oe", 0, 64), ind(A("xc"), L("own", 2)))
-            send(dst, A("oe", 64, 74), A("oe", 0, 10), "ao")
+            tr(A("xb", 7, 167), A("se", 16, 176))
+            tr(A("xb", 343, 535), A("se", 0, 192))
+            cp(A("oe", 0, 64), ind(A("xb"), L("own", 2)))
+            send(dst, A("oe", 64, 80), A("oe", 0, 16), "ao")
         ts(A("lu"), ind(A(sn), L("mg%d" % h)), 240.0, add)
         for half in range(2):
             c0, e0 = H * half, 640 * half
             for b in range(4):
                 cp(A("yt", e0 + b, e0 + 640, 4), ind(A("dw", 480 * b, 480 * b + 480), A("lu", 10 * half, 10 * half + 10)), "vs"[b % 2])
             quant(A("zq", c0, c0 + H), A("zs", c0, c0 + H), A("yt", e0, e0 + 640))
+        if t == R - 1:
+            ts(A("ou"), ind(A("oe"), L("ol")), 160.0, add)
         for half in range(2):
             c0, e0, nq, ns = H * half, 640 * half, "tq%d" % (t + 1), "ts%d" % (t + 1)
             for b in range(4):
@@ -606,10 +623,11 @@ def rank_program(g, core, T, topo):
                 act(rl, P(4 + b, 0, H), AF.Relu, 0.03125)
                 tt(A("xa", e0 + b, e0 + 640, 4), P(b, 0, H), rl, add)
             quant(A(nq, c0, c0 + H), A(ns, c0, c0 + H), A("xa", e0, e0 + 640))
-            if t + 1 == R:
+            if t + 1 < R:
+                send_t(t + 1, half)
+            else:
                 dma("y", T.oc[:, 4 * c0:4 * c0 + 640], u8(A(nq, c0, c0 + H)), "dout")
                 if half == 0:
-                    ts(A("ou"), ind(A("oe"), L("ol")), 160.0, add)
                     cp(A("er"), ind(A("j1"), A("ou", 0, 10)), "s")
                     dma("y", T.ol[:], A("er", rows=slice(0, 128, 16)), "dout")
 

@@ -17,7 +17,7 @@ for _n, _w, _t in [
     ("yy", 320, BF), ("yz", 320, BF), ("o2", 320, BF), ("xb", 704, BF), ("xc", 352, BF), ("mm", 60, F32), ("stb", 640, BF), ("bw", 656, BF),
     ("wb", 352, BF), ("wb2", 352, BF), ("jj", 128, F32), ("yp", 64, F32), ("se", 816, BF), ("oe", 96, BF),
     ("ti", 1920, BF), ("pi", 8, I32), ("ui", 32, I32), ("ul", 32, U16), ("cc", 64, F32), ("ci", 20, F32), ("cl", 20, U16),
-    ("tl", 40, F32), ("tlu", 20, U16), ("s3", 320, F32),
+    ("tl", 40, F32), ("tlu", 20, U16),
 ]:
     SCRATCH[_n] = ("sbuf", [128, _w], _t)
 for _t in range(R + 1):
@@ -30,10 +30,10 @@ for _t in range(R):
     SCRATCH["rw%d" % _t] = ("sbuf", [128, 64], F32)
     SCRATCH["ml%d" % _t] = ("sbuf", [128, 128], BF)
     SCRATCH["sn%d" % _t] = ("sbuf", [128, 96], BF)
-SEMAPHORES = (["cv", "cs", "cp", "cg", "dx", "dx2", "du", "dv", "dwq", "dwp", "dsa", "dyz", "det", "dout", "sent", "dacc", "ao", "dm"]
+SEMAPHORES = (["cv", "cs", "cp", "cg", "dx", "dx2", "du", "dv", "dwq", "dwp", "dsa", "dyz", "det", "dout", "sent", "dacc", "ao", "dm", "ds2"]
               + ["%s%d" % (k, t) for k in ("aq", "as", "an", "at", "ar", "ac", "am", "d1", "d2", "d3", "d4") for t in range(R)])
 
-NS = (5, 5, 4, 5, 6)
+NS = (5, 5, 4, 5, 7)
 BIG = 1.0e6
 
 
@@ -145,7 +145,7 @@ def rank_program(g, core, T, topo):
             op("v", lambda: g.vector.tensor_scalar(out[0], a[0], x(s1), x(s2), o0, o1), [out], [a, s1, s2])
 
     def scan(out, d0, d1, o0, o1=ALU.add, first=0.0):
-        op("v", lambda: g.vector.tensor_tensor_scan(out[0], d0[0], d1[0], first, o0, o1), [out], [d0, d1])
+        op("v", lambda: g.vector.tensor_tensor_scan(out[0], d0[0], d1[0], x(first), o0, o1), [out], [d0, d1, first])
 
     def tr(out, in_):
         op("v", lambda: g.vector.transpose(out[0], in_[0]), [out], [in_])
@@ -221,10 +221,26 @@ def rank_program(g, core, T, topo):
     dma("s", A("ut"), T.u[:], "du")
     dma("y", A("x0", 0, 640), T.x[:, 0:640], "dx")
     dma("y", A("x0", 640, 1280), T.x[:, 640:1280], "dx2")
-    iota(A("pi", 0, 1), [[0, 1]], 0, 1, False)
-    iota(A("ui"), [[8, 4], [32, 4], [0, 2]], 0, 0, False)
     iota(A("j1"), [[1, 320]])
+    iota(A("pi", 0, 1), [[0, 1]], 0, 1, False)
+    iota(A("tl", 0, 20), [[32, 10], [320, 2]])
+    iota(A("ui"), [[8, 4], [32, 4], [0, 2]], 0, 0, False)
     fill(A("one"), 1.0)
+    fill(A("ck", 0, 40), 160.0)
+    fill(A("ck", 40, 60), 480.0)
+    for t in range(R):
+        fill(A("ml%d" % t), 0.0)
+        fill(A("rw%d" % t, 24, 64), 0.0)
+        fill(A("rw%d" % t, 12 * hs[t] + 8, 12 * hs[t] + 12), 0.0)
+    for c0, c1 in ((0, 16), (176, 208), (368, 384)):
+        fill(A("xd", c0, c1), 0.0)
+    fill(A("pf", 4, 810, 805), 0.0)
+    fill(A("ck", 3, 5), 80.0)
+    fill(A("cu", 0, 32), 0.0)
+    for c0, n, step, base in ((0, 320, 1, -224), (320, 128, 2, -496), (448, 192, 2, 112), (640, 160, 2, -496), (800, 160, 2, 176), (960, 320, 1, -160)):
+        lin(A("ti", c0, c0 + n), A("j1", 0, n), float(step), float(base))
+    for k in range(5):
+        lin(A("ti", 1280 + 128 * k, 1408 + 128 * k), A("j1", 0, 128), 2.0 ** k, 128.0 * 2 ** k)
     sel(A("eqm", rows=slice(0, 32)), A("one", 0, 320, rows=slice(0, 32)), [[0, 10], [-1, 32]], ALU.not_equal, 0, 1)
     for a in range(1, 4):
         dma("y", A("eqm", rows=slice(32 * a, 32 * a + 32)), A("eqm", rows=slice(0, 32)), "dm", 48)
@@ -235,28 +251,16 @@ def rank_program(g, core, T, topo):
     ts(A("pi", 3, 4), p0, 1, shr, 7, band)
     ts(A("pi", 4, 5), p0, 1, band)
     ts(A("pi", 5, 6), p0, 31, band)
-    cp(A("ul"), A("ui"))
+    fill(A("yz"), BIG)
     cp(K(0, 5), A("pi", 1, 6))
-    fill(A("ck", 0, 40), 160.0)
-    fill(A("ck", 40, 60), 480.0)
+    fill(A("st"), BIG)
+    ts(A("tlu"), A("tl", 0, 20), p5, add)
     tt(both, par, run, mul)
     ts(K(6), i4, 5.0, ALU.is_equal)
     ts(K(7), i4, 6.0, ALU.is_equal)
-    for t in range(R):
-        fill(A("ml%d" % t), 0.0)
-        fill(A("rw%d" % t, 24, 64), 0.0)
-        fill(A("rw%d" % t, 12 * hs[t] + 8, 12 * hs[t] + 12), 0.0)
-    for c0, c1 in ((0, 16), (176, 208), (368, 384)):
-        fill(A("xd", c0, c1), 0.0)
-    fill(A("pf", 4, 810, 805), 0.0)
-    fill(A("cu", 0, 32), 0.0)
-    fill(A("st"), BIG)
-    fill(A("yz"), BIG)
-    iota(A("tl", 0, 20), [[32, 10], [320, 2]])
-    for k in range(5):
-        iota(A("ti", 1280 + 128 * k, 1408 + 128 * k), [[2 ** k, 128]], 128 * 2 ** k)
-    iota(A("s3"), [[32, 10], [0, 32]], -160)
-    sel(A("e0"), A("one"), [[-1, 528]], ALU.is_equal, 3, 4)
+    cp(A("ul"), A("ui"))
+    cp(A("sa"), ind(A("ti", 0, 640), A("tlu")))
+    iota(A("s2", rows=slice(0, 32)), [[32, 10], [0, 32]], -160, 1)
     keep_, big_, base_ = K(8), K(9), K(10)
     lin(keep_, K(6), 1.0, K(7))
     lin(base_, run, -64.0, 560.0)
@@ -276,57 +280,93 @@ def rank_program(g, core, T, topo):
                     lin(*((k1, src, float(f), k0) if level % 2 else (k0, src, float(f), k1)))
 
     for k in range(6):
-        n = NS[(0, 1, 2, 3, 2, 3)[k]]
+        n = NS[(0, 1, 2, 3, 2, 3)[k]] if k else 3
         lin(A("ck", 10 * k, 10 * k + n), A("j1", 0, n), 32.0, 32.0 + 320 * (k // 4))
-    for c0, n, step, base in ((0, 320, 1, -160), (320, 160, 2, -496), (480, 160, 2, 176), (640, 192, 2, -496), (832, 128, 2, 240), (960, 320, 1, -96)):
-        lin(A("ti", c0, c0 + n), A("j1", 0, n), float(step), float(base))
     lin(big_, keep_, -BIG, BIG)
-    short_lists(0, 3)
-    ts(A("tlu"), A("tl", 0, 20), p5, add)
     quant(A("uq"), A("us"), A("ut"))
     pick_u(1 - hs[0])
     pick_u(hs[0])
-    for half in range(2):
-        quant(A("tq0", H * half, H * half + H), A("ts0", H * half, H * half + H), A("x0", 640 * half, 640 * half + 640))
+    short_lists(0, 3)
 
     def table_constants():
-        cp(A("sa"), ind(A("ti", 0, 640), A("tlu")), "s")
-        cp(A("sb"), ind(A("ti", 640, 1280), A("tlu")), "s")
-        lin(A("s2"), A("s3"), 1.0, p5)
+        cp(A("sb"), ind(A("ti", 640, 1280), A("tlu")))
         low = slice(0, 4)
         for hh in range(2):
             for r_, c0 in ((0, 320 * hh), (1, 640 + 320 * hh), (6, 1280 + 320 * hh)):
                 dma("y", A("sa", rows=slice(r_ + 16 * hh, 128, 32)), A("ti", c0, c0 + 320, rows=low), "dsa", 128)
             dma("y", A("yz", rows=slice(5 + 16 * hh, 128, 32)), A("ti", 1280 + 320 * hh, 1600 + 320 * hh, rows=low), "dyz", 32)
-        dma("y", A("sa", rows=slice(7, 128, 16)), A("ti", 0, 320, rows=slice(0, 8)), "dsa", 128)
+        dma("y", A("sa", rows=slice(7, 128, 16)), A("ti", 960, 1280, rows=slice(0, 8)), "dsa", 128)
         dma("y", A("sa", rows=slice(3, 128, 16)), A("sb", rows=slice(3, 128, 16)), "dsa", 128)
-        for b in range(4):
-            dma("y", A("et", 512 * b, 512 * b + 512), A("e0", 3 - b, 515 - b), "det", 64)
+        for a in range(1, 4):
+            dma("y", A("s2", rows=slice(32 * a, 32 * a + 32)), A("s2", rows=slice(0, 32)), "ds2", 48)
 
     def late_constants():
         zero(A("xb", 0, 16), A("xb", 336, 352))
         for w in ("w0", "w1"):
-            zero(A(w, 1, 384, 2), A(w, 384, 400), A(w, 720, 736), A(w, 737, 1056, 2))
+            zero(A(w, 1, 320, 2), A(w, 320, 336), A(w, 656, 672), A(w, 673, 1056, 2))
         iota(A("jj", 0, 64), [[320, 2], [16, 32]], 160)
         iota(A("se", 176, 496), [[1, 320]], -80)
         zero(A("stb"), A("bw", 320, 336), A("se", 0, 176), A("se", 496, 816), A("oe", 80, 96))
         zero(*[A(w, c, c + 16) for w in ("wb", "wb2") for c in (0, 336)])
         zero(*[A("sn%d" % t, 88, 96) for t in range(R)])
 
-    def O(w, pad=0):
-        c0 = 400 if w in ("w0", "w1") else 16
-        return A(w, c0 - pad, c0 + 320 + pad)
+    def O(w, lo=0, hi=C):
+        c0 = 336 if w in ("w0", "w1") else 16
+        return A(w, c0 + lo, c0 + hi)
 
-    def own(w, xb="xb", back=0):
-        tr(A(xb, 16 - back, 336 - back), O(w))
+    def own(w, part=None, back=0):
+        lo, hi = {None: (0, C), 0: (0, H), 1: (H, C)}[part]
+        tr(A("xb", 16 - back + lo, 16 - back + hi), O(w, lo, hi))
 
-    def shifted(w, xb="xb", back=0):
-        tr(A(xb, 352 - back, 704 - back), O(w, 16))
+    def shifted(w, part=None, back=0):
+        lo, hi = {None: (0, 352), 0: (0, H), 1: (H, 352)}[part]
+        tr(A("xb", 352 - back + lo, 352 - back + hi), O(w, lo - 16, hi - 16))
 
-    def other(w):
-        tr(A(w, 0, 384, 2), A("xb", 0, 192))
-        tr(A(w, 736, 1056, 2), A("xb", 192, 352))
+    def other(w, part):
+        if part:
+            tr(A(w, 672, 1056, 2), A("xb", H, 352))
+        else:
+            tr(A(w, 0, 320, 2), A("xb", 0, H))
 
+    def gather(w, win, lst, l0, low=None):
+        for lo in (0, H):
+            src = ind(win, A(lst, l0 + lo // 16, l0 + lo // 16 + 10))
+            if low:
+                tt(O(w, lo, lo + H), src, A(low, lo, lo + H), mn)
+            else:
+                cp(O(w, lo, lo + H), src)
+
+    def early(t, part):
+        if part == 0:
+            for bank in (6, 7):
+                mm(bank, "up", "ups", 256 * (1 - hs[t]), "tq%d" % t, "ts%d" % t, 0, H)
+        if part == 1:
+            tr(A("xt", 0, H), P(6, 0, H))
+            for c in range(3):
+                act(A("sg", C * (17 + c), C * (17 + c) + H), P(7, 0, H), AF.Sign, -1.0, A("xt", 32 * c, 32 * c + 1))
+            for c in range(3):
+                f0, n = C * (17 + c), 32 * c + 32
+                act(A("sg", f0, f0 + n), A("sg", f0, f0 + n), AF.Relu, None, None, A("ac", 60 + c, 61 + c))
+                act(A("sg", f0 + n, f0 + H), A("sg", f0 + n, f0 + H), AF.Relu, -1.0, None, A("ac", c, c + 1))
+        if part == 2:
+            f0 = C * 18
+            tt(A("eqf", 0, H), P(6, 0, H), A("xt", 0, H), ALU.is_equal)
+            ts(A("fl", f0, f0 + 128), P(6, 0, 128), A("xt", 96, 97), ALU.is_ge, 0.5, sub)
+            ts(A("fl", f0 + 128, f0 + H), P(6, 128, H), A("xt", 96, 97), ALU.is_gt, 0.5, sub)
+            ts(A("fl", f0 + H, f0 + C), P(6, 0, H), A("xt", 128, 129), ALU.is_ge, 0.5, sub)
+            scan(A("eqs", 0, H), A("eqm", 0, H), A("eqf", 0, H), mul)
+            for c in (3, 4):
+                f1 = f0 + H * (c - 3)
+                scan(A("so", 160 * c + 80, 160 * c + 160), A("fl", f1, f1 + 80), A("fl", f1 + 80, f1 + H), add)
+
+    quant(A("tq0", 0, H), A("ts0", 0, H), A("x0", 0, 640))
+    send_t(0, 0)
+    early(0, 0)
+    table_constants()
+    quant(A("tq0", H, C), A("ts0", H, C), A("x0", 640, 1280))
+    send_t(0, 1)
+    early(0, 1)
+    early(0, 2)
     for t in range(R):
         h = hs[t]
         tq, tsc, lq, ls = "tq%d" % t, "ts%d" % t, "lq%d" % t, "ls%d" % t
@@ -339,7 +379,7 @@ def rank_program(g, core, T, topo):
             while len(pend[q]) > keep:
                 pend[q].pop(0)()
 
-        def unit(q, k, c):
+        def unit(q, k, c, first=0.0):
             n, slot = 32 * c + 32, 10 * k + c
             thr = A("xt", C * k + 32 * c, C * k + 32 * c + 1) if k < 4 else A(th, 16 + c, 17 + c)
             f0 = C * (cnt[q] % 20)
@@ -356,7 +396,7 @@ def rank_program(g, core, T, topo):
                 ts(A("fl", f0, f0 + n), P(k, 0, n), thr, ALU.is_ge, 0.5, sub)
                 if n < C:
                     ts(A("fl", f0 + n, f0 + C), P(k, n, C), thr, ALU.is_gt, 0.5, sub)
-                pend[q].append(lambda: scan(A("so", 160 * slot, 160 * slot + 160), A("fl", f0, f0 + 160), A("fl", f0 + 160, f0 + C), add))
+                pend[q].append(lambda: scan(A("so", 160 * slot, 160 * slot + 160), A("fl", f0, f0 + 160), A("fl", f0 + 160, f0 + C), add, add, first))
             else:
                 act(A("sg", f0, f0 + C), P(4 + k), AF.Sign, -1.0, thr)
 
@@ -377,10 +417,10 @@ def rank_program(g, core, T, topo):
             tr(A("xt", C * k, C * k + C), P(k))
 
         def ties(k):
-            c0 = C * k
-            tt(A("eqf", c0, c0 + C), P(k), A("xt", c0, c0 + C), ALU.is_equal)
+            c0, lo = C * k, 0 if k else H
+            tt(A("eqf", c0 + lo, c0 + C), P(k, lo, C), A("xt", c0 + lo, c0 + C), ALU.is_equal)
             flush("v")
-            pend["v"].append(lambda: scan(A("eqs", c0, c0 + C), A("eqm"), A("eqf", c0, c0 + C), mul))
+            pend["v"].append(lambda: scan(A("eqs", c0 + lo, c0 + C), A("eqm", lo, C), A("eqf", c0 + lo, c0 + C), mul))
 
         def tie_sums(k):
             k1 = 10 * (k + 2 * h if k > 1 else k)
@@ -389,18 +429,19 @@ def rank_program(g, core, T, topo):
         def ends(k, c0, c1):
             return A("so", 160 * (10 * k + c0) + 159, 160 * (10 * k + c1), 160)
 
-        def differences(k):
-            k0 = 10 * k
-            tt(A("d1", k0, k0 + NS[k]), A("ac", k0, k0 + NS[k]), A("ac", 60 + k0, 60 + k0 + NS[k]), sub)
+        def differences(k, n=None):
+            k0, n = 10 * k, n or NS[k]
+            tt(A("d1", k0, k0 + n), A("ac", k0, k0 + n), A("ac", 60 + k0, 60 + k0 + n), sub)
 
-        def places(k, name, c0):
-            k0, n = 10 * k, NS[k]
+        def places(k, name, c0, n=None):
+            k0, n = 10 * k, n or NS[k]
             tt(A(name, c0 + n, c0 + 10), ends(k, n, 10), A("ce", k0 + n, k0 + 10), add)
             tt(A(name, c0, c0 + n), A("d1", k0, k0 + n), A("ce", k0, k0 + n), add)
 
         def self_count(k, between=()):
             us, between = units("v", k), list(between)
-            ties(k)
+            if k:
+                ties(k)
             for u in us:
                 unit(*u)
                 if between:
@@ -409,30 +450,34 @@ def rank_program(g, core, T, topo):
                 f()
             tie_sums(k)
 
-        if t == 0:
-            table_constants()
-        for bank in (0, 4, 2, 1, 5, 6, 3, 7):
+        for bank in (0, 4, 1, 5, 2, 6, 3, 7):
             k = bank % 4
             mm(bank, "up", "ups", 128 * (2 * (h if k % 2 else 1 - h) + k // 2), tq, tsc)
-        thresholds(0)
-        run_units(units("s", 0))
+        tr(A("xt", H, C), P(0, H, C))
+        for c in range(5):
+            act(A("sg", C * c, C * c + H), P(4, H, C), AF.Sign, -1.0, A("xt", 32 * c, 32 * c + 1))
+        for c in range(5):
+            act(A("sg", C * c, C * c + H), A("sg", C * c, C * c + H), AF.Relu, -1.0, None, A("ac", 50 + c, 51 + c))
+        cnt["s"] = 5
 
         def first_write():
             cp(A(th, 0, 10), A("xt", 2 * C, 3 * C, 32))
             send(dst, A(th, 16, 26), A(th, 0, 10), "at%d" % t)
 
-        self_count(0, [lambda: thresholds(2), lambda: thresholds(1), first_write])
+        self_count(0, [lambda: thresholds(1), lambda: ties(0), lambda: thresholds(2), lambda: None, first_write])
         run_units(units("s", 1))
         flush("s")
         mine = units("v", 1)
         ties(1)
+        differences(0, 3)
+        tt(A("ce", 0, 5), A("ce", 0, 5), A("ac", 50, 55), add)
         unit(*mine[0])
-        differences(0)
-        unit(*mine[1])
-        places(0, rw, 52)
+        places(0, rw, 52, 3)
         send(dst, A(rw, 12 * h, 12 * h + 12), A(rw, 52, 64), "ar%d" % t, A(rw, 12 - 12 * h, 24 - 12 * h))
         iota(A("sc2"), [[0, 640]])
-        run_units(mine[2:])
+        if t == 0:
+            sel(A("e0"), A("one"), [[-1, 528]], ALU.is_equal, 3, 4)
+        run_units(mine[1:])
         tie_sums(1)
         thresholds(3)
         if t == 0:
@@ -453,36 +498,48 @@ def rank_program(g, core, T, topo):
         run_units(srest[:2])
         ties(3)
         differences(2)
-        gap()
+        unit(*units("v", 4)[0])
         places(2, th, 32)
         send(dst, A(th, 48, 58), A(th, 32, 42), "ac%d" % t)
         if t == 0:
             zero(A("xc", 0, 18), A("xc", 336, 352))
-        gap()
-        gap()
+            for b in range(4):
+                dma("y", A("et", 512 * b, 512 * b + 512), A("e0", 3 - b, 515 - b), "det", 64)
         run_units(units("s", 4))
         flush("s")
-        run_units(units("v", 4))
+        run_units(units("v", 4)[1:])
+        fillers = [(lambda k: lambda: ts(A("ii", 10 * k, 10 * k + 10), A(rw, 12 * k, 12 * k + 10), 0.5, mul, 0.25, sub))(k) for k in range(2)]
+        fillers += [(lambda k: lambda: ts(A("s2", 24 - 16 * k, 320, 32), A("ii", 10 * k, 10 * k + 10), 240.0, sub))(k) for k in range(2)]
+        fillers += [lambda: tr(A("xc", 18, 338), A("wa")), lambda: tr(A("pr"), A("s2")), lambda: ts(A("az"), ind(A("xc"), L("turn")), base_, add)]
+
+        def filler():
+            if fillers:
+                fillers.pop(0)()
+
         run_units(srest[2:3])
         cp(A("zl"), ind(A(rw), L("zm")))
         for k in range(2):
             ts(A("xl", k, 20, 2), A(rw, 12 * k, 12 * k + 10), K(11 + k), add)
         flush("v")
         scat(A("sc1"), A("zl", 0, 20), A("sa"))
+        tie_sums(3)
         for e in range(2):
             tr(A("xd", 16 + 192 * e, 176 + 192 * e), A("sc1", e, 320, 2))
-        tie_sums(3)
+        gap()
         for e in range(2):
             cp(A("xd", 21 + 192 * e, 176 + 192 * e, 16), A("xd", 214 - 192 * e, 368 - 192 * e, 16))
         cp(A(ml, 0, 22), A("xd", 23, 368, 16))
+        gap()
         send(dst, A(ml, 32, 54), A(ml, 0, 22), "am%d" % t)
         up, down = (slice(0, 112), slice(16, 128)), (slice(16, 128), slice(0, 112))
         for c0, s0, way, sem in ((64, 0, (up, down)[h], "d3%d" % t), (96, 32, (down, up)[h], "d4%d" % t)):
             dma("y", A(ml, c0, c0 + 22, rows=way[0]), A(ml, s0, s0 + 22, rows=way[1]), sem)
-            if t == 0 and s0 == 0:
-                send_t(0, 0)
-                send_t(0, 1)
-                late_constants()
+            if s0 == 0:
+                if t:
+                    send_t(t, 0)
+                    send_t(t, 1)
+                else:
+                    late_constants()
         flush("v")
         for e in range(2):
             tr(A("oa", 1 - e, 320, 2), A("xd", 16 + 192 * e, 176 + 192 * e))
@@ -498,81 +555,93 @@ def rank_program(g, core, T, topo):
         for k in range(2):
             tr(A("x1", 160 * k, 160 * k + 160), A("pf", 805 * k + 9, 805 * k + 805, 5))
             tr(A("x2", 160 * k, 160 * k + 160), A("pf", 805 * k + 4, 805 * k + 800, 5))
-        gap()
+        flush("v")
+        filler()
+        filler()
         scan(A("cu", 32, 352), A("x1"), A("x2"), add, sub)
         n4, far = NS[4], (sub, add)[h]
         tt(A("rb", 1 - h, 2 * n4, 2), A(th, 48, 48 + n4), A("ac", 40, 40 + n4), far)
         tt(A("rb", 1 - h + 2 * n4, 20, 2), A(th, 48 + n4, 58), ends(4, n4, 10), far)
-        gap()
-        tt(A("pb", 0, 10), A("cu", 63, 352, 32), A("cu", 31, 320, 32), sub)
-        gap()
-        tt(A("ce", 30, 40), A("ce", 30, 40), A("pb", 0, 10), (add, sub)[h])
-        while rest:
+        while len(rest) > 2:
             gap()
+        tt(A("pb", 0, 10), A("cu", 63, 352, 32), A("cu", 31, 320, 32), sub)
+        cp(A("bl", 1 - h, 20, 2), A("rb", 1 - h, 20, 2))
+        unit("v", 3, 8, A("ce", 38, 39))
+        tt(A("ce", 30, 40), A("ce", 30, 40), A("pb", 0, 10), (add, sub)[h])
         differences(3)
-        flush("v")
+        last = pend["v"].pop()
+        unit("v", 3, 9, A("ce", 39, 40))
         n3 = NS[3]
-        tt(A("rb", h + 2 * n3, 20, 2), ends(3, n3, 10), A("ce", 30 + n3, 40), add)
+        last()
+        tt(A("rb", h + 2 * n3, 16, 2), ends(3, n3, 8), A("ce", 30 + n3, 38), add)
         tt(A("rb", h, 2 * n3, 2), A("d1", 30, 30 + n3), A("ce", 30, 30 + n3), add)
-        cp(A("bl"), A("rb"))
+        flush("v")
+        filler()
+        filler()
+        cp(A("bl", h, 16, 2), A("rb", h, 16, 2))
+        cp(A("bl", h + 16, 20, 2), ends(3, 8, 10))
+        filler()
+        filler()
         scat(A("sc2"), A("bl"), A("wa"))
         if t == 0:
-            quant(A("eq"), A("es"), A("et"))
             short_lists(3, len(LISTS))
+            fillers = [(lambda b: lambda: quant(A("eq", 128 * b, 128 * b + 128), A("es", 128 * b, 128 * b + 128), A("et", 512 * b, 512 * b + 512)))(b)
+                       for b in range(4)] + fillers
+            filler()
+        filler()
+        for e in range(2):
+            tr(A("xs", C * e, C * e + C), A("sc2", e, 640, 2))
+        filler()
+        for ks, kd in ((0, 0), (1, 1), (2, 2), (3, 3), (5, 6)):
+            for hh in range(2):
+                tt(A("st", kd + 16 * hh, 640, 32), A("xs", ks, 640, 32), A("xs", 16 + ks, 640, 32), add)
+        filler()
+        for e in range(2):
+            tr(A("ob", 1 - e, 640, 2), A("st", C * e, C * e + C))
         for b in range(4):
             mm(b, "eq", "es", 128 * b, tq, tsc)
         for b in range(4):
             mm(4 + b, "eq", "es", 128 * b, lq, ls)
         for b in range(4):
             cp(A("dw", 480 * b + 160, 480 * b + 480), P(b), "s")
-        for b in range(4):
-            act(A("dp", C * b, C * b + C), P(4 + b), AF.Copy, 0.5)
-        for e in range(2):
-            tr(A("xs", C * e, C * e + C), A("sc2", e, 640, 2))
-        for ks, kd in ((0, 0), (1, 1), (2, 2), (3, 3), (5, 6)):
-            for hh in range(2):
-                tt(A("st", kd + 16 * hh, 640, 32), A("xs", ks, 640, 32), A("xs", 16 + ks, 640, 32), add)
-        for e in range(2):
-            tr(A("ob", 1 - e, 640, 2), A("st", C * e, C * e + C))
-        tt(O("w0"), ind(A("ob"), A("bl")), A("wi"), mn)
-        halves = [(lambda b, e: lambda: cp(A(("bt", "bu")[e], b, 640, 4), ind(A("dp", C * b, C * b + C), A("mu", 12 * e, 12 * e + 10)), "s"))(b, e)
-                  for b in range(4) for e in range(2)]
-        fillers = [(lambda k: lambda: ts(A("ii", 10 * k, 10 * k + 10), A(rw, 12 * k, 12 * k + 10), 0.5, mul, 0.25, sub))(k) for k in range(2)]
-        fillers += [lambda: ts(A("cl", 6, 20), A("ci", 6, 20), 703.0, mn) if t == 0 else None, lambda: ts(A("mu"), ind(A(ml), L("mm%d" % h)), 160.0, add)]
-        fillers += [(lambda k: lambda: ts(A("s2", 24 - 16 * k, 320, 32), A("ii", 10 * k, 10 * k + 10), 240.0, sub))(k) for k in range(2)]
-        fillers += [lambda: tr(A("xc", 18, 338), A("wa")), lambda: tr(A("pr"), A("s2")), lambda: ts(A("az"), ind(A("xc"), L("turn")), base_, add)]
-
-        def filler():
-            if fillers:
-                fillers.pop(0)()
-
+        filler()
+        gather("w0", A("ob"), "bl", 0, "wi")
+        halves = [(lambda b: lambda: act(A("dp", C * b, C * b + C), P(4 + b), AF.Copy, 0.5))(b) for b in range(4)]
+        halves += [(lambda b, e: lambda: cp(A(("bt", "bu")[e], b, 640, 4), ind(A("dp", C * b, C * b + C), A("mu", 12 * e, 12 * e + 10)), "s"))(b, e)
+                   for b in range(4) for e in range(2)]
         for s in range(8):
             cur, nxt = "w%d" % (s % 2), "w%d" % (1 - s % 2)
             l0 = 32 * (min(s, 6) % 2)
             if s:
                 lin(A("yy"), O(cur), keep_, big_)
-            filler()
-            own(cur)
+            own(cur, 0)
+            if 0 < s < 7:
+                shifted(cur, 0)
+            own(cur, 1)
+            if 0 < s < 7:
+                shifted(cur, 1)
+            other(cur, 0)
+            other(cur, 1)
+            if s < 7:
+                ts(A("li", l0, l0 + 32), ind(A("xb", 0, 704 if s else 352), L("next" if s else "turn")), base_, add)
+            else:
+                cp(A("o2"), ind(A(cur), A("az", 0, 20)), "s")
             if s == 1 and t == 0:
                 dma("y", u8(A("wq")), T.wc[:], "dwq")
                 dma("y", A("wp"), T.ws[:], "dwp")
                 dma("y", A("vt"), T.v[:], "dv")
                 lin(A("jj", 64, 128), A("jj", 0, 64), 1.0, i4)
-            if 0 < s < 7:
-                shifted(cur)
-            other(cur)
-            if s < 7:
-                ts(A("li", l0, l0 + 32), ind(A("xb", 0, 704 if s else 352), L("next" if s else "turn")), base_, add)
-            else:
-                cp(A("o2"), ind(A(cur), A("az", 0, 20)), "s")
-            filler()
-            if 2 <= s < 6:
+                ts(A("cl", 6, 20), A("ci", 6, 20), 703.0, mn)
+            if s == 2:
+                ts(A("mu"), ind(A(ml), L("mm%d" % h)), 160.0, add)
+            if 1 <= s < 7:
                 halves.pop(0)()
                 halves.pop(0)()
-            if s == 6:
+            if s == 7:
                 dma("g", A("bt"), A("bu"), "dacc", None, True)
-            tt(O(nxt), ind(A(cur), A("li", l0, l0 + 20)), A("yy" if s else "yz"), mn)
-        own("w0")
+            gather(nxt, A(cur), "li", l0, "yy" if s else "yz")
+        own("w0", 0)
+        own("w0", 1)
         tr(A("xc", 16, 336), A("o2"))
         tt(A("mm", 0, 20), A("xb", 21, 336, 16), A("xc", 22, 336, 16), mn)
         tt(A("mm", 20, 40), A("xb", 22, 336, 16), A("xc", 21, 336, 16), mn)
@@ -587,9 +656,10 @@ def rank_program(g, core, T, topo):
         tt(A("yp"), ind(A("xb"), L("own", 2)), A("jj", 64, 128), mn)
         cp(A("yl"), A("yp"))
         scat(A("se", 16, 816), A("yl", 32, 52), A("pr"))
-        cp(O("wb"), ind(A("se", 16, 496), A("yl", 0, 20)))
-        own("wb", "xb", 8)
-        shifted("wb", "xb", 8)
+        gather("wb", A("se", 16, 496), "yl", 0)
+        for part in range(2):
+            own("wb", part, 8)
+            shifted("wb", part, 8)
         cp(A(sn, 0, 64), ind(A("xb"), L("own", 2)))
         send(dst, A(sn, 64, 88), A(sn, 32, 56), "an%d" % t)
         quant(A("bq"), A("bs"), A("bt"))
@@ -622,10 +692,13 @@ def rank_program(g, core, T, topo):
                 rl = A("rl", C * b + c0, C * b + c0 + H)
                 act(rl, P(4 + b, 0, H), AF.Relu, 0.03125)
                 tt(A("xa", e0 + b, e0 + 640, 4), P(b, 0, H), rl, add)
+            if half and t + 1 < R:
+                early(t + 1, 0)
+                early(t + 1, 1)
             quant(A(nq, c0, c0 + H), A(ns, c0, c0 + H), A("xa", e0, e0 + 640))
-            if t + 1 < R:
-                send_t(t + 1, half)
-            else:
+            if half and t + 1 < R:
+                early(t + 1, 2)
+            if t + 1 == R:
                 dma("y", T.oc[:, 4 * c0:4 * c0 + 640], u8(A(nq, c0, c0 + H)), "dout")
                 if half == 0:
                     cp(A("er"), ind(A("j1"), A("ou", 0, 10)), "s")

@@ -6,35 +6,42 @@ SCRATCH = {"ps": ("psum", [128, 4096], F32)}
 for _n, _w, _t in [
     ("x0", 1280, BF), ("xa", 1280, BF), ("ut", 512, BF), ("vt", 512, BF), ("uq", 128, MX), ("us", 128, U8), ("up", 512, MX), ("ups", 512, U8),
     ("vq", 128, MX), ("vs", 128, U8), ("wq", 512, MX), ("wp", 512, U8), ("one", 528, BF), ("e0", 528, BF), ("et", 2048, BF), ("eq", 512, MX), ("es", 512, U8),
-    ("bq", 160, MX), ("bs", 160, U8), ("zq", 320, MX), ("zs", 320, U8), ("bt", 640, BF), ("bu", 640, BF), ("yt", 1280, BF), ("dw", 1920, BF), ("dp", 1280, BF),
+    ("zq", 320, MX), ("zs", 320, U8), ("bt", 640, BF), ("bu", 640, BF), ("yt", 1280, BF), ("dw", 1920, BF),
+    ("dz", 1280, BF), ("td", 640, BF), ("aq", 160, MX), ("az2", 160, U8), ("xe", 704, BF),
     ("rl", 1280, F32), ("ysb", 320, F32), ("er", 160, F32),
     ("xt", 1280, F32), ("fl", 6400, BF), ("sg", 6400, BF), ("so", 8000, F16), ("ac", 120, F32), ("eqf", 1280, BF), ("eqs", 1280, BF), ("eqm", 320, BF),
-    ("cf", 3200, BF), ("pf", 1616, F16), ("x1", 320, F16), ("x2", 320, F16), ("cu", 352, F32),
+    ("cf", 3200, BF), ("pf", 1616, F16), ("x1", 320, F16), ("x2", 320, F16), ("cu", 384, F16),
     ("ck", 60, F32), ("ce", 40, F32), ("d1", 40, F32), ("pb", 40, F32), ("rb", 20, F32), ("ii", 20, I32),
-    ("zl", 32, U16), ("xl", 20, U16), ("bl", 20, U16), ("az", 32, U16), ("mu", 32, U16), ("li", 64, U16), ("yl", 64, U16), ("lu", 32, U16), ("ou", 32, U16),
+    ("zl", 32, U16), ("xl", 20, U16), ("bl", 20, U16), ("az", 32, U16), ("mu", 32, U16), ("li", 64, U16), ("yl", 64, U16), ("lu", 32, U16),
     ("sa", 320, BF), ("sb", 320, BF), ("j1", 320, F32), ("sc1", 320, BF), ("xd", 384, BF), ("oa", 704, BF), ("wa", 320, BF), ("wi", 320, BF),
-    ("s2", 320, BF), ("pr", 320, BF), ("sc2", 640, BF), ("xs", 640, BF), ("st", 640, BF), ("ob", 640, BF), ("w0", 1056, BF), ("w1", 1056, BF),
-    ("yy", 320, BF), ("yz", 320, BF), ("o2", 320, BF), ("xb", 704, BF), ("xc", 352, BF), ("mm", 60, F32), ("stb", 640, BF), ("bw", 656, BF),
+    ("s2", 320, BF), ("pr", 320, BF), ("sc2", 640, BF), ("ob", 640, BF), ("w0", 1056, BF), ("w1", 1056, BF),
+    ("yy", 320, BF), ("yz", 320, BF), ("o2", 320, BF), ("xb", 704, BF), ("xc", 352, BF), ("mm", 160, F32), ("stb", 336, BF), ("bw", 656, BF),
     ("wb", 352, BF), ("wb2", 352, BF), ("jj", 128, F32), ("yp", 64, F32), ("se", 816, BF), ("oe", 96, BF),
-    ("ti", 1920, BF), ("pi", 8, I32), ("ui", 32, I32), ("ul", 32, U16), ("cc", 64, F32), ("ci", 20, F32), ("cl", 20, U16),
-    ("tl", 40, F32), ("tlu", 20, U16),
+    ("ti", 1920, BF), ("pi", 40, I32), ("ul", 32, U16), ("cc", 64, F32), ("ci", 28, F32), ("cl", 28, U16),
+    ("tl", 40, F32),
 ]:
     SCRATCH[_n] = ("sbuf", [128, _w], _t)
+for _n in ("xs", "st"):
+    SCRATCH[_n] = ("sbuf", [128, 20, 32], BF)
 for _t in range(R + 1):
     SCRATCH["tq%d" % _t] = ("sbuf", [128, C], MX)
     SCRATCH["ts%d" % _t] = ("sbuf", [128, C], U8)
 for _t in range(R):
-    SCRATCH["lq%d" % _t] = ("sbuf", [128, C], MX)
-    SCRATCH["ls%d" % _t] = ("sbuf", [128, C], U8)
+    for _n in ("lq", "bq"):
+        SCRATCH["%s%d" % (_n, _t)] = ("sbuf", [128, C // 2], MX)
+    for _n in ("ls", "bs"):
+        SCRATCH["%s%d" % (_n, _t)] = ("sbuf", [128, C // 2], U8)
     SCRATCH["th%d" % _t] = ("sbuf", [128, 64], F32)
     SCRATCH["rw%d" % _t] = ("sbuf", [128, 64], F32)
     SCRATCH["ml%d" % _t] = ("sbuf", [128, 128], BF)
     SCRATCH["sn%d" % _t] = ("sbuf", [128, 96], BF)
 SEMAPHORES = (["cv", "cs", "cp", "cg", "dx", "dx2", "du", "dv", "dwq", "dwp", "dsa", "dyz", "det", "dout", "sent", "dacc", "ao", "dm", "ds2"]
-              + ["%s%d" % (k, t) for k in ("aq", "as", "an", "at", "ar", "ac", "am", "d1", "d2", "d3", "d4") for t in range(R)])
+              + ["%s%d" % (k, t) for k in ("aq", "as", "an", "al", "at", "ar", "ac", "am", "d1", "d2", "d3", "d4") for t in range(R)])
 
-NS = (5, 5, 4, 5, 7)
-BIG = 1.0e6
+NS = (5, 5, 5, 5, 7)
+BIG = 1.0e8
+BACK = 300
+NT = 2
 
 
 def rank_program(g, core, T, topo):
@@ -45,6 +52,7 @@ def rank_program(g, core, T, topo):
     total = {}
     seen = {q: {} for q in Q}
     log = {}
+    knew, size = {}, {}
 
     def A(name, lo=0, hi=None, step=1, rows=None):
         hi = SCRATCH[name][1][1] if hi is None else hi
@@ -58,14 +66,26 @@ def rank_program(g, core, T, topo):
             m = sum(1 << c for c in range(lo, hi, step))
         return (ap, [(name, m)])
 
+    def B(name, b0=0, b1=20, c0=0, c1=32):
+        return (T[name][:, b0:b1, c0:c1], [(name, sum(1 << (32 * b + c) for b in range(b0, b1) for c in range(c0, c1)))])
+
     def ind(win, off, word=False):
         ap = win[0].bitcast(dt.uint32) if word else win[0]
         return (ap.indirect(off[0]), win[1] + off[1])
 
     def wait(q, tok):
-        if seen[q].get(tok[0], 0) < tok[1]:
-            Q[q].wait_ge(T.sem[tok[0]], tok[1])
-            seen[q][tok[0]] = tok[1]
+        s, n = tok
+        if seen[q].get(s, 0) < n:
+            if s == "c" + q:
+                k, gone = total[s], 0
+                while k > n and gone < BACK:
+                    gone += size[(s, k)]
+                    k -= 1
+                n = k
+            Q[q].wait_ge(T.sem[s], n)
+            seen[q][s] = n
+            for s2, n2 in knew.get((s, n), {}).items():
+                seen[q][s2] = max(seen[q].get(s2, 0), n2)
 
     def order(q, reads, writes):
         need = {}
@@ -74,7 +94,7 @@ def rank_program(g, core, T, topo):
                 for e in log.get(name, []):
                     if e[0] & m and (w or e[2] or (name == "ps" and e[3] != q)) and not (q == "p" and e[3] == "p"):
                         need[e[1][0]] = max(need.get(e[1][0], 0), e[1][1])
-        for s in need:
+        for s in sorted(need, key=lambda s: s == "c" + q):
             wait(q, (s, need[s]))
 
     def note(q, tok, reads, writes):
@@ -92,6 +112,9 @@ def rank_program(g, core, T, topo):
             wait(q, (s, total.get(s, 0)))
         total[s] = total.get(s, 0) + 1
         fn().then_inc(T.sem[s], 1)
+        knew[(s, total[s])] = dict(seen[q])
+        narrow = q == "v" and all(SCRATCH[n][2] in (BF, F16) or bin(m).count("1") < 2 and n != "ps" for n, m in writes + reads)
+        size[(s, total[s])] = max(64, bin(writes[0][1]).count("1") // (2 if narrow else 1))
         note(q, (s, total[s]), reads, writes)
 
     def x(a):
@@ -196,11 +219,12 @@ def rank_program(g, core, T, topo):
     band, shr = ALU.bitwise_and, ALU.arith_shift_right
     parts = [rank ^ (1 << t) for t in range(R)]
     hs = [1 if rank > p else 0 for p in parts]
-    H = C // 2
+    H, CUT = C // 2, 192
 
     LISTS = [("next", 32, ((16, 369), (384, 33))), ("turn", 32, ((18, 19), (34, 35))), ("zm", 1, ((0, 40), (24, 12))),
-             ("own", 32, ((16, 368), (384, 32))), ("far", 32, ((32, 352), (400, 16))), ("mm0", 2, ((1, 97), (65, 33))), ("mm1", 2, ((32, 64), (96, 0))),
-             ("mg0", 2, ((0, 64), (1, 65))), ("mg1", 2, ((64, 0), (65, 1))), ("ol", 2, (((32, 64), (33, 65)), ((64, 32), (65, 33)))[hs[R - 1]])]
+             ("own", 32, ((16, 368), (384, 32))), ("far", 32, ((32, 352), (400, 16))), ("mm0", 2, ((0, 96), (64, 32))), ("mm1", 2, ((33, 65), (97, 1))),
+             ("ol", 2, (((32, 64), (33, 65)), ((64, 32), (65, 33)))[hs[R - 1]]), ("mg0", 2, ((16, 32), (17, 33))), ("mg1", 2, ((32, 16), (33, 17))),
+             ("far2", 64, ((48, 17), (113, 16))), ("own2", 64, ((16, 49), (81, 48)))]
 
     def L(name, k=1):
         i = [e[0] for e in LISTS].index(name)
@@ -212,19 +236,13 @@ def rank_program(g, core, T, topo):
         op("v", lambda: g.vector.tensor_copy(o_[0].bitcast(dt.uint32), i_[0]), [o_], [i_])
         cp(A("ups", 256 * hh, 256 * hh + 256), ind(A("us"), l_), "s")
 
-    def send_t(t, half):
-        dst = T.cores[parts[t]]
-        send(dst, u8(A("lq%d" % t, H * half, H * half + H)), u8(A("tq%d" % t, H * half, H * half + H)), "aq%d" % t, None, 2)
-        if half:
-            send(dst, A("ls%d" % t), A("ts%d" % t), "as%d" % t)
-
     dma("s", A("ut"), T.u[:], "du")
     dma("y", A("x0", 0, 640), T.x[:, 0:640], "dx")
     dma("y", A("x0", 640, 1280), T.x[:, 640:1280], "dx2")
     iota(A("j1"), [[1, 320]])
     iota(A("pi", 0, 1), [[0, 1]], 0, 1, False)
     iota(A("tl", 0, 20), [[32, 10], [320, 2]])
-    iota(A("ui"), [[8, 4], [32, 4], [0, 2]], 0, 0, False)
+    iota(A("pi", 8, 40), [[8, 4], [32, 4], [0, 2]], 0, 0, False)
     fill(A("one"), 1.0)
     fill(A("ck", 0, 40), 160.0)
     fill(A("ck", 40, 60), 480.0)
@@ -235,12 +253,13 @@ def rank_program(g, core, T, topo):
     for c0, c1 in ((0, 16), (176, 208), (368, 384)):
         fill(A("xd", c0, c1), 0.0)
     fill(A("pf", 4, 810, 805), 0.0)
-    fill(A("ck", 3, 5), 80.0)
-    fill(A("cu", 0, 32), 0.0)
-    for c0, n, step, base in ((0, 320, 1, -224), (320, 128, 2, -496), (448, 192, 2, 112), (640, 160, 2, -496), (800, 160, 2, 176), (960, 320, 1, -160)):
+    fill(A("ck", 2, 5), 80.0)
+    fill(A("tl", 20, 40), -1.0)
+    fill(A("cu", 31, 224, 192), 0.0)
+    for c0, n, step, base in ((0, 320, 1, -160), (320, 160, 2, -496), (480, 160, 2, 176), (640, 192, 2, -496), (832, 128, 2, 240), (960, 320, 1, -96)):
         lin(A("ti", c0, c0 + n), A("j1", 0, n), float(step), float(base))
     for k in range(5):
-        lin(A("ti", 1280 + 128 * k, 1408 + 128 * k), A("j1", 0, 128), 2.0 ** k, 128.0 * 2 ** k)
+        lin(A("ti", 1280 + 128 * k, 1408 + 128 * k), A("j1", 0, 128), 2.0 ** (k + 10), 128.0 * 2 ** (k + 10))
     sel(A("eqm", rows=slice(0, 32)), A("one", 0, 320, rows=slice(0, 32)), [[0, 10], [-1, 32]], ALU.not_equal, 0, 1)
     for a in range(1, 4):
         dma("y", A("eqm", rows=slice(32 * a, 32 * a + 32)), A("eqm", rows=slice(0, 32)), "dm", 48)
@@ -251,26 +270,24 @@ def rank_program(g, core, T, topo):
     ts(A("pi", 3, 4), p0, 1, shr, 7, band)
     ts(A("pi", 4, 5), p0, 1, band)
     ts(A("pi", 5, 6), p0, 31, band)
+    fill(A("tl", 20, 40, 3), 0.0)
     fill(A("yz"), BIG)
     cp(K(0, 5), A("pi", 1, 6))
-    fill(A("st"), BIG)
-    ts(A("tlu"), A("tl", 0, 20), p5, add)
+    fill(B("st"), BIG)
+    ts(A("xl"), A("tl", 0, 20), p5, add)
     tt(both, par, run, mul)
     ts(K(6), i4, 5.0, ALU.is_equal)
     ts(K(7), i4, 6.0, ALU.is_equal)
-    cp(A("ul"), A("ui"))
-    cp(A("sa"), ind(A("ti", 0, 640), A("tlu")))
+    cp(A("ul"), A("pi", 8, 40))
+    cp(A("sa"), ind(A("ti", 0, 640), A("xl")))
     iota(A("s2", rows=slice(0, 32)), [[32, 10], [0, 32]], -160, 1)
     keep_, big_, base_ = K(8), K(9), K(10)
-    lin(keep_, K(6), 1.0, K(7))
-    lin(base_, run, -64.0, 560.0)
-    lin(K(11), run, 320.0, 0.0)
-    lin(K(12), run, -384.0, 384.0)
 
-    def short_lists(i0, i1):
-        for level in range(5):
-            for i, (name, step, b) in list(enumerate(LISTS))[i0:i1]:
-                k0, k1 = K(20 + i), K(30 + i)
+    def short_lists(which, levels=range(5)):
+        for level in levels:
+            for i in which:
+                name, step, b = LISTS[i]
+                k0, k1 = K(20 + i), K(40 + i)
                 if level == 0:
                     lin(k0, hq, float(step), float(b[0][0]))
                 elif level == 4:
@@ -279,23 +296,30 @@ def rank_program(g, core, T, topo):
                     src, f = ((par, b[1][0] - b[0][0]), (run, b[0][1] - b[0][0]), (both, b[1][1] - b[1][0] - b[0][1] + b[0][0]))[level - 1]
                     lin(*((k1, src, float(f), k0) if level % 2 else (k0, src, float(f), k1)))
 
+    short_lists([2], [0])
+    lin(keep_, K(6), 1.0, K(7))
+    lin(base_, run, -64.0, 560.0)
+    lin(K(11), run, 320.0, 0.0)
+    lin(K(12), run, -384.0, 384.0)
     for k in range(6):
-        n = NS[(0, 1, 2, 3, 2, 3)[k]] if k else 3
+        if k % 4 == 0:
+            short_lists([2], [1 + k // 4])
+        n = NS[(0, 1, 2, 3, 2, 3)[k]] if k else 2
         lin(A("ck", 10 * k, 10 * k + n), A("j1", 0, n), 32.0, 32.0 + 320 * (k // 4))
     lin(big_, keep_, -BIG, BIG)
+    short_lists([2], [3])
     quant(A("uq"), A("us"), A("ut"))
     pick_u(1 - hs[0])
-    pick_u(hs[0])
-    short_lists(0, 3)
+    short_lists([2], [4])
+    cp(A("sb"), ind(A("ti", 640, 1280), A("xl")), "s")
 
     def table_constants():
-        cp(A("sb"), ind(A("ti", 640, 1280), A("tlu")))
         low = slice(0, 4)
         for hh in range(2):
             for r_, c0 in ((0, 320 * hh), (1, 640 + 320 * hh), (6, 1280 + 320 * hh)):
                 dma("y", A("sa", rows=slice(r_ + 16 * hh, 128, 32)), A("ti", c0, c0 + 320, rows=low), "dsa", 128)
             dma("y", A("yz", rows=slice(5 + 16 * hh, 128, 32)), A("ti", 1280 + 320 * hh, 1600 + 320 * hh, rows=low), "dyz", 32)
-        dma("y", A("sa", rows=slice(7, 128, 16)), A("ti", 960, 1280, rows=slice(0, 8)), "dsa", 128)
+        dma("y", A("sa", rows=slice(7, 128, 16)), A("ti", 0, 320, rows=slice(0, 8)), "dsa", 128)
         dma("y", A("sa", rows=slice(3, 128, 16)), A("sb", rows=slice(3, 128, 16)), "dsa", 128)
         for a in range(1, 4):
             dma("y", A("s2", rows=slice(32 * a, 32 * a + 32)), A("s2", rows=slice(0, 32)), "ds2", 48)
@@ -303,38 +327,46 @@ def rank_program(g, core, T, topo):
     def late_constants():
         zero(A("xb", 0, 16), A("xb", 336, 352))
         for w in ("w0", "w1"):
-            zero(A(w, 1, 320, 2), A(w, 320, 336), A(w, 656, 672), A(w, 673, 1056, 2))
+            zero(A(w, 1, 384, 2), A(w, 384, 400), A(w, 720, 736), A(w, 737, 1056, 2))
         iota(A("jj", 0, 64), [[320, 2], [16, 32]], 160)
         iota(A("se", 176, 496), [[1, 320]], -80)
-        zero(A("stb"), A("bw", 320, 336), A("se", 0, 176), A("se", 496, 816), A("oe", 80, 96))
+        zero(A("bw", 320, 336), A("oe", 80, 96), A("mm", 1, 160, 4), A("mm", 82, 160, 4))
+        iota(A("mm", 2, 80, 4), [[0, 20]], 1)
+        iota(A("mm", 3, 80, 4), [[0, 20]], -16000000)
+        iota(A("mm", 83, 160, 4), [[0, 20]], 16000000)
         zero(*[A(w, c, c + 16) for w in ("wb", "wb2") for c in (0, 336)])
-        zero(*[A("sn%d" % t, 88, 96) for t in range(R)])
+        zero(A("xe", 640, 704, 2))
 
     def O(w, lo=0, hi=C):
-        c0 = 336 if w in ("w0", "w1") else 16
+        c0 = 400 if w in ("w0", "w1") else 16
         return A(w, c0 + lo, c0 + hi)
 
-    def own(w, part=None, back=0):
-        lo, hi = {None: (0, C), 0: (0, H), 1: (H, C)}[part]
-        tr(A("xb", 16 - back + lo, 16 - back + hi), O(w, lo, hi))
+    def own(w, part=None):
+        lo, hi = {None: (0, C), 0: (0, CUT), 1: (CUT, C)}[part]
+        tr(A("xb", 16 + lo, 16 + hi), O(w, lo, hi))
 
-    def shifted(w, part=None, back=0):
-        lo, hi = {None: (0, 352), 0: (0, H), 1: (H, 352)}[part]
-        tr(A("xb", 352 - back + lo, 352 - back + hi), O(w, lo - 16, hi - 16))
+    def shifted(w, part=None):
+        lo, hi = {None: (0, 352), 0: (0, CUT), 1: (CUT, 352)}[part]
+        tr(A("xb", 352 + lo, 352 + hi), O(w, lo - 16, hi - 16))
 
     def other(w, part):
         if part:
-            tr(A(w, 672, 1056, 2), A("xb", H, 352))
+            tr(A(w, 736, 1056, 2), A("xb", CUT, 352))
         else:
-            tr(A(w, 0, 320, 2), A("xb", 0, H))
+            tr(A(w, 0, 384, 2), A("xb", 0, CUT))
 
     def gather(w, win, lst, l0, low=None):
-        for lo in (0, H):
-            src = ind(win, A(lst, l0 + lo // 16, l0 + lo // 16 + 10))
+        for lo, hi in ((0, CUT), (CUT, C)):
+            src = ind(win, A(lst, l0 + lo // 16, l0 + hi // 16))
             if low:
-                tt(O(w, lo, lo + H), src, A(low, lo, lo + H), mn)
+                tt(O(w, lo, hi), src, A(low, lo, hi), mn)
             else:
-                cp(O(w, lo, lo + H), src)
+                cp(O(w, lo, hi), src)
+
+    def again():
+        quant(A("aq"), A("az2"), A("td"))
+        for b in range(NT):
+            mm(b, "eq", "es", 128 * b, "aq", "az2", 0, H)
 
     def early(t, part):
         if part == 0:
@@ -342,30 +374,32 @@ def rank_program(g, core, T, topo):
                 mm(bank, "up", "ups", 256 * (1 - hs[t]), "tq%d" % t, "ts%d" % t, 0, H)
         if part == 1:
             tr(A("xt", 0, H), P(6, 0, H))
-            for c in range(3):
+            for c in range(2):
                 act(A("sg", C * (17 + c), C * (17 + c) + H), P(7, 0, H), AF.Sign, -1.0, A("xt", 32 * c, 32 * c + 1))
-            for c in range(3):
+            for c in range(2):
                 f0, n = C * (17 + c), 32 * c + 32
                 act(A("sg", f0, f0 + n), A("sg", f0, f0 + n), AF.Relu, None, None, A("ac", 60 + c, 61 + c))
                 act(A("sg", f0 + n, f0 + H), A("sg", f0 + n, f0 + H), AF.Relu, -1.0, None, A("ac", c, c + 1))
         if part == 2:
             f0 = C * 18
             tt(A("eqf", 0, H), P(6, 0, H), A("xt", 0, H), ALU.is_equal)
-            ts(A("fl", f0, f0 + 128), P(6, 0, 128), A("xt", 96, 97), ALU.is_ge, 0.5, sub)
-            ts(A("fl", f0 + 128, f0 + H), P(6, 128, H), A("xt", 96, 97), ALU.is_gt, 0.5, sub)
-            ts(A("fl", f0 + H, f0 + C), P(6, 0, H), A("xt", 128, 129), ALU.is_ge, 0.5, sub)
+            for c in (2, 3, 4):
+                f1, n = f0 + H * (c - 2), 32 * c + 32
+                ts(A("fl", f1, f1 + n), P(6, 0, n), A("xt", 32 * c, 32 * c + 1), ALU.is_ge, 0.5, sub)
+                if n < H:
+                    ts(A("fl", f1 + n, f1 + H), P(6, n, H), A("xt", 32 * c, 32 * c + 1), ALU.is_gt, 0.5, sub)
+        if part == 3:
             scan(A("eqs", 0, H), A("eqm", 0, H), A("eqf", 0, H), mul)
-            for c in (3, 4):
-                f1 = f0 + H * (c - 3)
+            for c in (2, 3, 4):
+                f1 = C * 18 + H * (c - 2)
                 scan(A("so", 160 * c + 80, 160 * c + 160), A("fl", f1, f1 + 80), A("fl", f1 + 80, f1 + H), add)
 
     quant(A("tq0", 0, H), A("ts0", 0, H), A("x0", 0, 640))
-    send_t(0, 0)
     early(0, 0)
-    table_constants()
-    quant(A("tq0", H, C), A("ts0", H, C), A("x0", 640, 1280))
-    send_t(0, 1)
+    pick_u(hs[0])
     early(0, 1)
+    quant(A("tq0", H, C), A("ts0", H, C), A("x0", 640, 1280))
+    table_constants()
     early(0, 2)
     for t in range(R):
         h = hs[t]
@@ -401,10 +435,11 @@ def rank_program(g, core, T, topo):
                 act(A("sg", f0, f0 + C), P(4 + k), AF.Sign, -1.0, thr)
 
                 def second():
-                    act(A("sg", f0, f0 + n), A("sg", f0, f0 + n), AF.Relu, None, None, A("ac", 60 + slot, 61 + slot))
-                    act(A("sg", f0 + n, f0 + C), A("sg", f0 + n, f0 + C), AF.Relu, -1.0, None, A("ac", slot, slot + 1))
+                    less, more = (("ac", 60 + slot), ("ac", slot)) if k < 3 else (("pb", 17 + 3 * c), ("pb", 18 + 3 * c))
+                    act(A("sg", f0, f0 + n), A("sg", f0, f0 + n), AF.Relu, None, None, A(*less, less[1] + 1))
+                    act(A("sg", f0 + n, f0 + C), A("sg", f0 + n, f0 + C), AF.Relu, -1.0, None, A(*more, more[1] + 1))
                 pend[q].append(second)
-            flush(q, 1)
+            flush(q, 2)
 
         def units(q, k):
             return [(q, k, c) for c in (range(NS[k]) if q == "s" else range(NS[k], 10))]
@@ -446,14 +481,13 @@ def rank_program(g, core, T, topo):
                 unit(*u)
                 if between:
                     between.pop(0)()
-            for f in between:
-                f()
             tie_sums(k)
 
-        for bank in (0, 4, 1, 5, 2, 6, 3, 7):
+        for bank in (0, 4, 2, 1, 5, 6, 3, 7):
             k = bank % 4
             mm(bank, "up", "ups", 128 * (2 * (h if k % 2 else 1 - h) + k // 2), tq, tsc)
         tr(A("xt", H, C), P(0, H, C))
+        early(t, 3)
         for c in range(5):
             act(A("sg", C * c, C * c + H), P(4, H, C), AF.Sign, -1.0, A("xt", 32 * c, 32 * c + 1))
         for c in range(5):
@@ -464,15 +498,15 @@ def rank_program(g, core, T, topo):
             cp(A(th, 0, 10), A("xt", 2 * C, 3 * C, 32))
             send(dst, A(th, 16, 26), A(th, 0, 10), "at%d" % t)
 
-        self_count(0, [lambda: thresholds(1), lambda: ties(0), lambda: thresholds(2), lambda: None, first_write])
+        self_count(0, [lambda: thresholds(2), lambda: (first_write(), thresholds(1), ties(0))])
         run_units(units("s", 1))
         flush("s")
         mine = units("v", 1)
         ties(1)
-        differences(0, 3)
+        differences(0, 2)
         tt(A("ce", 0, 5), A("ce", 0, 5), A("ac", 50, 55), add)
         unit(*mine[0])
-        places(0, rw, 52, 3)
+        places(0, rw, 52, 2)
         send(dst, A(rw, 12 * h, 12 * h + 12), A(rw, 52, 64), "ar%d" % t, A(rw, 12 - 12 * h, 24 - 12 * h))
         iota(A("sc2"), [[0, 640]])
         if t == 0:
@@ -481,8 +515,7 @@ def rank_program(g, core, T, topo):
         tie_sums(1)
         thresholds(3)
         if t == 0:
-            ts(A("cl", 0, 2), A("ci", 0, 2), 703.0, mn)
-            ts(A("cl", 2, 6), A("ci", 2, 6), 351.0, mn)
+            cp(A("cl", 4, 6), A("ci", 4, 6))
         run_units(units("s", 2))
         flush("s")
         self_count(2, [lambda: differences(1), lambda: places(1, rw, 12 * h)])
@@ -495,7 +528,6 @@ def rank_program(g, core, T, topo):
             if rest:
                 unit(*rest.pop(0))
 
-        run_units(srest[:2])
         ties(3)
         differences(2)
         unit(*units("v", 4)[0])
@@ -511,12 +543,17 @@ def rank_program(g, core, T, topo):
         fillers = [(lambda k: lambda: ts(A("ii", 10 * k, 10 * k + 10), A(rw, 12 * k, 12 * k + 10), 0.5, mul, 0.25, sub))(k) for k in range(2)]
         fillers += [(lambda k: lambda: ts(A("s2", 24 - 16 * k, 320, 32), A("ii", 10 * k, 10 * k + 10), 240.0, sub))(k) for k in range(2)]
         fillers += [lambda: tr(A("xc", 18, 338), A("wa")), lambda: tr(A("pr"), A("s2")), lambda: ts(A("az"), ind(A("xc"), L("turn")), base_, add)]
+        if t == 0:
+            fillers = [(lambda b: lambda: quant(A("eq", 128 * b, 128 * b + 128), A("es", 128 * b, 128 * b + 128), A("et", 512 * b, 512 * b + 512)))(b)
+                       for b in range(4)] + fillers
+            for k in (1, 3):
+                fillers.insert(k, lambda: None)
 
         def filler():
             if fillers:
                 fillers.pop(0)()
 
-        run_units(srest[2:3])
+        run_units(srest[:3])
         cp(A("zl"), ind(A(rw), L("zm")))
         for k in range(2):
             ts(A("xl", k, 20, 2), A(rw, 12 * k, 12 * k + 10), K(11 + k), add)
@@ -534,12 +571,8 @@ def rank_program(g, core, T, topo):
         up, down = (slice(0, 112), slice(16, 128)), (slice(16, 128), slice(0, 112))
         for c0, s0, way, sem in ((64, 0, (up, down)[h], "d3%d" % t), (96, 32, (down, up)[h], "d4%d" % t)):
             dma("y", A(ml, c0, c0 + 22, rows=way[0]), A(ml, s0, s0 + 22, rows=way[1]), sem)
-            if s0 == 0:
-                if t:
-                    send_t(t, 0)
-                    send_t(t, 1)
-                else:
-                    late_constants()
+            if s0 == 0 and t == 0:
+                late_constants()
         flush("v")
         for e in range(2):
             tr(A("oa", 1 - e, 320, 2), A("xd", 16 + 192 * e, 176 + 192 * e))
@@ -556,59 +589,59 @@ def rank_program(g, core, T, topo):
             tr(A("x1", 160 * k, 160 * k + 160), A("pf", 805 * k + 9, 805 * k + 805, 5))
             tr(A("x2", 160 * k, 160 * k + 160), A("pf", 805 * k + 4, 805 * k + 800, 5))
         flush("v")
-        filler()
-        filler()
-        scan(A("cu", 32, 352), A("x1"), A("x2"), add, sub)
-        n4, far = NS[4], (sub, add)[h]
+        n3, n4, far = NS[3], NS[4], (sub, add)[h]
         tt(A("rb", 1 - h, 2 * n4, 2), A(th, 48, 48 + n4), A("ac", 40, 40 + n4), far)
         tt(A("rb", 1 - h + 2 * n4, 20, 2), A(th, 48 + n4, 58), ends(4, n4, 10), far)
+        for k in range(2):
+            scan(A("cu", 32 + 192 * k, 192 + 192 * k), A("x1", H * k, H * k + H), A("x2", H * k, H * k + H), add, sub)
         while len(rest) > 2:
             gap()
-        tt(A("pb", 0, 10), A("cu", 63, 352, 32), A("cu", 31, 320, 32), sub)
-        cp(A("bl", 1 - h, 20, 2), A("rb", 1 - h, 20, 2))
         unit("v", 3, 8, A("ce", 38, 39))
-        tt(A("ce", 30, 40), A("ce", 30, 40), A("pb", 0, 10), (add, sub)[h])
-        differences(3)
+        for k in range(2):
+            tt(A("pb", 5 * k, 5 * k + 5), A("cu", 63 + 192 * k, 192 + 192 * k, 32), A("cu", 31 + 192 * k, 160 + 192 * k, 32), sub)
         last = pend["v"].pop()
         unit("v", 3, 9, A("ce", 39, 40))
-        n3 = NS[3]
-        last()
+        tt(A("ce", 30 + n3, 40), A("ce", 30 + n3, 40), A("pb", n3, 10), (add, sub)[h])
+        tt(A("pb", 16, 16 + 3 * n3, 3), A("ce", 30, 30 + n3), A("pb", 0, n3), (add, sub)[h])
+        cp(A("bl", 1 - h, 20, 2), A("rb", 1 - h, 20, 2))
+        filler()
+        filler()
         tt(A("rb", h + 2 * n3, 16, 2), ends(3, n3, 8), A("ce", 30 + n3, 38), add)
-        tt(A("rb", h, 2 * n3, 2), A("d1", 30, 30 + n3), A("ce", 30, 30 + n3), add)
+        last()
         flush("v")
+        scan(A("yp", 0, 3 * n3), A("tl", 20, 20 + 3 * n3), A("pb", 16, 16 + 3 * n3), mul)
+        cp(A("bl", h + 2 * n3, 16, 2), A("rb", h + 2 * n3, 16, 2))
         filler()
         filler()
-        cp(A("bl", h, 16, 2), A("rb", h, 16, 2))
         cp(A("bl", h + 16, 20, 2), ends(3, 8, 10))
-        filler()
+        cp(A("bl", h, 2 * n3, 2), A("yp", 2, 3 * n3, 3))
         filler()
         scat(A("sc2"), A("bl"), A("wa"))
         if t == 0:
-            short_lists(3, len(LISTS))
-            fillers = [(lambda b: lambda: quant(A("eq", 128 * b, 128 * b + 128), A("es", 128 * b, 128 * b + 128), A("et", 512 * b, 512 * b + 512)))(b)
-                       for b in range(4)] + fillers
-            filler()
+            short_lists([0, 1, 5, 6])
+            ts(A("cl", 2, 4), A("ci", 2, 4), 351.0, mn)
+            cp(A("cl", 10, 14), A("ci", 10, 14))
         filler()
         for e in range(2):
-            tr(A("xs", C * e, C * e + C), A("sc2", e, 640, 2))
-        filler()
-        for ks, kd in ((0, 0), (1, 1), (2, 2), (3, 3), (5, 6)):
+            tr(B("xs", 10 * e, 10 * e + 10), A("sc2", e, 640, 2))
+        for e in range(2):
+            b0, b1 = 10 * e, 10 * e + 10
             for hh in range(2):
-                tt(A("st", kd + 16 * hh, 640, 32), A("xs", ks, 640, 32), A("xs", 16 + ks, 640, 32), add)
-        filler()
+                for ks, kd, n in ((0, 0, 4), (5, 6, 1)):
+                    tt(B("st", b0, b1, kd + 16 * hh, kd + 16 * hh + n), B("xs", b0, b1, ks, ks + n), B("xs", b0, b1, 16 + ks, 16 + ks + n), add)
         for e in range(2):
-            tr(A("ob", 1 - e, 640, 2), A("st", C * e, C * e + C))
+            tr(A("ob", 1 - e, 640, 2), B("st", 10 * e, 10 * e + 10))
         for b in range(4):
             mm(b, "eq", "es", 128 * b, tq, tsc)
         for b in range(4):
-            mm(4 + b, "eq", "es", 128 * b, lq, ls)
-        for b in range(4):
             cp(A("dw", 480 * b + 160, 480 * b + 480), P(b), "s")
-        filler()
+            cp(A("td", b, 640, 4), P(b, 0, H), "s")
+        if t == 0:
+            short_lists([3, 4, 7, 8])
+        ts(A("mu"), ind(A(ml), L("mm%d" % h)), 160.0, add)
         gather("w0", A("ob"), "bl", 0, "wi")
-        halves = [(lambda b: lambda: act(A("dp", C * b, C * b + C), P(4 + b), AF.Copy, 0.5))(b) for b in range(4)]
-        halves += [(lambda b, e: lambda: cp(A(("bt", "bu")[e], b, 640, 4), ind(A("dp", C * b, C * b + C), A("mu", 12 * e, 12 * e + 10)), "s"))(b, e)
-                   for b in range(4) for e in range(2)]
+        halves = [(lambda b, e: lambda: act(A(("bt", "bu")[e], b, 640, 4), ind(A("dw", 480 * b + 160, 480 * b + 480), A("mu", 12 * e, 12 * e + 10)), AF.Copy, 0.5))(b, e)
+                  for b in range(4) for e in range(2)]
         for s in range(8):
             cur, nxt = "w%d" % (s % 2), "w%d" % (1 - s % 2)
             l0 = 32 * (min(s, 6) % 2)
@@ -625,48 +658,80 @@ def rank_program(g, core, T, topo):
             if s < 7:
                 ts(A("li", l0, l0 + 32), ind(A("xb", 0, 704 if s else 352), L("next" if s else "turn")), base_, add)
             else:
-                cp(A("o2"), ind(A(cur), A("az", 0, 20)), "s")
+                for lo, hi in ((0, CUT), (CUT, C)):
+                    cp(A("o2", lo, hi), ind(A(cur), A("az", lo // 16, hi // 16)), "s")
+            if s < 7 and (t == 0 or s not in (1, 6)):
+                filler()
+            if s == 0 and t == 0:
+                ts(A("cl", 0, 2), A("ci", 0, 2), 703.0, mn)
+            if s == 1:
+                again()
+            if s == 3:
+                for b in range(NT):
+                    cp(A("dz", C * b + H, C * b + C), P(b, 0, H), "s")
             if s == 1 and t == 0:
                 dma("y", u8(A("wq")), T.wc[:], "dwq")
                 dma("y", A("wp"), T.ws[:], "dwp")
                 dma("y", A("vt"), T.v[:], "dv")
                 lin(A("jj", 64, 128), A("jj", 0, 64), 1.0, i4)
-                ts(A("cl", 6, 20), A("ci", 6, 20), 703.0, mn)
+            if s == 3 and t == 0:
+                lin(A("se", 496, 816), A("ti", 496, 816), 0.0, 0.0)
+            if s == 5 and t == 0:
+                ts(A("cl", 6, 10), A("ci", 6, 10), 703.0, mn)
+                cp(A("cl", 14, 16), A("ci", 14, 16))
+            if s == 6 and t == 0:
+                for k in range(2):
+                    lin(A("ci", 24 + 2 * k, 26 + 2 * k), A("ci", 20, 24, 2), 1.0, 320.0 * k)
+                for name, c0, c1 in (("stb", 0, 336), ("se", 0, 176)):
+                    lin(A(name, c0, c1), A("ti", c0, c1), 0.0, 0.0)
+            if s == 7 and t == 0:
+                for c0, c1, top in ((16, 20, 41.0), (24, 26, 383.0), (26, 28, 703.0)):
+                    ts(A("cl", c0, c1), A("ci", c0, c1), top, mn)
+            for k in range((4, 3, 1, 0, 0, 0, 0, 0)[s]):
+                halves.pop(0)()
+            if t == 0 and s in (4, 5):
+                short_lists([9, 10, 11], range(3) if s == 4 else (3, 4))
+            if s == 6:
+                quant(A("bq%d" % t), A("bs%d" % t), A("bt"))
+                send(dst, u8(A(lq)), u8(A("bq%d" % t)), "aq%d" % t)
+                send(dst, A(ls), A("bs%d" % t), "as%d" % t)
             if s == 2:
-                ts(A("mu"), ind(A(ml), L("mm%d" % h)), 160.0, add)
-            if 1 <= s < 7:
-                halves.pop(0)()
-                halves.pop(0)()
-            if s == 7:
                 dma("g", A("bt"), A("bu"), "dacc", None, True)
             gather(nxt, A(cur), "li", l0, "yy" if s else "yz")
-        own("w0", 0)
-        own("w0", 1)
-        tr(A("xc", 16, 336), A("o2"))
-        tt(A("mm", 0, 20), A("xb", 21, 336, 16), A("xc", 22, 336, 16), mn)
-        tt(A("mm", 20, 40), A("xb", 22, 336, 16), A("xc", 21, 336, 16), mn)
-        tt(A("mm", 40, 60), A("mm", 20, 40), A("mm", 0, 20), sub)
-        ts(A("stb", 0, 320, 16), A("mm", 40, 60), -1024.0, mul, 1.0, mx)
-        ts(A("stb", 320, 640, 16), A("mm", 40, 60), 1024.0, mul, 0.0, mn)
-        tr(A("bw", 0, 320), A("stb", 0, 320))
-        tr(A("bw", 336, 656), A("stb", 320, 640))
-        scan(O("wb2"), A("bw", 335, 655), A("bw", 0, 320), add, add, -1.0)
+        for part, (lo, hi) in enumerate(((0, CUT), (CUT, C))):
+            own("w0", part)
+            tr(A("xc", 16 + lo, 16 + hi), A("o2", lo, hi))
+        tt(A("mm", 0, 80, 4), A("xb", 21, 336, 16), A("xc", 22, 336, 16), mn)
+        tt(A("mm", 80, 160, 4), A("xb", 22, 336, 16), A("xc", 21, 336, 16), mn)
+        scan(A("stb", 0, 320, 4), A("mm", 0, 80), A("mm", 80, 160), mx, sub, -BIG)
+        for c0, lane in ((0, 8), (336, 4)):
+            tr(A("bw", c0, c0 + C), A("stb", lane, lane + C))
+        scan(O("wb2"), A("bw", 0, 320), A("bw", 335, 655), add, sub, -1.0)
         own("wb2")
         shifted("wb2")
-        tt(A("yp"), ind(A("xb"), L("own", 2)), A("jj", 64, 128), mn)
-        cp(A("yl"), A("yp"))
+        for c0, name in ((32, "far"), (0, "own")):
+            tt(A("yp", c0, c0 + 32), ind(A("xb"), L(name)), A("jj", 64 + c0, 96 + c0), mn)
+        for c0 in (32, 0):
+            cp(A("yl", c0, c0 + 32), A("yp", c0, c0 + 32))
         scat(A("se", 16, 816), A("yl", 32, 52), A("pr"))
-        gather("wb", A("se", 16, 496), "yl", 0)
-        for part in range(2):
-            own("wb", part, 8)
-            shifted("wb", part, 8)
-        cp(A(sn, 0, 64), ind(A("xb"), L("own", 2)))
-        send(dst, A(sn, 64, 88), A(sn, 32, 56), "an%d" % t)
-        quant(A("bq"), A("bs"), A("bt"))
         for b in range(4):
-            mm(b, "eq", "es", 128 * b, "bq", "bs", 0, H)
+            mm(b, "eq", "es", 128 * b, lq, ls, 0, H)
+        for b in range(4):
+            cp(A("td", b, 640, 4), P(b, 0, H), "s")
         for b in range(4):
             cp(A("dw", 480 * b, 480 * b + 160), P(b, 0, H), "s")
+        gather("wb", A("se", 16, 496), "yl", 0)
+        for lo, hi in ((0, CUT), (CUT, C)):
+            tr(A("xe", 2 * lo, 2 * hi, 2), O("wb", lo, hi))
+            hi += 32 * (lo > 0)
+            tr(A("xe", 2 * lo + 1, 2 * hi, 2), O("wb", lo - 16, hi - 16))
+        for half in range(2):
+            c0 = 48 * half
+            cp(A(sn, c0, c0 + 32), ind(A("xe", 0, (2 * CUT, 704)[half]), A("cl", 24 + 2 * half, 26 + 2 * half)))
+            send(dst, A(sn, c0 + 32, c0 + 42), A(sn, c0, c0 + 10), "a%s%d" % ("nl"[half], t))
+        again()
+        for b in range(NT):
+            cp(A("dz", C * b, C * b + H), P(b, 0, H), "s")
         if t == 0:
             quant(A("vq"), A("vs"), A("vt"))
         if t == R - 1:
@@ -674,35 +739,47 @@ def rank_program(g, core, T, topo):
             tr(A("xb", 343, 535), A("se", 0, 192))
             cp(A("oe", 0, 64), ind(A("xb"), L("own", 2)))
             send(dst, A("oe", 64, 80), A("oe", 0, 16), "ao")
-        ts(A("lu"), ind(A(sn), L("mg%d" % h)), 240.0, add)
+        merge = A("cl", 16 + 2 * h, 17 + 2 * h)
+        ts(A("lu", 0, 16), ind(A(sn, 0, 42), merge), 240.0, add)
         for half in range(2):
             c0, e0 = H * half, 640 * half
             for b in range(4):
-                cp(A("yt", e0 + b, e0 + 640, 4), ind(A("dw", 480 * b, 480 * b + 480), A("lu", 10 * half, 10 * half + 10)), "vs"[b % 2])
+                cp(A("yt", e0 + b, e0 + 640, 4), ind(A("dw", 480 * b, 480 * b + 480), A("lu", 16 * half, 16 * half + 10)), "vs"[b % 2])
+                if half == 0 and b == 2:
+                    ts(A("lu", 16, 32), ind(A(sn, 48, 90), merge), 240.0, add)
             quant(A("zq", c0, c0 + H), A("zs", c0, c0 + H), A("yt", e0, e0 + 640))
         if t == R - 1:
-            ts(A("ou"), ind(A("oe"), L("ol")), 160.0, add)
+            ts(A("mu"), ind(A("oe"), L("ol")), 160.0, add)
+        nq, ns = "tq%d" % (t + 1), "ts%d" % (t + 1)
+
+        def new_state(half):
+            quant(A(nq, H * half, H * half + H), A(ns, H * half, H * half + H), A("xa", 640 * half, 640 * half + 640))
+            if t + 1 == R:
+                dma("y", T.oc[:, 640 * half:640 * half + 640], u8(A(nq, H * half, H * half + H)), "dout")
+
         for half in range(2):
-            c0, e0, nq, ns = H * half, 640 * half, "tq%d" % (t + 1), "ts%d" % (t + 1)
+            c0, e0 = H * half, 640 * half
             for b in range(4):
                 mm(4 + b, "wq", "wp", 128 * b, "zq", "zs", c0, c0 + H)
-            for b in range(4):
+            for b in range(0 if half else NT, 4):
                 mm(b, "eq", "es", 128 * b, "zq", "zs", c0, c0 + H)
             for b in range(4):
-                rl = A("rl", C * b + c0, C * b + c0 + H)
-                act(rl, P(4 + b, 0, H), AF.Relu, 0.03125)
-                tt(A("xa", e0 + b, e0 + 640, 4), P(b, 0, H), rl, add)
-            if half and t + 1 < R:
-                early(t + 1, 0)
-                early(t + 1, 1)
-            quant(A(nq, c0, c0 + H), A(ns, c0, c0 + H), A("xa", e0, e0 + 640))
-            if half and t + 1 < R:
-                early(t + 1, 2)
-            if t + 1 == R:
-                dma("y", T.oc[:, 4 * c0:4 * c0 + 640], u8(A(nq, c0, c0 + H)), "dout")
-                if half == 0:
-                    cp(A("er"), ind(A("j1"), A("ou", 0, 10)), "s")
-                    dma("y", T.ol[:], A("er", rows=slice(0, 128, 16)), "dout")
+                act(A("rl", C * b + c0, C * b + c0 + H), P(4 + b, 0, H), AF.Relu, 0.03125)
+            for b in range(4):
+                if half and b == 0:
+                    new_state(0)
+                    if t + 1 < R:
+                        early(t + 1, 0)
+                    else:
+                        cp(A("er"), ind(A("j1"), A("mu", 0, 10)), "s")
+                        dma("y", T.ol[:], A("er", rows=slice(0, 128, 16)), "dout")
+                d = P(b, 0, H) if half or b >= NT else ind(A("dz", C * b, C * b + C), A("lu", 0, 10))
+                tt(A("xa", e0 + b, e0 + 640, 4), d, A("rl", C * b + c0, C * b + c0 + H), add)
+        if t + 1 < R:
+            early(t + 1, 1)
+        new_state(1)
+        if t + 1 < R:
+            early(t + 1, 2)
 
     for half in range(2):
         mm(4 + half, "vq", "vs", 0, "tq3", "ts3", H * half, H * half + H)
@@ -710,5 +787,5 @@ def rank_program(g, core, T, topo):
         dma("sy"[half], T.y[:, H * half:H * half + H], A("ysb", H * half, H * half + H), "dout")
     for k in range(4):
         dma("s", T.osc[4 * k:4 * k + 4, :], A("ts3", rows=slice(32 * k, 32 * k + 4)), "dout")
-    for s in total:
+    for s in sorted(total, key=lambda s: s == "dout"):
         wait("g", (s, total[s]))

from concourse.mybir import dt, AluOpType as ALU, ActivationFunctionType as AF

C, R = 320, 3
F32, BF, I32, U16, U8, MX, F16 = "float32", "bfloat16", "int32", "uint16", "uint8", "float8_e4m3fn_x4", "float16"
SCRATCH = {"ps": ("psum", [128, 4096], F32)}
for _n, _w, _t in [
    ("x0", 1280, BF), ("xa", 1280, BF), ("ut", 512, BF), ("vt", 512, BF), ("uq", 128, MX), ("us", 128, U8), ("up", 512, MX), ("ups", 512, U8),
    ("vq", 128, MX), ("vs", 128, U8), ("wq", 512, MX), ("wp", 512, U8), ("one", 528, BF), ("e0", 528, BF), ("et", 2048, BF), ("eq", 512, MX), ("es", 512, U8),
    ("zq", 320, MX), ("zs", 320, U8), ("bt", 640, BF), ("bu", 640, BF), ("yt", 1280, BF), ("dw", 1920, BF),
    ("dz", 1280, BF), ("td", 640, BF), ("aq", 160, MX), ("az2", 160, U8), ("xe", 704, BF),
    ("rl", 1280, F32), ("ysb", 320, F32), ("er", 160, F32),
    ("xt", 1280, F32), ("fl", 6400, BF), ("sg", 6400, BF), ("so", 8000, F16), ("ac", 120, F32), ("eqf", 1280, BF), ("eqs", 1280, BF), ("eqm", 320, BF),
    ("cf", 3200, BF), ("pf", 1616, F16), ("x1", 320, F16), ("x2", 320, F16), ("cu", 384, F16),
    ("ck", 60, F32), ("ce", 40, F32), ("d1", 40, F32), ("pb", 40, F32), ("rb", 20, F32), ("ii", 20, I32),
    ("zl", 32, U16), ("xl", 20, U16), ("bl", 20, U16), ("az", 32, U16), ("mu", 32, U16), ("li", 64, U16), ("yl", 64, U16), ("lu", 32, U16),
    ("sa", 320, BF), ("sb", 320, BF), ("j1", 320, F32), ("sc1", 320, BF), ("xd", 384, BF), ("oa", 704, BF), ("wa", 320, BF), ("wi", 320, BF),
    ("s2", 320, BF), ("pr", 320, BF), ("sc2", 640, BF), ("ob", 640, BF), ("w0", 1056, BF), ("w1", 1056, BF),
    ("yy", 320, BF), ("yz", 320, BF), ("o2", 320, BF), ("xb", 704, BF), ("xc", 352, BF), ("mm", 160, F32), ("stb", 336, BF), ("bw", 656, BF),
    ("wb", 352, BF), ("wb2", 352, BF), ("jj", 128, F32), ("yp", 64, F32), ("se", 816, BF), ("oe", 96, BF),
    ("ti", 1920, BF), ("pi", 40, I32), ("ul", 32, U16), ("cc", 64, F32), ("ci", 28, F32), ("cl", 28, U16),
    ("tl", 40, F32),
]:
    SCRATCH[_n] = ("sbuf", [128, _w], _t)
for _n in ("xs", "st"):
    SCRATCH[_n] = ("sbuf", [128, 20, 32], BF)
for _t in range(R + 1):
    SCRATCH["tq%d" % _t] = ("sbuf", [128, C], MX)
    SCRATCH["ts%d" % _t] = ("sbuf", [128, C], U8)
for _t in range(R):
    for _n in ("lq", "bq"):
        SCRATCH["%s%d" % (_n, _t)] = ("sbuf", [128, C // 2], MX)
    for _n in ("ls", "bs"):
        SCRATCH["%s%d" % (_n, _t)] = ("sbuf", [128, C // 2], U8)
    SCRATCH["th%d" % _t] = ("sbuf", [128, 64], F32)
    SCRATCH["rw%d" % _t] = ("sbuf", [128, 64], F32)
    SCRATCH["ml%d" % _t] = ("sbuf", [128, 128], BF)
    SCRATCH["sn%d" % _t] = ("sbuf", [128, 96], BF)
SEMAPHORES = (["cv", "cs", "cp", "cg", "dx", "dx2", "du", "dv", "dwq", "dwp", "dsa", "dyz", "det", "dout", "sent", "dacc", "ao", "dm", "ds2"]
              + ["%s%d" % (k, t) for k in ("aq", "as", "an", "al", "at", "ar", "ac", "am", "d1", "d2", "d3", "d4") for t in range(R)])

NS = (5, 5, 5, 5, 7)
BIG = 1.0e8
BACK = 300
NT = 2


def rank_program(g, core, T, topo):
    rank = T.rank_of(core)
    if rank is None:
        return
    Q = {"v": g.vector, "s": g.scalar, "p": g.tensor, "g": g, "y": g.sync}
    total = {}
    seen = {q: {} for q in Q}
    log = {}
    knew, size = {}, {}

    def A(name, lo=0, hi=None, step=1, rows=None):
        hi = SCRATCH[name][1][1] if hi is None else hi
        cols = slice(lo, hi) if step == 1 else slice(lo, hi, step)
        ap = T[name][(slice(None) if rows is None else rows), cols]
        if name == "ps":
            m = ((1 << ((hi - 1) // 512 + 1)) - 1) ^ ((1 << (lo // 512)) - 1)
        elif step == 1:
            m = ((1 << hi) - 1) ^ ((1 << lo) - 1)
        else:
            m = sum(1 << c for c in range(lo, hi, step))
        return (ap, [(name, m)])

    def B(name, b0=0, b1=20, c0=0, c1=32):
        return (T[name][:, b0:b1, c0:c1], [(name, sum(1 << (32 * b + c) for b in range(b0, b1) for c in range(c0, c1)))])

    def ind(win, off, word=False):
        ap = win[0].bitcast(dt.uint32) if word else win[0]
        return (ap.indirect(off[0]), win[1] + off[1])

    def wait(q, tok):
        s, n = tok
        if seen[q].get(s, 0) < n:
            if s == "c" + q:
                k, gone = total[s], 0
                while k > n and gone < BACK:
                    gone += size[(s, k)]
                    k -= 1
                n = k
            Q[q].wait_ge(T.sem[s], n)
            seen[q][s] = n
            for s2, n2 in knew.get((s, n), {}).items():
                seen[q][s2] = max(seen[q].get(s2, 0), n2)

    def order(q, reads, writes):
        need = {}
        for regs, w in ((reads, False), (writes, True)):
            for name, m in regs:
                for e in log.get(name, []):
                    if e[0] & m and (w or e[2] or (name == "ps" and e[3] != q)) and not (q == "p" and e[3] == "p"):
                        need[e[1][0]] = max(need.get(e[1][0], 0), e[1][1])
        for s in sorted(need, key=lambda s: s == "c" + q):
            wait(q, (s, need[s]))

    def note(q, tok, reads, writes):
        for name, m in writes:
            log[name] = [[e[0] & ~m] + e[1:] for e in log.get(name, []) if e[0] & ~m] + [[m, tok, True, q]]
        for name, m in reads:
            log[name] = [e for e in log.get(name, []) if e[2] or e[3] != q or e[1][0] != tok[0] or e[0] & ~m] + [[m, tok, False, q]]

    def op(q, fn, outs, ins, lists=()):
        reads = [r for a in ins if isinstance(a, tuple) for r in a[1]] + list(lists)
        writes = [r for a in outs for r in a[1] if r not in lists]
        order(q, reads, writes)
        s = "c" + q
        if q == "g":
            wait(q, (s, total.get(s, 0)))
        total[s] = total.get(s, 0) + 1
        fn().then_inc(T.sem[s], 1)
        knew[(s, total[s])] = dict(seen[q])
        narrow = q == "v" and all(SCRATCH[n][2] in (BF, F16) or bin(m).count("1") < 2 and n != "ps" for n, m in writes + reads)
        size[(s, total[s])] = max(64, bin(writes[0][1]).count("1") // (2 if narrow else 1))
        note(q, (s, total[s]), reads, writes)

    def x(a):
        return a[0] if isinstance(a, tuple) else a

    def dma(q, out, in_, sem, last=None, adds=False):
        reads = in_[1] if isinstance(in_, tuple) else []
        writes = out[1] if isinstance(out, tuple) else []
        keep = {n: log.get(n, []) for n, m in writes}
        for n, m in writes:
            log[n] = [e for e in log.get(n, []) if e[1][0] != sem or adds]
        order(q, reads, writes)
        for n in keep:
            log[n] = keep[n]
        total[sem] = total.get(sem, 0) + 16
        if adds:
            Q[q].dma_start(x(out), x(in_), accum_op=ALU.add).then_inc(T.sem[sem], 16)
        else:
            Q[q].dma_start(x(out), x(in_)).then_inc(T.sem[sem], 16)
        note(q, (sem, last or total[sem]), reads, writes)

    def send(dst, out, in_, sem, here=None, parts=1):
        here = here or out
        order("g", in_[1], [])
        rid, pid = topo.addr(dst)[0:2]
        g.remote_dma(out[0], in_[0], T.sem[sem], T.sem["sent"], pid, rid, topo.mask(core, dst))
        total["sent"] = total.get("sent", 0) + len(topo.engines(core, dst))
        total[sem] = parts * len(topo.engines(dst, core))
        note("r", (sem, total[sem]), [], here[1])

    def u8(a):
        return (a[0].bitcast(dt.uint8), a[1])

    def cp(out, in_, q="v"):
        if q == "v":
            op("v", lambda: g.vector.tensor_copy(out[0], in_[0]), [out], [in_])
        else:
            act(out, in_, AF.Copy)

    def scat(win, off, in_):
        o = ind(win, off)
        op("v", lambda: g.vector.tensor_copy(o[0], in_[0]), [o], [in_], lists=off[1])

    def tt(out, a, b, o):
        op("v", lambda: g.vector.tensor_tensor(out[0], a[0], b[0], o), [out], [a, b])

    def ts(out, a, s1, o0, s2=None, o1=None):
        if o1 is None:
            op("v", lambda: g.vector.tensor_scalar(out[0], a[0], x(s1), None, o0), [out], [a, s1])
        else:
            op("v", lambda: g.vector.tensor_scalar(out[0], a[0], x(s1), x(s2), o0, o1), [out], [a, s1, s2])

    def scan(out, d0, d1, o0, o1=ALU.add, first=0.0):
        op("v", lambda: g.vector.tensor_tensor_scan(out[0], d0[0], d1[0], x(first), o0, o1), [out], [d0, d1, first])

    def tr(out, in_):
        op("v", lambda: g.vector.transpose(out[0], in_[0]), [out], [in_])

    def fill(out, v):
        op("v", lambda: g.vector.memset(out[0], v), [out], [])

    def act(out, in_, f, scale=None, bias=None, acc=None):
        k = {}
        if scale is not None:
            k["scale"] = x(scale)
        if bias is not None:
            k["bias"] = x(bias)
        if acc is not None:
            k["accum_out"] = acc[0]
        op("s", lambda: g.scalar.activation(out[0], in_[0], f, **k), [out] + ([acc] if acc else []), [in_, scale, bias])

    def lin(out, in_, scale, bias):
        act(out, in_, AF.Identity, scale, bias)

    def iota(out, pat, base=0, cm=0, flt=True):
        if flt:
            op("g", lambda: g.iota(out[0], pat, base, cm, allow_small_or_imprecise_dtypes=True), [out], [])
        else:
            op("g", lambda: g.iota(out[0], pat, base, cm), [out], [])

    def zero(*regions):
        for a in regions:
            iota(a, [[0, bin(a[1][0][1]).count("1")]])

    def sel(out, in_, pat, o, base, cm):
        op("g", lambda: g.affine_select(out[0], in_[0], pat, o, 0.0, base, cm), [out], [in_])

    def quant(q, s, in_):
        op("v", lambda: g.vector.quantize_mx(q[0], s[0], in_[0]), [q, s], [in_])

    def mm(bank, wq, ws, c0, xq, xs, lo=0, hi=C):
        out, a, b, c, d = A("ps", 512 * bank, 512 * bank + hi - lo), A(wq, c0, c0 + 128), A(ws, c0, c0 + 128), A(xq, lo, hi), A(xs, lo, hi)
        op("p", lambda: g.tensor.matmul_mx(out[0], a[0], b[0], c[0], d[0], True, True), [out], [a, b, c, d])

    def P(bank, lo=0, hi=C):
        return A("ps", 512 * bank + lo, 512 * bank + hi)

    def K(i, j=None):
        return A("cc", i, (i if j is None else j - 1) + 1)

    add, sub, mul, mn, mx = ALU.add, ALU.subtract, ALU.mult, ALU.min, ALU.max
    band, shr = ALU.bitwise_and, ALU.arith_shift_right
    parts = [rank ^ (1 << t) for t in range(R)]
    hs = [1 if rank > p else 0 for p in parts]
    H, CUT = C // 2, 192

    LISTS = [("next", 32, ((16, 369), (384, 33))), ("turn", 32, ((18, 19), (34, 35))), ("zm", 1, ((0, 40), (24, 12))),
             ("own", 32, ((16, 368), (384, 32))), ("far", 32, ((32, 352), (400, 16))), ("mm0", 2, ((0, 96), (64, 32))), ("mm1", 2, ((33, 65), (97, 1))),
             ("ol", 2, (((32, 64), (33, 65)), ((64, 32), (65, 33)))[hs[R - 1]]), ("mg0", 2, ((16, 32), (17, 33))), ("mg1", 2, ((32, 16), (33, 17))),
             ("far2", 64, ((48, 17), (113, 16))), ("own2", 64, ((16, 49), (81, 48)))]

    def L(name, k=1):
        i = [e[0] for e in LISTS].index(name)
        return A("cl", 2 * i, 2 * i + 2 * k)

    def pick_u(hh):
        o_, l_ = A("up", 256 * hh, 256 * hh + 256), A("ul", 16 * hh, 16 * hh + 16)
        i_ = ind(A("uq"), l_, True)
        op("v", lambda: g.vector.tensor_copy(o_[0].bitcast(dt.uint32), i_[0]), [o_], [i_])
        cp(A("ups", 256 * hh, 256 * hh + 256), ind(A("us"), l_), "s")

    dma("s", A("ut"), T.u[:], "du")
    dma("y", A("x0", 0, 640), T.x[:, 0:640], "dx")
    dma("y", A("x0", 640, 1280), T.x[:, 640:1280], "dx2")
    iota(A("j1"), [[1, 320]])
    iota(A("pi", 0, 1), [[0, 1]], 0, 1, False)
    iota(A("tl", 0, 20), [[32, 10], [320, 2]])
    iota(A("pi", 8, 40), [[8, 4], [32, 4], [0, 2]], 0, 0, False)
    fill(A("one"), 1.0)
    fill(A("ck", 0, 40), 160.0)
    fill(A("ck", 40, 60), 480.0)
    for t in range(R):
        fill(A("ml%d" % t), 0.0)
        fill(A("rw%d" % t, 24, 64), 0.0)
        fill(A("rw%d" % t, 12 * hs[t] + 8, 12 * hs[t] + 12), 0.0)
    for c0, c1 in ((0, 16), (176, 208), (368, 384)):
        fill(A("xd", c0, c1), 0.0)
    fill(A("pf", 4, 810, 805), 0.0)
    fill(A("ck", 2, 5), 80.0)
    fill(A("tl", 20, 40), -1.0)
    fill(A("cu", 31, 224, 192), 0.0)
    for c0, n, step, base in ((0, 320, 1, -160), (320, 160, 2, -496), (480, 160, 2, 176), (640, 192, 2, -496), (832, 128, 2, 240), (960, 320, 1, -96)):
        lin(A("ti", c0, c0 + n), A("j1", 0, n), float(step), float(base))
    for k in range(5):
        lin(A("ti", 1280 + 128 * k, 1408 + 128 * k), A("j1", 0, 128), 2.0 ** (k + 10), 128.0 * 2 ** (k + 10))
    sel(A("eqm", rows=slice(0, 32)), A("one", 0, 320, rows=slice(0, 32)), [[0, 10], [-1, 32]], ALU.not_equal, 0, 1)
    for a in range(1, 4):
        dma("y", A("eqm", rows=slice(32 * a, 32 * a + 32)), A("eqm", rows=slice(0, 32)), "dm", 48)
    p0 = A("pi", 0, 1)
    i4, run, hq, par, p5, both = K(0), K(1), K(2), K(3), K(4), K(5)
    ts(A("pi", 1, 2), p0, 15, band)
    ts(A("pi", 2, 3), p0, 4, shr, 1, band)
    ts(A("pi", 3, 4), p0, 1, shr, 7, band)
    ts(A("pi", 4, 5), p0, 1, band)
    ts(A("pi", 5, 6), p0, 31, band)
    fill(A("tl", 20, 40, 3), 0.0)
    fill(A("yz"), BIG)
    cp(K(0, 5), A("pi", 1, 6))
    fill(B("st"), BIG)
    ts(A("xl"), A("tl", 0, 20), p5, add)
    tt(both, par, run, mul)
    ts(K(6), i4, 5.0, ALU.is_equal)
    ts(K(7), i4, 6.0, ALU.is_equal)
    cp(A("ul"), A("pi", 8, 40))
    cp(A("sa"), ind(A("ti", 0, 640), A("xl")))
    iota(A("s2", rows=slice(0, 32)), [[32, 10], [0, 32]], -160, 1)
    keep_, big_, base_ = K(8), K(9), K(10)

    def short_lists(which, levels=range(5)):
        for level in levels:
            for i in which:
                name, step, b = LISTS[i]
                k0, k1 = K(20 + i), K(40 + i)
                if level == 0:
                    lin(k0, hq, float(step), float(b[0][0]))
                elif level == 4:
                    lin(A("ci", 2 * i, 2 * i + 2), A("j1", 0, 2), 8.0 * step, k1)
                else:
                    src, f = ((par, b[1][0] - b[0][0]), (run, b[0][1] - b[0][0]), (both, b[1][1] - b[1][0] - b[0][1] + b[0][0]))[level - 1]
                    lin(*((k1, src, float(f), k0) if level % 2 else (k0, src, float(f), k1)))

    short_lists([2], [0])
    lin(keep_, K(6), 1.0, K(7))
    lin(base_, run, -64.0, 560.0)
    lin(K(11), run, 320.0, 0.0)
    lin(K(12), run, -384.0, 384.0)
    for k in range(6):
        if k % 4 == 0:
            short_lists([2], [1 + k // 4])
        n = NS[(0, 1, 2, 3, 2, 3)[k]] if k else 2
        lin(A("ck", 10 * k, 10 * k + n), A("j1", 0, n), 32.0, 32.0 + 320 * (k // 4))
    lin(big_, keep_, -BIG, BIG)
    short_lists([2], [3])
    quant(A("uq"), A("us"), A("ut"))
    pick_u(1 - hs[0])
    short_lists([2], [4])
    cp(A("sb"), ind(A("ti", 640, 1280), A("xl")), "s")

    def table_constants():
        low = slice(0, 4)
        for hh in range(2):
            for r_, c0 in ((0, 320 * hh), (1, 640 + 320 * hh), (6, 1280 + 320 * hh)):
                dma("y", A("sa", rows=slice(r_ + 16 * hh, 128, 32)), A("ti", c0, c0 + 320, rows=low), "dsa", 128)
            dma("y", A("yz", rows=slice(5 + 16 * hh, 128, 32)), A("ti", 1280 + 320 * hh, 1600 + 320 * hh, rows=low), "dyz", 32)
        dma("y", A("sa", rows=slice(7, 128, 16)), A("ti", 0, 320, rows=slice(0, 8)), "dsa", 128)
        dma("y", A("sa", rows=slice(3, 128, 16)), A("sb", rows=slice(3, 128, 16)), "dsa", 128)
        for a in range(1, 4):
            dma("y", A("s2", rows=slice(32 * a, 32 * a + 32)), A("s2", rows=slice(0, 32)), "ds2", 48)

    def late_constants():
        zero(A("xb", 0, 16), A("xb", 336, 352))
        for w in ("w0", "w1"):
            zero(A(w, 1, 384, 2), A(w, 384, 400), A(w, 720, 736), A(w, 737, 1056, 2))
        iota(A("jj", 0, 64), [[320, 2], [16, 32]], 160)
        iota(A("se", 176, 496), [[1, 320]], -80)
        zero(A("bw", 320, 336), A("oe", 80, 96), A("mm", 1, 160, 4), A("mm", 82, 160, 4))
        iota(A("mm", 2, 80, 4), [[0, 20]], 1)
        iota(A("mm", 3, 80, 4), [[0, 20]], -16000000)
        iota(A("mm", 83, 160, 4), [[0, 20]], 16000000)
        zero(*[A(w, c, c + 16) for w in ("wb", "wb2") for c in (0, 336)])
        zero(A("xe", 640, 704, 2))

    def O(w, lo=0, hi=C):
        c0 = 400 if w in ("w0", "w1") else 16
        return A(w, c0 + lo, c0 + hi)

    def own(w, part=None):
        lo, hi = {None: (0, C), 0: (0, CUT), 1: (CUT, C)}[part]
        tr(A("xb", 16 + lo, 16 + hi), O(w, lo, hi))

    def shifted(w, part=None):
        lo, hi = {None: (0, 352), 0: (0, CUT), 1: (CUT, 352)}[part]
        tr(A("xb", 352 + lo, 352 + hi), O(w, lo - 16, hi - 16))

    def other(w, part):
        if part:
            tr(A(w, 736, 1056, 2), A("xb", CUT, 352))
        else:
            tr(A(w, 0, 384, 2), A("xb", 0, CUT))

    def gather(w, win, lst, l0, low=None):
        for lo, hi in ((0, CUT), (CUT, C)):
            src = ind(win, A(lst, l0 + lo // 16, l0 + hi // 16))
            if low:
                tt(O(w, lo, hi), src, A(low, lo, hi), mn)
            else:
                cp(O(w, lo, hi), src)

    def again():
        quant(A("aq"), A("az2"), A("td"))
        for b in range(NT):
            mm(b, "eq", "es", 128 * b, "aq", "az2", 0, H)

    def early(t, part):
        if part == 0:
            for bank in (6, 7):
                mm(bank, "up", "ups", 256 * (1 - hs[t]), "tq%d" % t, "ts%d" % t, 0, H)
        if part == 1:
            tr(A("xt", 0, H), P(6, 0, H))
            for c in range(2):
                act(A("sg", C * (17 + c), C * (17 + c) + H), P(7, 0, H), AF.Sign, -1.0, A("xt", 32 * c, 32 * c + 1))
            for c in range(2):
                f0, n = C * (17 + c), 32 * c + 32
                act(A("sg", f0, f0 + n), A("sg", f0, f0 + n), AF.Relu, None, None, A("ac", 60 + c, 61 + c))
                act(A("sg", f0 + n, f0 + H), A("sg", f0 + n, f0 + H), AF.Relu, -1.0, None, A("ac", c, c + 1))
        if part == 2:
            f0 = C * 18
            tt(A("eqf", 0, H), P(6, 0, H), A("xt", 0, H), ALU.is_equal)
            for c in (2, 3, 4):
                f1, n = f0 + H * (c - 2), 32 * c + 32
                ts(A("fl", f1, f1 + n), P(6, 0, n), A("xt", 32 * c, 32 * c + 1), ALU.is_ge, 0.5, sub)
                if n < H:
                    ts(A("fl", f1 + n, f1 + H), P(6, n, H), A("xt", 32 * c, 32 * c + 1), ALU.is_gt, 0.5, sub)
        if part == 3:
            scan(A("eqs", 0, H), A("eqm", 0, H), A("eqf", 0, H), mul)
            for c in (2, 3, 4):
                f1 = C * 18 + H * (c - 2)
                scan(A("so", 160 * c + 80, 160 * c + 160), A("fl", f1, f1 + 80), A("fl", f1 + 80, f1 + H), add)

    quant(A("tq0", 0, H), A("ts0", 0, H), A("x0", 0, 640))
    early(0, 0)
    pick_u(hs[0])
    early(0, 1)
    quant(A("tq0", H, C), A("ts0", H, C), A("x0", 640, 1280))
    table_constants()
    early(0, 2)
    for t in range(R):
        h = hs[t]
        tq, tsc, lq, ls = "tq%d" % t, "ts%d" % t, "lq%d" % t, "ls%d" % t
        th, rw, ml, sn = "th%d" % t, "rw%d" % t, "ml%d" % t, "sn%d" % t
        dst = T.cores[parts[t]]
        pend = {"v": [], "s": []}
        cnt = {"v": 0, "s": 0}

        def flush(q, keep=0):
            while len(pend[q]) > keep:
                pend[q].pop(0)()

        def unit(q, k, c, first=0.0):
            n, slot = 32 * c + 32, 10 * k + c
            thr = A("xt", C * k + 32 * c, C * k + 32 * c + 1) if k < 4 else A(th, 16 + c, 17 + c)
            f0 = C * (cnt[q] % 20)
            cnt[q] += 1
            if k == 4:
                f = A("cf", c, 3200, 10)
                if q == "s":
                    act(f, P(7), AF.Sign, -1.0, thr)
                    pend[q].append(lambda: act(f, f, AF.Relu, 1.0 - 2.0 * h, None, A("ac", slot, slot + 1)))
                else:
                    ts(f, P(3), thr, ALU.is_gt if h else ALU.is_lt)
                    pend[q].append(lambda: scan(A("so", 160 * slot, 160 * slot + 160), A("cf", c, 1600, 10), A("cf", 1600 + c, 3200, 10), add))
            elif q == "v":
                ts(A("fl", f0, f0 + n), P(k, 0, n), thr, ALU.is_ge, 0.5, sub)
                if n < C:
                    ts(A("fl", f0 + n, f0 + C), P(k, n, C), thr, ALU.is_gt, 0.5, sub)
                pend[q].append(lambda: scan(A("so", 160 * slot, 160 * slot + 160), A("fl", f0, f0 + 160), A("fl", f0 + 160, f0 + C), add, add, first))
            else:
                act(A("sg", f0, f0 + C), P(4 + k), AF.Sign, -1.0, thr)

                def second():
                    less, more = (("ac", 60 + slot), ("ac", slot)) if k < 3 else (("pb", 17 + 3 * c), ("pb", 18 + 3 * c))
                    act(A("sg", f0, f0 + n), A("sg", f0, f0 + n), AF.Relu, None, None, A(*less, less[1] + 1))
                    act(A("sg", f0 + n, f0 + C), A("sg", f0 + n, f0 + C), AF.Relu, -1.0, None, A(*more, more[1] + 1))
                pend[q].append(second)
            flush(q, 2)

        def units(q, k):
            return [(q, k, c) for c in (range(NS[k]) if q == "s" else range(NS[k], 10))]

        def run_units(us):
            for u in us:
                unit(*u)

        def thresholds(k):
            tr(A("xt", C * k, C * k + C), P(k))

        def ties(k):
            c0, lo = C * k, 0 if k else H
            tt(A("eqf", c0 + lo, c0 + C), P(k, lo, C), A("xt", c0 + lo, c0 + C), ALU.is_equal)
            flush("v")
            pend["v"].append(lambda: scan(A("eqs", c0 + lo, c0 + C), A("eqm", lo, C), A("eqf", c0 + lo, c0 + C), mul))

        def tie_sums(k):
            k1 = 10 * (k + 2 * h if k > 1 else k)
            tt(A("ce", 10 * k, 10 * k + 10), A("ck", k1, k1 + 10), A("eqs", C * k + 31, C * k + C, 32), sub)

        def ends(k, c0, c1):
            return A("so", 160 * (10 * k + c0) + 159, 160 * (10 * k + c1), 160)

        def differences(k, n=None):
            k0, n = 10 * k, n or NS[k]
            tt(A("d1", k0, k0 + n), A("ac", k0, k0 + n), A("ac", 60 + k0, 60 + k0 + n), sub)

        def places(k, name, c0, n=None):
            k0, n = 10 * k, n or NS[k]
            tt(A(name, c0 + n, c0 + 10), ends(k, n, 10), A("ce", k0 + n, k0 + 10), add)
            tt(A(name, c0, c0 + n), A("d1", k0, k0 + n), A("ce", k0, k0 + n), add)

        def self_count(k, between=()):
            us, between = units("v", k), list(between)
            if k:
                ties(k)
            for u in us:
                unit(*u)
                if between:
                    between.pop(0)()
            tie_sums(k)

        for bank in (0, 4, 2, 1, 5, 6, 3, 7):
            k = bank % 4
            mm(bank, "up", "ups", 128 * (2 * (h if k % 2 else 1 - h) + k // 2), tq, tsc)
        tr(A("xt", H, C), P(0, H, C))
        early(t, 3)
        for c in range(5):
            act(A("sg", C * c, C * c + H), P(4, H, C), AF.Sign, -1.0, A("xt", 32 * c, 32 * c + 1))
        for c in range(5):
            act(A("sg", C * c, C * c + H), A("sg", C * c, C * c + H), AF.Relu, -1.0, None, A("ac", 50 + c, 51 + c))
        cnt["s"] = 5

        def first_write():
            cp(A(th, 0, 10), A("xt", 2 * C, 3 * C, 32))
            send(dst, A(th, 16, 26), A(th, 0, 10), "at%d" % t)

        self_count(0, [lambda: thresholds(2), lambda: (first_write(), thresholds(1), ties(0))])
        run_units(units("s", 1))
        flush("s")
        mine = units("v", 1)
        ties(1)
        differences(0, 2)
        tt(A("ce", 0, 5), A("ce", 0, 5), A("ac", 50, 55), add)
        unit(*mine[0])
        places(0, rw, 52, 2)
        send(dst, A(rw, 12 * h, 12 * h + 12), A(rw, 52, 64), "ar%d" % t, A(rw, 12 - 12 * h, 24 - 12 * h))
        iota(A("sc2"), [[0, 640]])
        if t == 0:
            sel(A("e0"), A("one"), [[-1, 528]], ALU.is_equal, 3, 4)
        run_units(mine[1:])
        tie_sums(1)
        thresholds(3)
        if t == 0:
            cp(A("cl", 4, 6), A("ci", 4, 6))
        run_units(units("s", 2))
        flush("s")
        self_count(2, [lambda: differences(1), lambda: places(1, rw, 12 * h)])
        dma("y", A(rw, 24, 34, rows=slice(0, 112)), A(rw, 0, 10, rows=slice(16, 128)), "d1%d" % t)
        dma("y", A(rw, 40, 50, rows=slice(16, 128)), A(rw, 12, 22, rows=slice(0, 112)), "d2%d" % t)
        rest = units("v", 3)
        srest = units("s", 3)

        def gap():
            if rest:
                unit(*rest.pop(0))

        ties(3)
        differences(2)
        unit(*units("v", 4)[0])
        places(2, th, 32)
        send(dst, A(th, 48, 58), A(th, 32, 42), "ac%d" % t)
        if t == 0:
            zero(A("xc", 0, 18), A("xc", 336, 352))
            for b in range(4):
                dma("y", A("et", 512 * b, 512 * b + 512), A("e0", 3 - b, 515 - b), "det", 64)
        run_units(units("s", 4))
        flush("s")
        run_units(units("v", 4)[1:])
        fillers = [(lambda k: lambda: ts(A("ii", 10 * k, 10 * k + 10), A(rw, 12 * k, 12 * k + 10), 0.5, mul, 0.25, sub))(k) for k in range(2)]
        fillers += [(lambda k: lambda: ts(A("s2", 24 - 16 * k, 320, 32), A("ii", 10 * k, 10 * k + 10), 240.0, sub))(k) for k in range(2)]
        fillers += [lambda: tr(A("xc", 18, 338), A("wa")), lambda: tr(A("pr"), A("s2")), lambda: ts(A("az"), ind(A("xc"), L("turn")), base_, add)]
        if t == 0:
            fillers = [(lambda b: lambda: quant(A("eq", 128 * b, 128 * b + 128), A("es", 128 * b, 128 * b + 128), A("et", 512 * b, 512 * b + 512)))(b)
                       for b in range(4)] + fillers
            for k in (1, 3):
                fillers.insert(k, lambda: None)

        def filler():
            if fillers:
                fillers.pop(0)()

        run_units(srest[:3])
        cp(A("zl"), ind(A(rw), L("zm")))
        for k in range(2):
            ts(A("xl", k, 20, 2), A(rw, 12 * k, 12 * k + 10), K(11 + k), add)
        flush("v")
        scat(A("sc1"), A("zl", 0, 20), A("sa"))
        tie_sums(3)
        for e in range(2):
            tr(A("xd", 16 + 192 * e, 176 + 192 * e), A("sc1", e, 320, 2))
        gap()
        for e in range(2):
            cp(A("xd", 21 + 192 * e, 176 + 192 * e, 16), A("xd", 214 - 192 * e, 368 - 192 * e, 16))
        cp(A(ml, 0, 22), A("xd", 23, 368, 16))
        gap()
        send(dst, A(ml, 32, 54), A(ml, 0, 22), "am%d" % t)
        up, down = (slice(0, 112), slice(16, 128)), (slice(16, 128), slice(0, 112))
        for c0, s0, way, sem in ((64, 0, (up, down)[h], "d3%d" % t), (96, 32, (down, up)[h], "d4%d" % t)):
            dma("y", A(ml, c0, c0 + 22, rows=way[0]), A(ml, s0, s0 + 22, rows=way[1]), sem)
            if s0 == 0 and t == 0:
                late_constants()
        flush("v")
        for e in range(2):
            tr(A("oa", 1 - e, 320, 2), A("xd", 16 + 192 * e, 176 + 192 * e))
            tr(A("oa", 321 - e, 704, 2), A("xd", 192 * e, 192 + 192 * e))
        flush("s")
        cp(A("wa"), ind(A("oa"), A("xl")), "s")
        run_units(srest[3:])
        flush("s")
        lin(A("wi"), A("wa"), keep_, big_)
        for k in range(2):
            scan(A("pf", 805 * k + 5, 805 * k + 805), A("cf", 1600 * k, 1600 * k + 1600, 2), A("cf", 1600 * k + 1, 1600 * k + 1600, 2), add)
        gap()
        for k in range(2):
            tr(A("x1", 160 * k, 160 * k + 160), A("pf", 805 * k + 9, 805 * k + 805, 5))
            tr(A("x2", 160 * k, 160 * k + 160), A("pf", 805 * k + 4, 805 * k + 800, 5))
        flush("v")
        n3, n4, far = NS[3], NS[4], (sub, add)[h]
        tt(A("rb", 1 - h, 2 * n4, 2), A(th, 48, 48 + n4), A("ac", 40, 40 + n4), far)
        tt(A("rb", 1 - h + 2 * n4, 20, 2), A(th, 48 + n4, 58), ends(4, n4, 10), far)
        for k in range(2):
            scan(A("cu", 32 + 192 * k, 192 + 192 * k), A("x1", H * k, H * k + H), A("x2", H * k, H * k + H), add, sub)
        while len(rest) > 2:
            gap()
        unit("v", 3, 8, A("ce", 38, 39))
        for k in range(2):
            tt(A("pb", 5 * k, 5 * k + 5), A("cu", 63 + 192 * k, 192 + 192 * k, 32), A("cu", 31 + 192 * k, 160 + 192 * k, 32), sub)
        last = pend["v"].pop()
        unit("v", 3, 9, A("ce", 39, 40))
        tt(A("ce", 30 + n3, 40), A("ce", 30 + n3, 40), A("pb", n3, 10), (add, sub)[h])
        tt(A("pb", 16, 16 + 3 * n3, 3), A("ce", 30, 30 + n3), A("pb", 0, n3), (add, sub)[h])
        cp(A("bl", 1 - h, 20, 2), A("rb", 1 - h, 20, 2))
        filler()
        filler()
        tt(A("rb", h + 2 * n3, 16, 2), ends(3, n3, 8), A("ce", 30 + n3, 38), add)
        last()
        flush("v")
        scan(A("yp", 0, 3 * n3), A("tl", 20, 20 + 3 * n3), A("pb", 16, 16 + 3 * n3), mul)
        cp(A("bl", h + 2 * n3, 16, 2), A("rb", h + 2 * n3, 16, 2))
        filler()
        filler()
        cp(A("bl", h + 16, 20, 2), ends(3, 8, 10))
        cp(A("bl", h, 2 * n3, 2), A("yp", 2, 3 * n3, 3))
        filler()
        scat(A("sc2"), A("bl"), A("wa"))
        if t == 0:
            short_lists([0, 1, 5, 6])
            ts(A("cl", 2, 4), A("ci", 2, 4), 351.0, mn)
            cp(A("cl", 10, 14), A("ci", 10, 14))
        filler()
        for e in range(2):
            tr(B("xs", 10 * e, 10 * e + 10), A("sc2", e, 640, 2))
        for e in range(2):
            b0, b1 = 10 * e, 10 * e + 10
            for hh in range(2):
                for ks, kd, n in ((0, 0, 4), (5, 6, 1)):
                    tt(B("st", b0, b1, kd + 16 * hh, kd + 16 * hh + n), B("xs", b0, b1, ks, ks + n), B("xs", b0, b1, 16 + ks, 16 + ks + n), add)
        for e in range(2):
            tr(A("ob", 1 - e, 640, 2), B("st", 10 * e, 10 * e + 10))
        for b in range(4):
            mm(b, "eq", "es", 128 * b, tq, tsc)
        for b in range(4):
            cp(A("dw", 480 * b + 160, 480 * b + 480), P(b), "s")
            cp(A("td", b, 640, 4), P(b, 0, H), "s")
        if t == 0:
            short_lists([3, 4, 7, 8])
        ts(A("mu"), ind(A(ml), L("mm%d" % h)), 160.0, add)
        gather("w0", A("ob"), "bl", 0, "wi")
        halves = [(lambda b, e: lambda: act(A(("bt", "bu")[e], b, 640, 4), ind(A("dw", 480 * b + 160, 480 * b + 480), A("mu", 12 * e, 12 * e + 10)), AF.Copy, 0.5))(b, e)
                  for b in range(4) for e in range(2)]
        for s in range(8):
            cur, nxt = "w%d" % (s % 2), "w%d" % (1 - s % 2)
            l0 = 32 * (min(s, 6) % 2)
            if s:
                lin(A("yy"), O(cur), keep_, big_)
            own(cur, 0)
            if 0 < s < 7:
                shifted(cur, 0)
            own(cur, 1)
            if 0 < s < 7:
                shifted(cur, 1)
            other(cur, 0)
            other(cur, 1)
            if s < 7:
                ts(A("li", l0, l0 + 32), ind(A("xb", 0, 704 if s else 352), L("next" if s else "turn")), base_, add)
            else:
                for lo, hi in ((0, CUT), (CUT, C)):
                    cp(A("o2", lo, hi), ind(A(cur), A("az", lo // 16, hi // 16)), "s")
            if s < 7 and (t == 0 or s not in (1, 6)):
                filler()
            if s == 0 and t == 0:
                ts(A("cl", 0, 2), A("ci", 0, 2), 703.0, mn)
            if s == 1:
                again()
            if s == 3:
                for b in range(NT):
                    cp(A("dz", C * b + H, C * b + C), P(b, 0, H), "s")
            if s == 1 and t == 0:
                dma("y", u8(A("wq")), T.wc[:], "dwq")
                dma("y", A("wp"), T.ws[:], "dwp")
                dma("y", A("vt"), T.v[:], "dv")
                lin(A("jj", 64, 128), A("jj", 0, 64), 1.0, i4)
            if s == 3 and t == 0:
                lin(A("se", 496, 816), A("ti", 496, 816), 0.0, 0.0)
            if s == 5 and t == 0:
                ts(A("cl", 6, 10), A("ci", 6, 10), 703.0, mn)
                cp(A("cl", 14, 16), A("ci", 14, 16))
            if s == 6 and t == 0:
                for k in range(2):
                    lin(A("ci", 24 + 2 * k, 26 + 2 * k), A("ci", 20, 24, 2), 1.0, 320.0 * k)
                for name, c0, c1 in (("stb", 0, 336), ("se", 0, 176)):
                    lin(A(name, c0, c1), A("ti", c0, c1), 0.0, 0.0)
            if s == 7 and t == 0:
                for c0, c1, top in ((16, 20, 41.0), (24, 26, 383.0), (26, 28, 703.0)):
                    ts(A("cl", c0, c1), A("ci", c0, c1), top, mn)
            for k in range((4, 3, 1, 0, 0, 0, 0, 0)[s]):
                halves.pop(0)()
            if t == 0 and s in (4, 5):
                short_lists([9, 10, 11], range(3) if s == 4 else (3, 4))
            if s == 6:
                quant(A("bq%d" % t), A("bs%d" % t), A("bt"))
                send(dst, u8(A(lq)), u8(A("bq%d" % t)), "aq%d" % t)
                send(dst, A(ls), A("bs%d" % t), "as%d" % t)
            if s == 2:
                dma("g", A("bt"), A("bu"), "dacc", None, True)
            gather(nxt, A(cur), "li", l0, "yy" if s else "yz")
        for part, (lo, hi) in enumerate(((0, CUT), (CUT, C))):
            own("w0", part)
            tr(A("xc", 16 + lo, 16 + hi), A("o2", lo, hi))
        tt(A("mm", 0, 80, 4), A("xb", 21, 336, 16), A("xc", 22, 336, 16), mn)
        tt(A("mm", 80, 160, 4), A("xb", 22, 336, 16), A("xc", 21, 336, 16), mn)
        scan(A("stb", 0, 320, 4), A("mm", 0, 80), A("mm", 80, 160), mx, sub, -BIG)
        for c0, lane in ((0, 8), (336, 4)):
            tr(A("bw", c0, c0 + C), A("stb", lane, lane + C))
        scan(O("wb2"), A("bw", 0, 320), A("bw", 335, 655), add, sub, -1.0)
        own("wb2")
        shifted("wb2")
        for c0, name in ((32, "far"), (0, "own")):
            tt(A("yp", c0, c0 + 32), ind(A("xb"), L(name)), A("jj", 64 + c0, 96 + c0), mn)
        for c0 in (32, 0):
            cp(A("yl", c0, c0 + 32), A("yp", c0, c0 + 32))
        scat(A("se", 16, 816), A("yl", 32, 52), A("pr"))
        for b in range(4):
            mm(b, "eq", "es", 128 * b, lq, ls, 0, H)
        for b in range(4):
            cp(A("td", b, 640, 4), P(b, 0, H), "s")
        for b in range(4):
            cp(A("dw", 480 * b, 480 * b + 160), P(b, 0, H), "s")
        gather("wb", A("se", 16, 496), "yl", 0)
        for lo, hi in ((0, CUT), (CUT, C)):
            tr(A("xe", 2 * lo, 2 * hi, 2), O("wb", lo, hi))
            hi += 32 * (lo > 0)
            tr(A("xe", 2 * lo + 1, 2 * hi, 2), O("wb", lo - 16, hi - 16))
        for half in range(2):
            c0 = 48 * half
            cp(A(sn, c0, c0 + 32), ind(A("xe", 0, (2 * CUT, 704)[half]), A("cl", 24 + 2 * half, 26 + 2 * half)))
            send(dst, A(sn, c0 + 32, c0 + 42), A(sn, c0, c0 + 10), "a%s%d" % ("nl"[half], t))
        again()
        for b in range(NT):
            cp(A("dz", C * b, C * b + H), P(b, 0, H), "s")
        if t == 0:
            quant(A("vq"), A("vs"), A("vt"))
        if t == R - 1:
            tr(A("xb", 7, 167), A("se", 16, 176))
            tr(A("xb", 343, 535), A("se", 0, 192))
            cp(A("oe", 0, 64), ind(A("xb"), L("own", 2)))
            send(dst, A("oe", 64, 80), A("oe", 0, 16), "ao")
        merge = A("cl", 16 + 2 * h, 17 + 2 * h)
        ts(A("lu", 0, 16), ind(A(sn, 0, 42), merge), 240.0, add)
        for half in range(2):
            c0, e0 = H * half, 640 * half
            for b in range(4):
                cp(A("yt", e0 + b, e0 + 640, 4), ind(A("dw", 480 * b, 480 * b + 480), A("lu", 16 * half, 16 * half + 10)), "vs"[b % 2])
                if half == 0 and b == 2:
                    ts(A("lu", 16, 32), ind(A(sn, 48, 90), merge), 240.0, add)
            quant(A("zq", c0, c0 + H), A("zs", c0, c0 + H), A("yt", e0, e0 + 640))
        if t == R - 1:
            ts(A("mu"), ind(A("oe"), L("ol")), 160.0, add)
        nq, ns = "tq%d" % (t + 1), "ts%d" % (t + 1)

        def new_state(half):
            quant(A(nq, H * half, H * half + H), A(ns, H * half, H * half + H), A("xa", 640 * half, 640 * half + 640))
            if t + 1 == R:
                dma("y", T.oc[:, 640 * half:640 * half + 640], u8(A(nq, H * half, H * half + H)), "dout")

        for half in range(2):
            c0, e0 = H * half, 640 * half
            for b in range(4):
                mm(4 + b, "wq", "wp", 128 * b, "zq", "zs", c0, c0 + H)
            for b in range(0 if half else NT, 4):
                mm(b, "eq", "es", 128 * b, "zq", "zs", c0, c0 + H)
            for b in range(4):
                act(A("rl", C * b + c0, C * b + c0 + H), P(4 + b, 0, H), AF.Relu, 0.03125)
            for b in range(4):
                if half and b == 0:
                    new_state(0)
                    if t + 1 < R:
                        early(t + 1, 0)
                    else:
                        cp(A("er"), ind(A("j1"), A("mu", 0, 10)), "s")
                        dma("y", T.ol[:], A("er", rows=slice(0, 128, 16)), "dout")
                d = P(b, 0, H) if half or b >= NT else ind(A("dz", C * b, C * b + C), A("lu", 0, 10))
                tt(A("xa", e0 + b, e0 + 640, 4), d, A("rl", C * b + c0, C * b + c0 + H), add)
        if t + 1 < R:
            early(t + 1, 1)
        new_state(1)
        if t + 1 < R:
            early(t + 1, 2)

    for half in range(2):
        mm(4 + half, "vq", "vs", 0, "tq3", "ts3", H * half, H * half + H)
        cp(A("ysb", H * half, H * half + H), P(4 + half, 0, H), "sv"[half])
        dma("sy"[half], T.y[:, H * half:H * half + H], A("ysb", H * half, H * half + H), "dout")
    for k in range(4):
        dma("s", T.osc[4 * k:4 * k + 4, :], A("ts3", rows=slice(32 * k, 32 * k + 4)), "dout")
    for s in sorted(total, key=lambda s: s == "dout"):
        wait("g", (s, total[s]))
